import numpy as np
import ml_dtypes


def mxq(x, axis, fmt="e4m3"):
    dtype, down = {"e4m3": (ml_dtypes.float8_e4m3fn, 7), "e5m2": (ml_dtypes.float8_e5m2, 14)}[fmt]
    v = np.moveaxis(np.asarray(x, np.float32).astype(ml_dtypes.bfloat16).astype(np.float64), axis, -1)
    blocks = v.reshape(v.shape[:-1] + (-1, 32))
    amax = np.abs(blocks).max(-1, keepdims=True)
    byte = np.maximum(np.where(amax > 0, np.frexp(amax)[1] - 1 + 127, 0) - down, 1)
    scale = np.exp2(byte - 127.0)
    codes = (blocks / scale).astype(np.float32).astype(dtype).astype(np.float64)
    return np.moveaxis((codes * scale).reshape(v.shape), -1, axis)


WIDE = False


def mx_kscale(k):
    if not WIDE:
        return np.ones(k)
    levels = np.array([10, -10, 5, -5, 0])
    if k % 512:
        return np.exp2(np.random.permutation(np.resize(levels, k // 32))).repeat(32)
    a = np.empty((k // 512, 16))
    for p in range(k // 512):
        a[p, :8] = np.random.permutation(np.resize(levels, 8))
        for g in range(8):
            far = levels[np.abs(levels - a[p, g]) >= 10]
            a[p, g + 8] = far[np.random.randint(len(far))]
    return np.exp2(a.ravel()).repeat(32)


def f64(x):
    return np.asarray(x).astype(np.float64)


def striped(idx):
    return np.tile(idx.reshape(-1, 16).T, (8, 1)).astype(np.uint16)


def unstriped(offs):
    return offs[:16].T.reshape(-1).astype(np.int64)


E2M1 = np.array([0.0, 0.5, 1.0, 1.5, 2.0, 3.0, 4.0, 6.0, -0.0, -0.5, -1.0, -1.5, -2.0, -3.0, -4.0, -6.0])


def pack_weight(w, fmt):
    k, n = w.shape
    w = f64(np.asarray(w, np.float32).astype(ml_dtypes.bfloat16)).reshape(k // 32, 32, n)
    amax = np.abs(w).max(1)
    if fmt == "e4m3":
        byte = np.frexp(amax)[1] - 1 + 127 - 7
    else:
        mant, ex = np.frexp(amax / 6.0)
        byte = np.where(mant > 0.5, ex, ex - 1) + 127
    byte = np.clip(np.where(amax > 0, byte, 1), 1, 254)
    scaled = (w * np.exp2(127.0 - byte)[:, None, :]).reshape(k, n).astype(np.float32)
    by_word = np.ascontiguousarray(scaled.reshape(k // 512, 128, 4, n).transpose(0, 1, 3, 2))
    if fmt == "e4m3":
        words = by_word.astype(ml_dtypes.float8_e4m3fn).view(np.uint8)
    else:
        c = by_word.astype(ml_dtypes.float4_e2m1fn).view(np.uint8) & 0xF
        words = (c[..., 0::2] | (c[..., 1::2] << 4)).reshape(k // 512, 128, 2 * n)
    return np.ascontiguousarray(words), np.ascontiguousarray(byte.astype(np.uint8).reshape(k // 512, 16, n))


def unpack_weight(words, scales, fmt):
    g, _, n = scales.shape
    words = np.ascontiguousarray(words).reshape(g, 128, n, -1)
    if fmt == "e4m3":
        vals = words.view(ml_dtypes.float8_e4m3fn).astype(np.float64)
    else:
        nib = np.empty((g, 128, n, 4), np.uint8)
        nib[..., 0::2] = words & 0xF
        nib[..., 1::2] = words >> 4
        vals = E2M1[nib]
    vals = vals * np.repeat(np.exp2(scales.astype(np.float64) - 127.0), 8, axis=1)[..., None]
    return vals.transpose(0, 1, 3, 2).reshape(g * 512, n)


def gelu(v):
    return 0.5 * v * (1.0 + np.tanh(np.sqrt(2.0 / np.pi) * (v + 0.044715 * v**3)))


K, I, H, N, T, S = 1024, 512, 1024, 512, 2048, 1024

def setup_inputs():
    n = np.random.standard_normal
    s, s2, u = mx_kscale(K)[:, None], mx_kscale(I)[:, None], mx_kscale(H)[:, None]
    tab_words, tab_scales = pack_weight(n((K, T)) * s, "e4m3")
    tab2_words, tab2_scales = pack_weight(n((I, T)) * s2, "e4m3")
    wb_words, wb_scales = pack_weight(n((I, H)) / np.sqrt(I) / s2, "e2m1")
    return {
        "tab_words": tab_words, "tab_scales": tab_scales,
        "tab2_words": tab2_words, "tab2_scales": tab2_scales,
        "offs": striped(np.random.permutation(T)[:S]),
        "offs2": striped(np.random.permutation(T)[:S]),
        "gT": (1.0 / (1.0 + np.exp(-n((H, T))))).astype(np.float32),
        "wa": (n((K, H)) / np.sqrt(K) / s * u.T).astype(np.float32),
        "wb_words": wb_words, "wb_scales": wb_scales,
        "wo": (1.5 * n((H, N)) / np.sqrt(H) / u).astype(np.float32),
        "bo": (0.5 * n(N)).astype(np.float32),
    }

def reference(tab_words, tab_scales, tab2_words, tab2_scales, offs, offs2, gT, wa, wb_words, wb_scales, wo, bo):
    v = unpack_weight(tab_words, tab_scales, "e4m3")[:, unstriped(offs)]
    v2 = unpack_weight(tab2_words, tab2_scales, "e4m3")[:, unstriped(offs2)]
    g = f64(gT)[:, unstriped(offs)]
    wb = unpack_weight(wb_words, wb_scales, "e2m1")
    a = mxq(f64(wa), 0, "e4m3").T @ v
    b = wb.T @ v2
    h = a * b * g
    y = mxq(f64(wo), 0, "e4m3").T @ mxq(h, 0, "e4m3")
    return np.tanh(y + f64(bo)[:, None])

@@ -1,0 +1,265 @@
+from contextlib import ExitStack
+
+import concourse.mybir as mybir
+
+K, I, H, N, T, S = 1024, 512, 1024, 512, 2048, 1024
+FLOPS = 2 * S * (K * H + I * H + H * N)
+
+F32 = mybir.dt.float32
+BF16 = mybir.dt.bfloat16
+I32 = mybir.dt.int32
+U32 = mybir.dt.uint32
+U16 = mybir.dt.uint16
+U8 = mybir.dt.uint8
+FP8X4 = mybir.dt.float8_e4m3fn_x4
+FP4X4 = mybir.dt.float4_e2m1fn_x4
+MULT = mybir.AluOpType.mult
+TANH = mybir.ActivationFunctionType.Tanh
+
+P = 128
+PACK = 4
+PASS = P * PACK
+BANK = 512
+GROUP = 16
+A_COLS = BANK // PACK
+
+
+def tile_list_gated_preference_features_kernel(
+    tc, tab_words, tab_scales, tab2_words, tab2_scales, offs, offs2, gT, wa, wb_words, wb_scales, wo, bo, out
+):
+    nc = tc.nc
+    with ExitStack() as ctx:
+        keep = ctx.enter_context(tc.tile_pool(name="keep", bufs=1))
+        ring = ctx.enter_context(tc.tile_pool(name="ring", bufs=3))
+        psum = ctx.enter_context(tc.psum_pool(name="psum", bufs=1))
+
+        users = keep.tile([P, S // GROUP], U16, name="users")
+        items = keep.tile([P, S // GROUP], U16, name="items")
+        item_scale_tab = keep.tile([P, T // 4], I32, name="item_scale_tab")
+        user_scale_tab = keep.tile([P, T // 4], I32, name="user_scale_tab")
+        wb_scale_raw = keep.tile([P, H // 4], I32, name="wb_scale_raw")
+        wb_code_raw = keep.tile([P, H // 2], I32, name="wb_code_raw")
+        item_code_tab = keep.tile([P, T], I32, name="item_code_tab")
+        user_code_tab = [keep.tile([P, T], I32, name=f"user_code_tab{g}") for g in range(2)]
+        bias = keep.tile([P, PACK], F32, name="bias")
+
+        item_codes = keep.tile([P, S], U32, name="item_codes", align_bytes=64)
+        item_scales = keep.tile([P, S], U8, name="item_scales", align_bytes=64)
+        user_codes = [keep.tile([P, S], U32, name=f"user_codes{g}", align_bytes=64) for g in range(2)]
+        user_scales = keep.tile([P, S], U8, name="user_scales", align_bytes=64)
+        wb_codes = keep.tile([P, 2 * H], U8, name="wb_codes", align_bytes=64)
+        wb_plane = keep.tile([P, H], U8, name="wb_plane", align_bytes=64)
+        gb = [keep.tile([P, PACK, S], F32, name=f"gb{half}") for half in range(2)]
+        h_codes = [keep.tile([P, S], U32, name=f"h_codes{half}", align_bytes=64) for half in range(2)]
+        h_scales = [keep.tile([P, S], U8, name=f"h_scales{half}", align_bytes=64) for half in range(2)]
+
+        def words(ap):
+            return ap.rearrange("p t i -> p (t i)").bitcast(I32)
+
+        nc.vector.memset(item_scale_tab[:], 0)
+        nc.gpsimd.memset(wb_scale_raw[:], 0)
+        nc.gpsimd.memset(user_scale_tab[:], 0)
+
+        nc.sync.dma_start(items[:], offs2)
+        nc.sync.dma_start(wb_code_raw[:], wb_words[0].bitcast(I32))
+        nc.sync.dma_start(users[:], offs)
+        nc.sync.dma_start(bias[:], bo.rearrange("(p c) -> p c", c=PACK))
+        for q in range(4):
+            nc.sync.dma_start(item_scale_tab[32 * q : 32 * q + 4, :], tab2_scales[0, 4 * q : 4 * q + 4, :].bitcast(I32))
+        nc.sync.dma_start(item_code_tab[:], words(tab2_words[0]))
+        for q in range(4):
+            nc.sync.dma_start(wb_scale_raw[32 * q : 32 * q + 4, :], wb_scales[0, 4 * q : 4 * q + 4, :].bitcast(I32))
+        for g in range(2):
+            nc.sync.dma_start(user_code_tab[g][:], words(tab_words[g]))
+        for q in range(4):
+            nc.sync.dma_start(user_scale_tab[32 * q : 32 * q + 8, :], tab_scales[:, 4 * q : 4 * q + 4, :].bitcast(I32))
+
+        gate = {}
+
+        def load_gate(u):
+            half, t = divmod(u, PACK)
+            gate[u] = ring.tile([P, T], F32, name="gate", bufs=5)
+            nc.sync.dma_start(gate[u][:], gT[half * PASS : (half + 1) * PASS, :].rearrange("(p t) s -> p t s", t=PACK)[:, t, :])
+
+        raw = {}
+        rounded = {}
+        codes = {}
+        scales = {}
+
+        def load_weight(key, rows):
+            raw[key] = ring.tile([P, PACK, PASS], F32, name="raw")
+            nc.sync.dma_start(raw[key][:], rows.rearrange("(p j) c -> p j c", j=PACK))
+
+        def round_weight(key):
+            rounded[key] = ring.tile([P, PACK * PASS], BF16, name="rounded", align_bytes=64)
+            nc.scalar.copy(
+                rounded[key][:].rearrange("p (t m j) -> p m j t", t=PACK, j=PACK),
+                raw[key][:].rearrange("p j (m t) -> p m j t", t=PACK),
+            )
+
+        def quantize_weight(key):
+            codes[key] = keep.tile([P, PASS], U32, name=f"codes_{key[0]}{key[1]}{key[2]}", align_bytes=64)
+            scales[key] = keep.tile([P, PASS], U8, name=f"scales_{key[0]}{key[1]}{key[2]}", align_bytes=64)
+            nc.vector.quantize_mx(codes[key][:].bitcast(FP8X4), scales[key][:], rounded[key][:])
+
+        def wa_rows(half, g):
+            return wa[g * PASS : (g + 1) * PASS, half * PASS : (half + 1) * PASS]
+
+        item_factor = {}
+
+        def make_b(u):
+            item_factor[u] = ring.tile([P, S], F32, name="item_factor", bufs=4)
+            for j0 in range(0, S, BANK):
+                acc = psum.tile([P, BANK], F32, name="wide", bufs=3)
+                nc.tensor.matmul_mx(
+                    acc[:],
+                    lhsT=wb_codes[:, 2 * P * u : 2 * P * (u + 1)].bitcast(FP4X4),
+                    lhsT_scale=wb_plane[:, P * u : P * (u + 1)],
+                    rhs=item_codes[:, j0 : j0 + BANK].bitcast(FP8X4),
+                    rhs_scale=item_scales[:, j0 : j0 + BANK],
+                    start=True,
+                    stop=True,
+                )
+                nc.scalar.copy(item_factor[u][:, j0 : j0 + BANK], acc[:])
+
+        def gate_b(u, j0, n):
+            half, t = divmod(u, PACK)
+            picked = gate[u][:].indirect(users[:, j0 // GROUP : (j0 + n) // GROUP])
+            nc.vector.tensor_tensor(gb[half][:, t, j0 : j0 + n], picked, item_factor[u][:, j0 : j0 + n], MULT)
+
+        def make_h(half, hb, c0, j0):
+            acc = psum.tile([P, PACK, A_COLS], F32, name="a_acc", bufs=5)
+            for t in range(PACK):
+                for g in range(2):
+                    key = ("a", half, g)
+                    nc.tensor.matmul_mx(
+                        acc[:, t, :],
+                        lhsT=codes[key][:, P * t : P * (t + 1)].bitcast(FP8X4),
+                        lhsT_scale=scales[key][:, P * t : P * (t + 1)],
+                        rhs=user_codes[g][:, j0 : j0 + A_COLS].bitcast(FP8X4),
+                        rhs_scale=user_scales[4 * g : P, j0 : j0 + A_COLS],
+                        start=(g == 0),
+                        stop=(g == 1),
+                    )
+            nc.vector.tensor_tensor(
+                hb[:, PACK * c0 : PACK * (c0 + A_COLS)].rearrange("p (c i t) -> p c t i", i=4, t=PACK),
+                acc[:].rearrange("p t (c i) -> p c t i", i=4),
+                gb[half][:, :, j0 : j0 + A_COLS].rearrange("p t (c i) -> p c t i", i=4),
+                MULT,
+            )
+
+        def make_h_chunk(half, j0, n):
+            hb = ring.tile([P, PACK * n], BF16, name="hb", align_bytes=64)
+            for c0 in range(0, n, A_COLS):
+                make_h(half, hb, c0, j0 + c0)
+            return hb
+
+        def quantize_h(half, hb, j0, n):
+            nc.vector.quantize_mx(h_codes[half][:, j0 : j0 + n].bitcast(FP8X4), h_scales[half][:, j0 : j0 + n], hb[:])
+
+        out_rows = out.rearrange("(p c) j -> p c j", c=PACK)
+
+        def finish(j0, n):
+            res = ring.tile([P, PACK, n], F32, name="res")
+            per_bank = 2
+            for c0 in range(0, PACK, per_bank):
+                acc = psum.tile([P, per_bank, n], F32, name="wide", bufs=3)
+                for c in range(c0, c0 + per_bank):
+                    for half in range(2):
+                        key = ("o", half, 0)
+                        nc.tensor.matmul_mx(
+                            acc[:, c - c0, :],
+                            lhsT=codes[key][:, P * c : P * (c + 1)].bitcast(FP8X4),
+                            lhsT_scale=scales[key][:, P * c : P * (c + 1)],
+                            rhs=h_codes[half][:, j0 : j0 + n].bitcast(FP8X4),
+                            rhs_scale=h_scales[half][:, j0 : j0 + n],
+                            start=(half == 0),
+                            stop=(half == 1),
+                        )
+                for c in range(c0, c0 + per_bank):
+                    nc.scalar.activation(res[:, c, :], acc[:, c - c0, :], TANH, bias=bias[:, c : c + 1])
+            nc.sync.dma_start(out_rows[:, :, j0 : j0 + n], res[:])
+
+        load_gate(0)
+        load_gate(1)
+        load_weight(("a", 0, 0), wa_rows(0, 0))
+        load_weight(("a", 0, 1), wa_rows(0, 1))
+        load_gate(2)
+        load_gate(3)
+        load_gate(4)
+        load_weight(("a", 1, 0), wa_rows(1, 0))
+
+        nc.vector.tensor_copy(
+            wb_codes[:].bitcast(U16).rearrange("p (a t m) -> p a t m", a=2, t=PACK),
+            wb_code_raw[:].bitcast(U16).rearrange("p (a m t) -> p a t m", a=2, t=PACK),
+        )
+        nc.vector.tensor_copy(item_scales[:], item_scale_tab[:].bitcast(U8).indirect(items[:]))
+        nc.vector.tensor_copy(item_codes[:], item_code_tab[:].bitcast(U32).indirect(items[:]))
+        nc.vector.tensor_copy(
+            wb_plane[:].rearrange("p (a t m) -> p a t m", a=2, t=PACK),
+            wb_scale_raw[:].bitcast(U8).rearrange("p (a m t) -> p a t m", a=2, t=PACK),
+        )
+        for u in range(2):
+            make_b(u)
+        for g in range(2):
+            nc.vector.tensor_copy(user_codes[g][:], user_code_tab[g][:].bitcast(U32).indirect(users[:]))
+        nc.vector.tensor_copy(user_scales[:], user_scale_tab[:].bitcast(U8).indirect(users[:]))
+
+        for u in range(2, 4):
+            make_b(u)
+        round_weight(("a", 0, 0))
+        round_weight(("a", 0, 1))
+        load_weight(("a", 1, 1), wa_rows(1, 1))
+        gate_b(0, 0, S)
+        load_gate(5)
+        make_b(4)
+        gate_b(1, 0, S)
+        load_gate(6)
+        make_b(5)
+        quantize_weight(("a", 0, 0))
+        quantize_weight(("a", 0, 1))
+        round_weight(("a", 1, 0))
+        round_weight(("a", 1, 1))
+        gate_b(2, 0, S)
+        load_gate(7)
+        load_weight(("o", 0, 0), wo[0:PASS, :])
+        load_weight(("o", 1, 0), wo[PASS : 2 * PASS, :])
+        make_b(6)
+        gate_b(3, 0, S)
+        make_b(7)
+        round_weight(("o", 0, 0))
+        round_weight(("o", 1, 0))
+
+        hb0 = make_h_chunk(0, 0, BANK)
+        gate_b(4, 0, BANK)
+        quantize_h(0, hb0, 0, BANK)
+        quantize_weight(("a", 1, 0))
+        quantize_weight(("a", 1, 1))
+        hb1 = make_h_chunk(0, BANK, BANK)
+        gate_b(5, 0, BANK)
+        quantize_h(0, hb1, BANK, BANK)
+        gate_b(6, 0, BANK)
+        gate_b(7, 0, BANK)
+        gate_b(4, 512, 256)
+        hb2 = make_h_chunk(1, 0, BANK)
+        quantize_weight(("o", 0, 0))
+        quantize_weight(("o", 1, 0))
+        quantize_h(1, hb2, 0, BANK)
+        finish(0, 256)
+        finish(256, 256)
+        for u in range(5, 8):
+            gate_b(u, 512, 256)
+        gate_b(4, 768, 256)
+        hb3 = make_h_chunk(1, 512, 256)
+        gate_b(5, 768, 256)
+        quantize_h(1, hb3, 512, 256)
+        finish(512, 256)
+        gate_b(6, 768, 256)
+        gate_b(7, 768, 128)
+        gate_b(7, 896, 128)
+        hb4 = make_h_chunk(1, 768, 128)
+        hb5 = make_h_chunk(1, 896, 128)
+        quantize_h(1, hb4, 768, 128)
+        quantize_h(1, hb5, 896, 128)
+        finish(768, 128)
+        finish(896, 128)

@@ -22,6 +22,7 @@ PASS = P * PACK
 BANK = 512
 GROUP = 16
 A_COLS = BANK // PACK
+LAST_CHUNKS = (256, 256, 256, 128, 128)
 
 
 def tile_list_gated_preference_features_kernel(
@@ -57,20 +58,19 @@ def tile_list_gated_preference_features_kernel(
             return ap.rearrange("p t i -> p (t i)").bitcast(I32)
 
         nc.vector.memset(item_scale_tab[:], 0)
-        nc.gpsimd.memset(wb_scale_raw[:], 0)
-        nc.gpsimd.memset(user_scale_tab[:], 0)
+        nc.vector.memset(wb_scale_raw[:], 0)
+        nc.vector.memset(user_scale_tab[:], 0)
 
         nc.sync.dma_start(items[:], offs2)
-        nc.sync.dma_start(wb_code_raw[:], wb_words[0].bitcast(I32))
         nc.sync.dma_start(users[:], offs)
-        nc.sync.dma_start(bias[:], bo.rearrange("(p c) -> p c", c=PACK))
         for q in range(4):
             nc.sync.dma_start(item_scale_tab[32 * q : 32 * q + 4, :], tab2_scales[0, 4 * q : 4 * q + 4, :].bitcast(I32))
         nc.sync.dma_start(item_code_tab[:], words(tab2_words[0]))
+        nc.sync.dma_start(user_code_tab[0][:], words(tab_words[0]))
+        nc.sync.dma_start(wb_code_raw[:], wb_words[0].bitcast(I32))
         for q in range(4):
             nc.sync.dma_start(wb_scale_raw[32 * q : 32 * q + 4, :], wb_scales[0, 4 * q : 4 * q + 4, :].bitcast(I32))
-        for g in range(2):
-            nc.sync.dma_start(user_code_tab[g][:], words(tab_words[g]))
+        nc.sync.dma_start(user_code_tab[1][:], words(tab_words[1]))
         for q in range(4):
             nc.sync.dma_start(user_scale_tab[32 * q : 32 * q + 8, :], tab_scales[:, 4 * q : 4 * q + 4, :].bitcast(I32))
 
@@ -79,7 +79,7 @@ def tile_list_gated_preference_features_kernel(
         def load_gate(u):
             half, t = divmod(u, PACK)
             gate[u] = ring.tile([P, T], F32, name="gate", bufs=5)
-            nc.sync.dma_start(gate[u][:], gT[half * PASS : (half + 1) * PASS, :].rearrange("(p t) s -> p t s", t=PACK)[:, t, :])
+            nc.sync.dma_start(gate[u][:], gT[half * PASS : (half + 1) * PASS, :].rearrange("(g t i) s -> t g i s", t=PACK, i=4)[t])
 
         raw = {}
         rounded = {}
@@ -89,6 +89,20 @@ def tile_list_gated_preference_features_kernel(
         def load_weight(key, rows):
             raw[key] = ring.tile([P, PACK, PASS], F32, name="raw")
             nc.sync.dma_start(raw[key][:], rows.rearrange("(p j) c -> p j c", j=PACK))
+
+        def load_wo(half):
+            key = ("o", half, 0)
+            raw[key] = ring.tile([P, PACK, PASS], F32, name="raw")
+            rows = wo[half * PASS : (half + 1) * PASS, :].rearrange("(g t i) n -> t g i n", t=PACK, i=4)
+            for t in range(PACK):
+                nc.sync.dma_start(raw[key][:, t, :], rows[t])
+
+        def round_wa(key):
+            rounded[key] = ring.tile([P, PACK * PASS], BF16, name="rounded", align_bytes=64)
+            nc.scalar.copy(
+                rounded[key][:].rearrange("p (t g i j) -> p g t j i", t=PACK, i=4, j=PACK),
+                raw[key][:].rearrange("p j (g t i) -> p g t j i", t=PACK, i=4),
+            )
 
         def round_weight(key):
             rounded[key] = ring.tile([P, PACK * PASS], BF16, name="rounded", align_bytes=64)
@@ -108,9 +122,9 @@ def tile_list_gated_preference_features_kernel(
         item_factor = {}
 
         def make_b(u):
-            item_factor[u] = ring.tile([P, S], F32, name="item_factor", bufs=4)
+            item_factor[u] = ring.tile([P, S], F32, name="item_factor", bufs=6)
             for j0 in range(0, S, BANK):
-                acc = psum.tile([P, BANK], F32, name="wide", bufs=3)
+                acc = psum.tile([P, BANK], F32, name="wide", bufs=4)
                 nc.tensor.matmul_mx(
                     acc[:],
                     lhsT=wb_codes[:, 2 * P * u : 2 * P * (u + 1)].bitcast(FP4X4),
@@ -128,7 +142,7 @@ def tile_list_gated_preference_features_kernel(
             nc.vector.tensor_tensor(gb[half][:, t, j0 : j0 + n], picked, item_factor[u][:, j0 : j0 + n], MULT)
 
         def make_h(half, hb, c0, j0):
-            acc = psum.tile([P, PACK, A_COLS], F32, name="a_acc", bufs=5)
+            acc = psum.tile([P, PACK, A_COLS], F32, name="a_acc", bufs=4)
             for t in range(PACK):
                 for g in range(2):
                     key = ("a", half, g)
@@ -163,7 +177,7 @@ def tile_list_gated_preference_features_kernel(
             res = ring.tile([P, PACK, n], F32, name="res")
             per_bank = 2
             for c0 in range(0, PACK, per_bank):
-                acc = psum.tile([P, per_bank, n], F32, name="wide", bufs=3)
+                acc = psum.tile([P, per_bank, n], F32, name="wide", bufs=4)
                 for c in range(c0, c0 + per_bank):
                     for half in range(2):
                         key = ("o", half, 0)
@@ -180,86 +194,67 @@ def tile_list_gated_preference_features_kernel(
                     nc.scalar.activation(res[:, c, :], acc[:, c - c0, :], TANH, bias=bias[:, c : c + 1])
             nc.sync.dma_start(out_rows[:, :, j0 : j0 + n], res[:])
 
-        load_gate(0)
-        load_gate(1)
+        for u in range(4):
+            load_gate(u)
         load_weight(("a", 0, 0), wa_rows(0, 0))
         load_weight(("a", 0, 1), wa_rows(0, 1))
-        load_gate(2)
-        load_gate(3)
         load_gate(4)
+        nc.sync.dma_start(bias[:], bo.rearrange("(p c) -> p c", c=PACK))
         load_weight(("a", 1, 0), wa_rows(1, 0))
 
-        nc.vector.tensor_copy(
-            wb_codes[:].bitcast(U16).rearrange("p (a t m) -> p a t m", a=2, t=PACK),
-            wb_code_raw[:].bitcast(U16).rearrange("p (a m t) -> p a t m", a=2, t=PACK),
-        )
         nc.vector.tensor_copy(item_scales[:], item_scale_tab[:].bitcast(U8).indirect(items[:]))
         nc.vector.tensor_copy(item_codes[:], item_code_tab[:].bitcast(U32).indirect(items[:]))
+        nc.vector.tensor_copy(user_codes[0][:], user_code_tab[0][:].bitcast(U32).indirect(users[:]))
         nc.vector.tensor_copy(
-            wb_plane[:].rearrange("p (a t m) -> p a t m", a=2, t=PACK),
-            wb_scale_raw[:].bitcast(U8).rearrange("p (a m t) -> p a t m", a=2, t=PACK),
+            wb_codes[:].bitcast(I32).rearrange("p (a t g w) -> p a t g w", a=2, t=PACK, w=2),
+            wb_code_raw[:].rearrange("p (a g t w) -> p a t g w", a=2, t=PACK, w=2),
         )
-        for u in range(2):
-            make_b(u)
-        for g in range(2):
-            nc.vector.tensor_copy(user_codes[g][:], user_code_tab[g][:].bitcast(U32).indirect(users[:]))
+        nc.vector.tensor_copy(
+            wb_plane[:].bitcast(I32).rearrange("p (a t g) -> p a t g", a=2, t=PACK),
+            wb_scale_raw[:].rearrange("p (a g t) -> p a t g", a=2, t=PACK),
+        )
+        nc.vector.tensor_copy(user_codes[1][:], user_code_tab[1][:].bitcast(U32).indirect(users[:]))
         nc.vector.tensor_copy(user_scales[:], user_scale_tab[:].bitcast(U8).indirect(users[:]))
 
-        for u in range(2, 4):
+        for u in range(6):
             make_b(u)
-        round_weight(("a", 0, 0))
-        round_weight(("a", 0, 1))
-        load_weight(("a", 1, 1), wa_rows(1, 1))
         gate_b(0, 0, S)
-        load_gate(5)
-        make_b(4)
+        make_b(6)
         gate_b(1, 0, S)
-        load_gate(6)
-        make_b(5)
+        make_b(7)
+        gate_b(2, 0, S)
+        gate_b(3, 0, S)
+        round_wa(("a", 0, 0))
+        round_wa(("a", 0, 1))
+        load_weight(("a", 1, 1), wa_rows(1, 1))
+        load_gate(5)
+        load_wo(0)
         quantize_weight(("a", 0, 0))
         quantize_weight(("a", 0, 1))
-        round_weight(("a", 1, 0))
-        round_weight(("a", 1, 1))
-        gate_b(2, 0, S)
+        round_wa(("a", 1, 0))
+        load_wo(1)
+        load_gate(6)
         load_gate(7)
-        load_weight(("o", 0, 0), wo[0:PASS, :])
-        load_weight(("o", 1, 0), wo[PASS : 2 * PASS, :])
-        make_b(6)
-        gate_b(3, 0, S)
-        make_b(7)
-        round_weight(("o", 0, 0))
-        round_weight(("o", 1, 0))
-
+        round_wa(("a", 1, 1))
+        gate_b(4, 0, S)
         hb0 = make_h_chunk(0, 0, BANK)
-        gate_b(4, 0, BANK)
+        hb1 = make_h_chunk(0, BANK, BANK)
         quantize_h(0, hb0, 0, BANK)
         quantize_weight(("a", 1, 0))
-        quantize_weight(("a", 1, 1))
-        hb1 = make_h_chunk(0, BANK, BANK)
-        gate_b(5, 0, BANK)
         quantize_h(0, hb1, BANK, BANK)
-        gate_b(6, 0, BANK)
-        gate_b(7, 0, BANK)
-        gate_b(4, 512, 256)
-        hb2 = make_h_chunk(1, 0, BANK)
+        quantize_weight(("a", 1, 1))
+        round_weight(("o", 0, 0))
+        round_weight(("o", 1, 0))
+        gate_b(5, 0, S)
         quantize_weight(("o", 0, 0))
         quantize_weight(("o", 1, 0))
-        quantize_h(1, hb2, 0, BANK)
-        finish(0, 256)
-        finish(256, 256)
-        for u in range(5, 8):
-            gate_b(u, 512, 256)
-        gate_b(4, 768, 256)
-        hb3 = make_h_chunk(1, 512, 256)
-        gate_b(5, 768, 256)
-        quantize_h(1, hb3, 512, 256)
-        finish(512, 256)
-        gate_b(6, 768, 256)
-        gate_b(7, 768, 128)
-        gate_b(7, 896, 128)
-        hb4 = make_h_chunk(1, 768, 128)
-        hb5 = make_h_chunk(1, 896, 128)
-        quantize_h(1, hb4, 768, 128)
-        quantize_h(1, hb5, 896, 128)
-        finish(768, 128)
-        finish(896, 128)
+        gate_b(6, 0, S)
+
+        starts = [sum(LAST_CHUNKS[:i]) for i in range(len(LAST_CHUNKS))]
+        gate_b(7, 0, LAST_CHUNKS[0])
+        for i, n in enumerate(LAST_CHUNKS):
+            hb = make_h_chunk(1, starts[i], n)
+            if i + 1 < len(LAST_CHUNKS):
+                gate_b(7, starts[i + 1], LAST_CHUNKS[i + 1])
+            quantize_h(1, hb, starts[i], n)
+            finish(starts[i], n)

@@ -57,7 +57,7 @@ def tile_list_gated_preference_features_kernel(
         def words(ap):
             return ap.rearrange("p t i -> p (t i)").bitcast(I32)
 
-        nc.vector.memset(item_scale_tab[:], 0)
+        nc.gpsimd.memset(item_scale_tab[:], 0)
         nc.vector.memset(wb_scale_raw[:], 0)
         nc.vector.memset(user_scale_tab[:], 0)
 
@@ -71,8 +71,6 @@ def tile_list_gated_preference_features_kernel(
         for q in range(4):
             nc.sync.dma_start(wb_scale_raw[32 * q : 32 * q + 4, :], wb_scales[0, 4 * q : 4 * q + 4, :].bitcast(I32))
         nc.sync.dma_start(user_code_tab[1][:], words(tab_words[1]))
-        for q in range(4):
-            nc.sync.dma_start(user_scale_tab[32 * q : 32 * q + 8, :], tab_scales[:, 4 * q : 4 * q + 4, :].bitcast(I32))
 
         gate = {}
 
@@ -107,8 +105,8 @@ def tile_list_gated_preference_features_kernel(
         def round_weight(key):
             rounded[key] = ring.tile([P, PACK * PASS], BF16, name="rounded", align_bytes=64)
             nc.scalar.copy(
-                rounded[key][:].rearrange("p (t m j) -> p m j t", t=PACK, j=PACK),
-                raw[key][:].rearrange("p j (m t) -> p m j t", t=PACK),
+                rounded[key][:].rearrange("p (c i t) -> p c t i", i=4, t=PACK),
+                raw[key][:].rearrange("p t (c i) -> p c t i", i=4),
             )
 
         def quantize_weight(key):
@@ -171,7 +169,33 @@ def tile_list_gated_preference_features_kernel(
         def quantize_h(half, hb, j0, n):
             nc.vector.quantize_mx(h_codes[half][:, j0 : j0 + n].bitcast(FP8X4), h_scales[half][:, j0 : j0 + n], hb[:])
 
-        out_rows = out.rearrange("(p c) j -> p c j", c=PACK)
+        out_rows = out.rearrange("(c p) j -> p c j", p=P)
+
+        def y_pass(acc, c, half, j0, n):
+            key = ("o", half, 0)
+            nc.tensor.matmul_mx(
+                acc,
+                lhsT=codes[key][:, P * c : P * (c + 1)].bitcast(FP8X4),
+                lhsT_scale=scales[key][:, P * c : P * (c + 1)],
+                rhs=h_codes[half][:, j0 : j0 + n].bitcast(FP8X4),
+                rhs_scale=h_scales[half][:, j0 : j0 + n],
+                start=(half == 0),
+                stop=(half == 1),
+            )
+
+        def open_last(j0, n):
+            accs = [psum.tile([P, n], F32, name="a_acc", bufs=4) for c in range(PACK)]
+            for c in range(PACK):
+                y_pass(accs[c][:], c, 0, j0, n)
+            return accs
+
+        def finish_last(accs, j0, n):
+            res = ring.tile([P, PACK, n], F32, name="res")
+            for c in range(PACK):
+                y_pass(accs[c][:], c, 1, j0, n)
+                nc.scalar.activation(res[:, c, :], accs[c][:], TANH, bias=bias[:, c : c + 1])
+                if c % 2 == 1:
+                    nc.sync.dma_start(out_rows[:, c - 1 : c + 1, j0 : j0 + n], res[:, c - 1 : c + 1, :])
 
         def finish(j0, n):
             res = ring.tile([P, PACK, n], F32, name="res")
@@ -194,12 +218,14 @@ def tile_list_gated_preference_features_kernel(
                     nc.scalar.activation(res[:, c, :], acc[:, c - c0, :], TANH, bias=bias[:, c : c + 1])
             nc.sync.dma_start(out_rows[:, :, j0 : j0 + n], res[:])
 
-        for u in range(4):
-            load_gate(u)
+        for q in range(4):
+            load_gate(q)
+            for g in range(2):
+                row = 32 * q + 4 * g
+                nc.sync.dma_start(user_scale_tab[row : row + 4, :], tab_scales[g, 4 * q : 4 * q + 4, :].bitcast(I32))
         load_weight(("a", 0, 0), wa_rows(0, 0))
         load_weight(("a", 0, 1), wa_rows(0, 1))
         load_gate(4)
-        nc.sync.dma_start(bias[:], bo.rearrange("(p c) -> p c", c=PACK))
         load_weight(("a", 1, 0), wa_rows(1, 0))
 
         nc.vector.tensor_copy(item_scales[:], item_scale_tab[:].bitcast(U8).indirect(items[:]))
@@ -214,7 +240,6 @@ def tile_list_gated_preference_features_kernel(
             wb_scale_raw[:].rearrange("p (a g t) -> p a t g", a=2, t=PACK),
         )
         nc.vector.tensor_copy(user_codes[1][:], user_code_tab[1][:].bitcast(U32).indirect(users[:]))
-        nc.vector.tensor_copy(user_scales[:], user_scale_tab[:].bitcast(U8).indirect(users[:]))
 
         for u in range(6):
             make_b(u)
@@ -224,6 +249,7 @@ def tile_list_gated_preference_features_kernel(
         make_b(7)
         gate_b(2, 0, S)
         gate_b(3, 0, S)
+        nc.vector.tensor_copy(user_scales[:], user_scale_tab[:].bitcast(U8).indirect(users[:]))
         round_wa(("a", 0, 0))
         round_wa(("a", 0, 1))
         load_weight(("a", 1, 1), wa_rows(1, 1))
@@ -235,9 +261,12 @@ def tile_list_gated_preference_features_kernel(
         load_wo(1)
         load_gate(6)
         load_gate(7)
+        with nc.allow_non_contiguous_dma(reason="one bias value for each partition and output tile"):
+            nc.sync.dma_start(bias[:], bo.rearrange("(c p) -> p c", p=P))
         round_wa(("a", 1, 1))
-        gate_b(4, 0, S)
+        gate_b(4, 0, BANK)
         hb0 = make_h_chunk(0, 0, BANK)
+        gate_b(4, BANK, BANK)
         hb1 = make_h_chunk(0, BANK, BANK)
         quantize_h(0, hb0, 0, BANK)
         quantize_weight(("a", 1, 0))
@@ -256,5 +285,9 @@ def tile_list_gated_preference_features_kernel(
             hb = make_h_chunk(1, starts[i], n)
             if i + 1 < len(LAST_CHUNKS):
                 gate_b(7, starts[i + 1], LAST_CHUNKS[i + 1])
-            quantize_h(1, hb, starts[i], n)
-            finish(starts[i], n)
+                quantize_h(1, hb, starts[i], n)
+                finish(starts[i], n)
+            else:
+                accs = open_last(starts[i], n)
+                quantize_h(1, hb, starts[i], n)
+                finish_last(accs, starts[i], n)

@@ -21,7 +21,6 @@ PACK = 4
 PASS = P * PACK
 BANK = 512
 GROUP = 16
-A_COLS = BANK // PACK
 LAST_CHUNKS = (256, 256, 256, 128, 128)
 
 
@@ -50,7 +49,7 @@ def tile_list_gated_preference_features_kernel(
         user_scales = keep.tile([P, S], U8, name="user_scales", align_bytes=64)
         wb_codes = keep.tile([P, 2 * H], U8, name="wb_codes", align_bytes=64)
         wb_plane = keep.tile([P, H], U8, name="wb_plane", align_bytes=64)
-        gb = [keep.tile([P, PACK, S], F32, name=f"gb{half}") for half in range(2)]
+        planes = [keep.tile([P, PACK, S], BF16, name=f"planes{half}") for half in range(2)]
         h_codes = [keep.tile([P, S], U32, name=f"h_codes{half}", align_bytes=64) for half in range(2)]
         h_scales = [keep.tile([P, S], U8, name=f"h_scales{half}", align_bytes=64) for half in range(2)]
 
@@ -76,7 +75,7 @@ def tile_list_gated_preference_features_kernel(
 
         def load_gate(u):
             half, t = divmod(u, PACK)
-            gate[u] = ring.tile([P, T], F32, name="gate", bufs=5)
+            gate[u] = ring.tile([P, T], F32, name="gate", bufs=4)
             nc.sync.dma_start(gate[u][:], gT[half * PASS : (half + 1) * PASS, :].rearrange("(g t i) s -> t g i s", t=PACK, i=4)[t])
 
         raw = {}
@@ -134,41 +133,67 @@ def tile_list_gated_preference_features_kernel(
                 )
                 nc.scalar.copy(item_factor[u][:, j0 : j0 + BANK], acc[:])
 
-        def gate_b(u, j0, n):
-            half, t = divmod(u, PACK)
-            picked = gate[u][:].indirect(users[:, j0 // GROUP : (j0 + n) // GROUP])
-            nc.vector.tensor_tensor(gb[half][:, t, j0 : j0 + n], picked, item_factor[u][:, j0 : j0 + n], MULT)
+        gated = {}
+        a_sum = {}
 
-        def make_h(half, hb, c0, j0):
-            acc = psum.tile([P, PACK, A_COLS], F32, name="a_acc", bufs=4)
-            for t in range(PACK):
-                for g in range(2):
-                    key = ("a", half, g)
-                    nc.tensor.matmul_mx(
-                        acc[:, t, :],
-                        lhsT=codes[key][:, P * t : P * (t + 1)].bitcast(FP8X4),
-                        lhsT_scale=scales[key][:, P * t : P * (t + 1)],
-                        rhs=user_codes[g][:, j0 : j0 + A_COLS].bitcast(FP8X4),
-                        rhs_scale=user_scales[4 * g : P, j0 : j0 + A_COLS],
-                        start=(g == 0),
-                        stop=(g == 1),
-                    )
+        def gate_b(u, j0, n, dest):
+            picked = gate[u][:].indirect(users[:, j0 // GROUP : (j0 + n) // GROUP])
+            nc.vector.tensor_tensor(dest, picked, item_factor[u][:, j0 : j0 + n], MULT)
+
+        def gate_tile(u, j0, n):
+            if j0 == 0:
+                gated[u] = ring.tile([P, S], F32, name="gated", bufs=5)
+            for c0 in range(j0, j0 + n, BANK):
+                gated[u, c0] = gated[u][:, c0 : c0 + BANK]
+            gate_b(u, j0, n, gated[u][:, j0 : j0 + n])
+
+        pieces = [keep.tile([P, 256], F32, name=f"piece{e}") for e in range(2)]
+
+        def gate_piece(u, j0, n, e):
+            gated[u, j0] = pieces[e][:, :n]
+            gate_b(u, j0, n, gated[u, j0])
+
+        def make_a(u, b):
+            half, t = divmod(u, PACK)
+            a_sum[u, b] = psum.tile([P, BANK], F32, name="a_acc", bufs=4)
+            for g in range(2):
+                key = ("a", half, g)
+                nc.tensor.matmul_mx(
+                    a_sum[u, b][:],
+                    lhsT=codes[key][:, P * t : P * (t + 1)].bitcast(FP8X4),
+                    lhsT_scale=scales[key][:, P * t : P * (t + 1)],
+                    rhs=user_codes[g][:, b * BANK : (b + 1) * BANK].bitcast(FP8X4),
+                    rhs_scale=user_scales[4 * g : P, b * BANK : (b + 1) * BANK],
+                    start=(g == 0),
+                    stop=(g == 1),
+                )
+
+        def make_h(u, j0, n):
+            half, t = divmod(u, PACK)
+            b, c0 = divmod(j0, BANK)
             nc.vector.tensor_tensor(
-                hb[:, PACK * c0 : PACK * (c0 + A_COLS)].rearrange("p (c i t) -> p c t i", i=4, t=PACK),
-                acc[:].rearrange("p t (c i) -> p c t i", i=4),
-                gb[half][:, :, j0 : j0 + A_COLS].rearrange("p t (c i) -> p c t i", i=4),
-                MULT,
+                planes[half][:, t, j0 : j0 + n], a_sum[u, b][:, c0 : c0 + n], gated[u, j0], MULT
             )
 
-        def make_h_chunk(half, j0, n):
+        def make_h_tile(u):
+            for b in range(2):
+                make_a(u, b)
+                make_h(u, b * BANK, BANK)
+
+        def interleave(copy, half, j0, n):
             hb = ring.tile([P, PACK * n], BF16, name="hb", align_bytes=64)
-            for c0 in range(0, n, A_COLS):
-                make_h(half, hb, c0, j0 + c0)
+            step = min(n, 256)
+            for c0 in range(0, n, step):
+                copy(
+                    hb[:, PACK * c0 : PACK * (c0 + step)].rearrange("p (c i t) -> p c t i", i=4, t=PACK),
+                    planes[half][:, :, j0 + c0 : j0 + c0 + step].rearrange("p t (c i) -> p c t i", i=4),
+                )
             return hb
 
         def quantize_h(half, hb, j0, n):
             nc.vector.quantize_mx(h_codes[half][:, j0 : j0 + n].bitcast(FP8X4), h_scales[half][:, j0 : j0 + n], hb[:])
 
+        result = keep.tile([P, PACK, S], F32, name="result")
         out_rows = out.rearrange("(c p) j -> p c j", p=P)
 
         def y_pass(acc, c, half, j0, n):
@@ -190,7 +215,7 @@ def tile_list_gated_preference_features_kernel(
             return accs
 
         def finish_last(accs, j0, n):
-            res = ring.tile([P, PACK, n], F32, name="res")
+            res = result[:, :, j0 : j0 + n]
             for c in range(PACK):
                 y_pass(accs[c][:], c, 1, j0, n)
                 nc.scalar.activation(res[:, c, :], accs[c][:], TANH, bias=bias[:, c : c + 1])
@@ -198,7 +223,7 @@ def tile_list_gated_preference_features_kernel(
                     nc.sync.dma_start(out_rows[:, c - 1 : c + 1, j0 : j0 + n], res[:, c - 1 : c + 1, :])
 
         def finish(j0, n):
-            res = ring.tile([P, PACK, n], F32, name="res")
+            res = result[:, :, j0 : j0 + n]
             per_bank = 2
             for c0 in range(0, PACK, per_bank):
                 acc = psum.tile([P, per_bank, n], F32, name="wide", bufs=4)
@@ -216,7 +241,7 @@ def tile_list_gated_preference_features_kernel(
                         )
                 for c in range(c0, c0 + per_bank):
                     nc.scalar.activation(res[:, c, :], acc[:, c - c0, :], TANH, bias=bias[:, c : c + 1])
-            nc.sync.dma_start(out_rows[:, :, j0 : j0 + n], res[:])
+            nc.sync.dma_start(out_rows[:, :, j0 : j0 + n], res)
 
         for q in range(4):
             load_gate(q)
@@ -243,12 +268,12 @@ def tile_list_gated_preference_features_kernel(
 
         for u in range(6):
             make_b(u)
-        gate_b(0, 0, S)
+        gate_tile(0, 0, S)
         make_b(6)
-        gate_b(1, 0, S)
+        gate_tile(1, 0, S)
         make_b(7)
-        gate_b(2, 0, S)
-        gate_b(3, 0, S)
+        gate_tile(2, 0, S)
+        gate_tile(3, 0, S)
         nc.vector.tensor_copy(user_scales[:], user_scale_tab[:].bitcast(U8).indirect(users[:]))
         round_wa(("a", 0, 0))
         round_wa(("a", 0, 1))
@@ -264,30 +289,52 @@ def tile_list_gated_preference_features_kernel(
         with nc.allow_non_contiguous_dma(reason="one bias value for each partition and output tile"):
             nc.sync.dma_start(bias[:], bo.rearrange("(c p) -> p c", p=P))
         round_wa(("a", 1, 1))
-        gate_b(4, 0, BANK)
-        hb0 = make_h_chunk(0, 0, BANK)
-        gate_b(4, BANK, BANK)
-        hb1 = make_h_chunk(0, BANK, BANK)
-        quantize_h(0, hb0, 0, BANK)
+        gate_tile(4, 0, BANK)
+        make_h_tile(0)
+        make_h_tile(1)
+        gate_tile(4, BANK, BANK)
+        make_h_tile(2)
+        make_h_tile(3)
         quantize_weight(("a", 1, 0))
-        quantize_h(0, hb1, BANK, BANK)
         quantize_weight(("a", 1, 1))
         round_weight(("o", 0, 0))
         round_weight(("o", 1, 0))
-        gate_b(5, 0, S)
+        hb0 = interleave(nc.scalar.copy, 0, 0, BANK)
+        hb1 = interleave(nc.scalar.copy, 0, BANK, BANK)
+        gate_tile(5, 0, S)
+        make_h_tile(4)
+        quantize_h(0, hb0, 0, BANK)
+        make_h_tile(5)
+        quantize_h(0, hb1, BANK, BANK)
         quantize_weight(("o", 0, 0))
         quantize_weight(("o", 1, 0))
-        gate_b(6, 0, S)
+        gate_tile(6, 0, BANK)
+        make_a(6, 0)
+        make_h(6, 0, BANK)
+        make_a(7, 0)
+        make_a(6, 1)
+        make_a(7, 1)
 
         starts = [sum(LAST_CHUNKS[:i]) for i in range(len(LAST_CHUNKS))]
-        gate_b(7, 0, LAST_CHUNKS[0])
+        last = len(LAST_CHUNKS) - 1
+        jobs = []
         for i, n in enumerate(LAST_CHUNKS):
-            hb = make_h_chunk(1, starts[i], n)
-            if i + 1 < len(LAST_CHUNKS):
-                gate_b(7, starts[i + 1], LAST_CHUNKS[i + 1])
-                quantize_h(1, hb, starts[i], n)
-                finish(starts[i], n)
-            else:
-                accs = open_last(starts[i], n)
-                quantize_h(1, hb, starts[i], n)
-                finish_last(accs, starts[i], n)
+            if starts[i] >= BANK:
+                jobs.append((6, i))
+            jobs.append((7, i))
+        gate_piece(7, 0, LAST_CHUNKS[0], 0)
+        for e, (u, i) in enumerate(jobs):
+            n = LAST_CHUNKS[i]
+            if e + 1 < len(jobs):
+                nu, ni = jobs[e + 1]
+                gate_piece(nu, starts[ni], LAST_CHUNKS[ni], (e + 1) % 2)
+            make_h(u, starts[i], n)
+            if u == 7:
+                hb = interleave(nc.scalar.copy if i == 1 else nc.vector.tensor_copy, 1, starts[i], n)
+                if i < last:
+                    quantize_h(1, hb, starts[i], n)
+                    finish(starts[i], n)
+                else:
+                    accs = open_last(starts[i], n)
+                    quantize_h(1, hb, starts[i], n)
+                    finish_last(accs, starts[i], n)

@@ -17,11 +17,22 @@ MULT = mybir.AluOpType.mult
 TANH = mybir.ActivationFunctionType.Tanh
 
 P = 128
-PACK = 4
-PASS = P * PACK
+SLOTS = 4
+PASS = P * SLOTS
 BANK = 512
 GROUP = 16
-LAST_CHUNKS = (256, 256, 256, 128, 128)
+QUADS = 4
+QUAD = P // QUADS
+SCALE_ROWS = 4
+RUN = 4
+PASSES = 2
+TILES = PASSES * SLOTS
+OUT_TILES = N // P
+TILES_PER_BANK = 2
+CHUNKS = (256, 256, 256, 128, 128)
+PIECE = max(CHUNKS)
+SCALAR_CHUNK = 1
+GATE_BUFS, GATED_BUFS, B_BUFS, STAGE_BUFS, PSUM_BUFS = 4, 5, 6, 3, 4
 
 
 def tile_list_gated_preference_features_kernel(
@@ -30,8 +41,8 @@ def tile_list_gated_preference_features_kernel(
     nc = tc.nc
     with ExitStack() as ctx:
         keep = ctx.enter_context(tc.tile_pool(name="keep", bufs=1))
-        ring = ctx.enter_context(tc.tile_pool(name="ring", bufs=3))
-        psum = ctx.enter_context(tc.psum_pool(name="psum", bufs=1))
+        ring = ctx.enter_context(tc.tile_pool(name="ring", bufs=STAGE_BUFS))
+        psum = ctx.enter_context(tc.psum_pool(name="psum", bufs=PSUM_BUFS))
 
         users = keep.tile([P, S // GROUP], U16, name="users")
         items = keep.tile([P, S // GROUP], U16, name="items")
@@ -40,21 +51,183 @@ def tile_list_gated_preference_features_kernel(
         wb_scale_raw = keep.tile([P, H // 4], I32, name="wb_scale_raw")
         wb_code_raw = keep.tile([P, H // 2], I32, name="wb_code_raw")
         item_code_tab = keep.tile([P, T], I32, name="item_code_tab")
-        user_code_tab = [keep.tile([P, T], I32, name=f"user_code_tab{g}") for g in range(2)]
-        bias = keep.tile([P, PACK], F32, name="bias")
+        user_code_tab = [keep.tile([P, T], I32, name=f"user_code_tab{s}") for s in range(PASSES)]
+        bias = keep.tile([P, OUT_TILES], F32, name="bias")
 
         item_codes = keep.tile([P, S], U32, name="item_codes", align_bytes=64)
         item_scales = keep.tile([P, S], U8, name="item_scales", align_bytes=64)
-        user_codes = [keep.tile([P, S], U32, name=f"user_codes{g}", align_bytes=64) for g in range(2)]
+        user_codes = [keep.tile([P, S], U32, name=f"user_codes{s}", align_bytes=64) for s in range(PASSES)]
         user_scales = keep.tile([P, S], U8, name="user_scales", align_bytes=64)
         wb_codes = keep.tile([P, 2 * H], U8, name="wb_codes", align_bytes=64)
-        wb_plane = keep.tile([P, H], U8, name="wb_plane", align_bytes=64)
-        planes = [keep.tile([P, PACK, S], BF16, name=f"planes{half}") for half in range(2)]
-        h_codes = [keep.tile([P, S], U32, name=f"h_codes{half}", align_bytes=64) for half in range(2)]
-        h_scales = [keep.tile([P, S], U8, name=f"h_scales{half}", align_bytes=64) for half in range(2)]
+        wb_scale = keep.tile([P, H], U8, name="wb_scale", align_bytes=64)
+        h_tiles = [keep.tile([P, SLOTS, S], BF16, name=f"h_tiles{s}") for s in range(PASSES)]
+        h_codes = [keep.tile([P, S], U32, name=f"h_codes{s}", align_bytes=64) for s in range(PASSES)]
+        h_scales = [keep.tile([P, S], U8, name=f"h_scales{s}", align_bytes=64) for s in range(PASSES)]
+        pieces = [keep.tile([P, PIECE], F32, name=f"piece{e}") for e in range(2)]
+        result = keep.tile([P, OUT_TILES, S], F32, name="result")
+        out_rows = out.rearrange("(c p) j -> p c j", p=P)
+
+        gate, raw, rounded, codes, scales, b_tile, gated, a_sum = {}, {}, {}, {}, {}, {}, {}, {}
 
         def words(ap):
             return ap.rearrange("p t i -> p (t i)").bitcast(I32)
+
+        def load_scale_rows(tile, first_row, source, quad):
+            row = QUAD * quad + first_row
+            rows = source[SCALE_ROWS * quad : SCALE_ROWS * (quad + 1), :]
+            nc.sync.dma_start(tile[row : row + SCALE_ROWS, :], rows.bitcast(I32))
+
+        def factor_rows(ap, s):
+            return ap[s * PASS : (s + 1) * PASS, :].rearrange("(g t i) c -> t g i c", t=SLOTS, i=RUN)
+
+        def load_gate(u):
+            s, t = divmod(u, SLOTS)
+            gate[u] = ring.tile([P, T], F32, name="gate", bufs=GATE_BUFS)
+            nc.sync.dma_start(gate[u][:], factor_rows(gT, s)[t])
+
+        def load_wa(s, ks):
+            key = ("wa", s, ks)
+            raw[key] = ring.tile([P, SLOTS, PASS], F32, name="raw")
+            rows = wa[ks * PASS : (ks + 1) * PASS, s * PASS : (s + 1) * PASS]
+            nc.sync.dma_start(raw[key][:], rows.rearrange("(p j) c -> p j c", j=SLOTS))
+
+        def load_wo(s):
+            key = ("wo", s, 0)
+            raw[key] = ring.tile([P, SLOTS, N], F32, name="raw")
+            for t in range(SLOTS):
+                nc.sync.dma_start(raw[key][:, t, :], factor_rows(wo, s)[t])
+
+        def round_wa(s, ks):
+            key = ("wa", s, ks)
+            rounded[key] = ring.tile([P, SLOTS * PASS], BF16, name="rounded", align_bytes=64)
+            nc.scalar.copy(
+                rounded[key][:].rearrange("p (t g i j) -> p g t j i", t=SLOTS, i=RUN, j=SLOTS),
+                raw[key][:].rearrange("p j (g t i) -> p g t j i", t=SLOTS, i=RUN),
+            )
+
+        def round_wo(s):
+            key = ("wo", s, 0)
+            rounded[key] = ring.tile([P, SLOTS * N], BF16, name="rounded", align_bytes=64)
+            nc.scalar.copy(
+                rounded[key][:].rearrange("p (c i t) -> p c t i", i=RUN, t=SLOTS),
+                raw[key][:].rearrange("p t (c i) -> p c t i", i=RUN),
+            )
+
+        def quantize_weight(name, s, ks):
+            key = (name, s, ks)
+            codes[key] = keep.tile([P, PASS], U32, name=f"codes_{name}{s}{ks}", align_bytes=64)
+            scales[key] = keep.tile([P, PASS], U8, name=f"scales_{name}{s}{ks}", align_bytes=64)
+            nc.vector.quantize_mx(codes[key][:].bitcast(FP8X4), scales[key][:], rounded[key][:])
+
+        def make_b(u):
+            b_tile[u] = ring.tile([P, S], F32, name="b_tile", bufs=B_BUFS)
+            for j0 in range(0, S, BANK):
+                acc = psum.tile([P, BANK], F32, name="b_or_y")
+                nc.tensor.matmul_mx(
+                    acc[:],
+                    lhsT=wb_codes[:, 2 * P * u : 2 * P * (u + 1)].bitcast(FP4X4),
+                    lhsT_scale=wb_scale[:, P * u : P * (u + 1)],
+                    rhs=item_codes[:, j0 : j0 + BANK].bitcast(FP8X4),
+                    rhs_scale=item_scales[:, j0 : j0 + BANK],
+                    start=True,
+                    stop=True,
+                )
+                nc.scalar.copy(b_tile[u][:, j0 : j0 + BANK], acc[:])
+
+        def gate_b(dest, u, j0, n):
+            picked = gate[u][:].indirect(users[:, j0 // GROUP : (j0 + n) // GROUP])
+            nc.vector.tensor_tensor(dest, picked, b_tile[u][:, j0 : j0 + n], MULT)
+
+        def gate_tile(u, n):
+            whole = ring.tile([P, S], F32, name="gated", bufs=GATED_BUFS)
+            for j0 in range(0, n, BANK):
+                gated[u, j0] = whole[:, j0 : j0 + BANK]
+            gate_b(whole[:, :n], u, 0, n)
+
+        def gate_piece(u, j0, n, e):
+            gated[u, j0] = pieces[e][:, :n]
+            gate_b(gated[u, j0], u, j0, n)
+
+        def make_a(u, bank):
+            s, t = divmod(u, SLOTS)
+            pairs = slice(bank * BANK, (bank + 1) * BANK)
+            a_sum[u, bank] = psum.tile([P, BANK], F32, name="a_or_last_y")
+            for ks in range(PASSES):
+                key = ("wa", s, ks)
+                nc.tensor.matmul_mx(
+                    a_sum[u, bank][:],
+                    lhsT=codes[key][:, P * t : P * (t + 1)].bitcast(FP8X4),
+                    lhsT_scale=scales[key][:, P * t : P * (t + 1)],
+                    rhs=user_codes[ks][:, pairs].bitcast(FP8X4),
+                    rhs_scale=user_scales[SCALE_ROWS * ks : P, pairs],
+                    start=(ks == 0),
+                    stop=(ks == PASSES - 1),
+                )
+
+        def make_h(u, j0, n):
+            s, t = divmod(u, SLOTS)
+            bank, c0 = divmod(j0, BANK)
+            nc.vector.tensor_tensor(h_tiles[s][:, t, j0 : j0 + n], a_sum[u, bank][:, c0 : c0 + n], gated[u, j0], MULT)
+
+        def make_h_tile(u):
+            for bank in range(S // BANK):
+                make_a(u, bank)
+                make_h(u, bank * BANK, BANK)
+
+        def interleave(copy, s, j0, n):
+            packed = ring.tile([P, SLOTS * n], BF16, name="packed", align_bytes=64)
+            step = min(n, PIECE)
+            for c0 in range(0, n, step):
+                copy(
+                    packed[:, SLOTS * c0 : SLOTS * (c0 + step)].rearrange("p (c i t) -> p c t i", i=RUN, t=SLOTS),
+                    h_tiles[s][:, :, j0 + c0 : j0 + c0 + step].rearrange("p t (c i) -> p c t i", i=RUN),
+                )
+            return packed
+
+        def quantize_h(s, packed, j0, n):
+            nc.vector.quantize_mx(h_codes[s][:, j0 : j0 + n].bitcast(FP8X4), h_scales[s][:, j0 : j0 + n], packed[:])
+
+        def y_pass(acc, c, s, j0, n):
+            key = ("wo", s, 0)
+            nc.tensor.matmul_mx(
+                acc,
+                lhsT=codes[key][:, P * c : P * (c + 1)].bitcast(FP8X4),
+                lhsT_scale=scales[key][:, P * c : P * (c + 1)],
+                rhs=h_codes[s][:, j0 : j0 + n].bitcast(FP8X4),
+                rhs_scale=h_scales[s][:, j0 : j0 + n],
+                start=(s == 0),
+                stop=(s == PASSES - 1),
+            )
+
+        def tanh_out(c, acc, j0, n):
+            nc.scalar.activation(result[:, c, j0 : j0 + n], acc, TANH, bias=bias[:, c : c + 1])
+
+        def store(c0, j0, n):
+            tiles = slice(c0, c0 + TILES_PER_BANK)
+            nc.sync.dma_start(out_rows[:, tiles, j0 : j0 + n], result[:, tiles, j0 : j0 + n])
+
+        def finish(j0, n):
+            for c0 in range(0, OUT_TILES, TILES_PER_BANK):
+                acc = psum.tile([P, TILES_PER_BANK, n], F32, name="b_or_y")
+                for c in range(c0, c0 + TILES_PER_BANK):
+                    for s in range(PASSES):
+                        y_pass(acc[:, c - c0, :], c, s, j0, n)
+                for c in range(c0, c0 + TILES_PER_BANK):
+                    tanh_out(c, acc[:, c - c0, :], j0, n)
+                store(c0, j0, n)
+
+        def open_last(j0, n):
+            accs = [psum.tile([P, n], F32, name="a_or_last_y") for c in range(OUT_TILES)]
+            for c in range(OUT_TILES):
+                y_pass(accs[c][:], c, 0, j0, n)
+            return accs
+
+        def finish_last(accs, j0, n):
+            for c in range(OUT_TILES):
+                y_pass(accs[c][:], c, 1, j0, n)
+                tanh_out(c, accs[c][:], j0, n)
+                if (c + 1) % TILES_PER_BANK == 0:
+                    store(c + 1 - TILES_PER_BANK, j0, n)
 
         nc.gpsimd.memset(item_scale_tab[:], 0)
         nc.vector.memset(wb_scale_raw[:], 0)
@@ -62,279 +235,96 @@ def tile_list_gated_preference_features_kernel(
 
         nc.sync.dma_start(items[:], offs2)
         nc.sync.dma_start(users[:], offs)
-        for q in range(4):
-            nc.sync.dma_start(item_scale_tab[32 * q : 32 * q + 4, :], tab2_scales[0, 4 * q : 4 * q + 4, :].bitcast(I32))
+        for quad in range(QUADS):
+            load_scale_rows(item_scale_tab, 0, tab2_scales[0], quad)
         nc.sync.dma_start(item_code_tab[:], words(tab2_words[0]))
         nc.sync.dma_start(user_code_tab[0][:], words(tab_words[0]))
         nc.sync.dma_start(wb_code_raw[:], wb_words[0].bitcast(I32))
-        for q in range(4):
-            nc.sync.dma_start(wb_scale_raw[32 * q : 32 * q + 4, :], wb_scales[0, 4 * q : 4 * q + 4, :].bitcast(I32))
+        for quad in range(QUADS):
+            load_scale_rows(wb_scale_raw, 0, wb_scales[0], quad)
         nc.sync.dma_start(user_code_tab[1][:], words(tab_words[1]))
-
-        gate = {}
-
-        def load_gate(u):
-            half, t = divmod(u, PACK)
-            gate[u] = ring.tile([P, T], F32, name="gate", bufs=4)
-            nc.sync.dma_start(gate[u][:], gT[half * PASS : (half + 1) * PASS, :].rearrange("(g t i) s -> t g i s", t=PACK, i=4)[t])
-
-        raw = {}
-        rounded = {}
-        codes = {}
-        scales = {}
-
-        def load_weight(key, rows):
-            raw[key] = ring.tile([P, PACK, PASS], F32, name="raw")
-            nc.sync.dma_start(raw[key][:], rows.rearrange("(p j) c -> p j c", j=PACK))
-
-        def load_wo(half):
-            key = ("o", half, 0)
-            raw[key] = ring.tile([P, PACK, PASS], F32, name="raw")
-            rows = wo[half * PASS : (half + 1) * PASS, :].rearrange("(g t i) n -> t g i n", t=PACK, i=4)
-            for t in range(PACK):
-                nc.sync.dma_start(raw[key][:, t, :], rows[t])
-
-        def round_wa(key):
-            rounded[key] = ring.tile([P, PACK * PASS], BF16, name="rounded", align_bytes=64)
-            nc.scalar.copy(
-                rounded[key][:].rearrange("p (t g i j) -> p g t j i", t=PACK, i=4, j=PACK),
-                raw[key][:].rearrange("p j (g t i) -> p g t j i", t=PACK, i=4),
-            )
-
-        def round_weight(key):
-            rounded[key] = ring.tile([P, PACK * PASS], BF16, name="rounded", align_bytes=64)
-            nc.scalar.copy(
-                rounded[key][:].rearrange("p (c i t) -> p c t i", i=4, t=PACK),
-                raw[key][:].rearrange("p t (c i) -> p c t i", i=4),
-            )
-
-        def quantize_weight(key):
-            codes[key] = keep.tile([P, PASS], U32, name=f"codes_{key[0]}{key[1]}{key[2]}", align_bytes=64)
-            scales[key] = keep.tile([P, PASS], U8, name=f"scales_{key[0]}{key[1]}{key[2]}", align_bytes=64)
-            nc.vector.quantize_mx(codes[key][:].bitcast(FP8X4), scales[key][:], rounded[key][:])
-
-        def wa_rows(half, g):
-            return wa[g * PASS : (g + 1) * PASS, half * PASS : (half + 1) * PASS]
-
-        item_factor = {}
-
-        def make_b(u):
-            item_factor[u] = ring.tile([P, S], F32, name="item_factor", bufs=6)
-            for j0 in range(0, S, BANK):
-                acc = psum.tile([P, BANK], F32, name="wide", bufs=4)
-                nc.tensor.matmul_mx(
-                    acc[:],
-                    lhsT=wb_codes[:, 2 * P * u : 2 * P * (u + 1)].bitcast(FP4X4),
-                    lhsT_scale=wb_plane[:, P * u : P * (u + 1)],
-                    rhs=item_codes[:, j0 : j0 + BANK].bitcast(FP8X4),
-                    rhs_scale=item_scales[:, j0 : j0 + BANK],
-                    start=True,
-                    stop=True,
-                )
-                nc.scalar.copy(item_factor[u][:, j0 : j0 + BANK], acc[:])
-
-        gated = {}
-        a_sum = {}
-
-        def gate_b(u, j0, n, dest):
-            picked = gate[u][:].indirect(users[:, j0 // GROUP : (j0 + n) // GROUP])
-            nc.vector.tensor_tensor(dest, picked, item_factor[u][:, j0 : j0 + n], MULT)
-
-        def gate_tile(u, j0, n):
-            if j0 == 0:
-                gated[u] = ring.tile([P, S], F32, name="gated", bufs=5)
-            for c0 in range(j0, j0 + n, BANK):
-                gated[u, c0] = gated[u][:, c0 : c0 + BANK]
-            gate_b(u, j0, n, gated[u][:, j0 : j0 + n])
-
-        pieces = [keep.tile([P, 256], F32, name=f"piece{e}") for e in range(2)]
-
-        def gate_piece(u, j0, n, e):
-            gated[u, j0] = pieces[e][:, :n]
-            gate_b(u, j0, n, gated[u, j0])
-
-        def make_a(u, b):
-            half, t = divmod(u, PACK)
-            a_sum[u, b] = psum.tile([P, BANK], F32, name="a_acc", bufs=4)
-            for g in range(2):
-                key = ("a", half, g)
-                nc.tensor.matmul_mx(
-                    a_sum[u, b][:],
-                    lhsT=codes[key][:, P * t : P * (t + 1)].bitcast(FP8X4),
-                    lhsT_scale=scales[key][:, P * t : P * (t + 1)],
-                    rhs=user_codes[g][:, b * BANK : (b + 1) * BANK].bitcast(FP8X4),
-                    rhs_scale=user_scales[4 * g : P, b * BANK : (b + 1) * BANK],
-                    start=(g == 0),
-                    stop=(g == 1),
-                )
-
-        def make_h(u, j0, n):
-            half, t = divmod(u, PACK)
-            b, c0 = divmod(j0, BANK)
-            nc.vector.tensor_tensor(
-                planes[half][:, t, j0 : j0 + n], a_sum[u, b][:, c0 : c0 + n], gated[u, j0], MULT
-            )
-
-        def make_h_tile(u):
-            for b in range(2):
-                make_a(u, b)
-                make_h(u, b * BANK, BANK)
-
-        def interleave(copy, half, j0, n):
-            hb = ring.tile([P, PACK * n], BF16, name="hb", align_bytes=64)
-            step = min(n, 256)
-            for c0 in range(0, n, step):
-                copy(
-                    hb[:, PACK * c0 : PACK * (c0 + step)].rearrange("p (c i t) -> p c t i", i=4, t=PACK),
-                    planes[half][:, :, j0 + c0 : j0 + c0 + step].rearrange("p t (c i) -> p c t i", i=4),
-                )
-            return hb
-
-        def quantize_h(half, hb, j0, n):
-            nc.vector.quantize_mx(h_codes[half][:, j0 : j0 + n].bitcast(FP8X4), h_scales[half][:, j0 : j0 + n], hb[:])
-
-        result = keep.tile([P, PACK, S], F32, name="result")
-        out_rows = out.rearrange("(c p) j -> p c j", p=P)
-
-        def y_pass(acc, c, half, j0, n):
-            key = ("o", half, 0)
-            nc.tensor.matmul_mx(
-                acc,
-                lhsT=codes[key][:, P * c : P * (c + 1)].bitcast(FP8X4),
-                lhsT_scale=scales[key][:, P * c : P * (c + 1)],
-                rhs=h_codes[half][:, j0 : j0 + n].bitcast(FP8X4),
-                rhs_scale=h_scales[half][:, j0 : j0 + n],
-                start=(half == 0),
-                stop=(half == 1),
-            )
-
-        def open_last(j0, n):
-            accs = [psum.tile([P, n], F32, name="a_acc", bufs=4) for c in range(PACK)]
-            for c in range(PACK):
-                y_pass(accs[c][:], c, 0, j0, n)
-            return accs
-
-        def finish_last(accs, j0, n):
-            res = result[:, :, j0 : j0 + n]
-            for c in range(PACK):
-                y_pass(accs[c][:], c, 1, j0, n)
-                nc.scalar.activation(res[:, c, :], accs[c][:], TANH, bias=bias[:, c : c + 1])
-                if c % 2 == 1:
-                    nc.sync.dma_start(out_rows[:, c - 1 : c + 1, j0 : j0 + n], res[:, c - 1 : c + 1, :])
-
-        def finish(j0, n):
-            res = result[:, :, j0 : j0 + n]
-            per_bank = 2
-            for c0 in range(0, PACK, per_bank):
-                acc = psum.tile([P, per_bank, n], F32, name="wide", bufs=4)
-                for c in range(c0, c0 + per_bank):
-                    for half in range(2):
-                        key = ("o", half, 0)
-                        nc.tensor.matmul_mx(
-                            acc[:, c - c0, :],
-                            lhsT=codes[key][:, P * c : P * (c + 1)].bitcast(FP8X4),
-                            lhsT_scale=scales[key][:, P * c : P * (c + 1)],
-                            rhs=h_codes[half][:, j0 : j0 + n].bitcast(FP8X4),
-                            rhs_scale=h_scales[half][:, j0 : j0 + n],
-                            start=(half == 0),
-                            stop=(half == 1),
-                        )
-                for c in range(c0, c0 + per_bank):
-                    nc.scalar.activation(res[:, c, :], acc[:, c - c0, :], TANH, bias=bias[:, c : c + 1])
-            nc.sync.dma_start(out_rows[:, :, j0 : j0 + n], res)
-
-        for q in range(4):
-            load_gate(q)
-            for g in range(2):
-                row = 32 * q + 4 * g
-                nc.sync.dma_start(user_scale_tab[row : row + 4, :], tab_scales[g, 4 * q : 4 * q + 4, :].bitcast(I32))
-        load_weight(("a", 0, 0), wa_rows(0, 0))
-        load_weight(("a", 0, 1), wa_rows(0, 1))
+        for quad in range(QUADS):
+            load_gate(quad)
+            for ks in range(PASSES):
+                load_scale_rows(user_scale_tab, SCALE_ROWS * ks, tab_scales[ks], quad)
+        load_wa(0, 0)
+        load_wa(0, 1)
         load_gate(4)
-        load_weight(("a", 1, 0), wa_rows(1, 0))
+        load_wa(1, 0)
 
         nc.vector.tensor_copy(item_scales[:], item_scale_tab[:].bitcast(U8).indirect(items[:]))
         nc.vector.tensor_copy(item_codes[:], item_code_tab[:].bitcast(U32).indirect(items[:]))
         nc.vector.tensor_copy(user_codes[0][:], user_code_tab[0][:].bitcast(U32).indirect(users[:]))
         nc.vector.tensor_copy(
-            wb_codes[:].bitcast(I32).rearrange("p (a t g w) -> p a t g w", a=2, t=PACK, w=2),
-            wb_code_raw[:].rearrange("p (a g t w) -> p a t g w", a=2, t=PACK, w=2),
+            wb_codes[:].bitcast(I32).rearrange("p (s t g w) -> p s t g w", s=PASSES, t=SLOTS, w=2),
+            wb_code_raw[:].rearrange("p (s g t w) -> p s t g w", s=PASSES, t=SLOTS, w=2),
         )
         nc.vector.tensor_copy(
-            wb_plane[:].bitcast(I32).rearrange("p (a t g) -> p a t g", a=2, t=PACK),
-            wb_scale_raw[:].rearrange("p (a g t) -> p a t g", a=2, t=PACK),
+            wb_scale[:].bitcast(I32).rearrange("p (s t g) -> p s t g", s=PASSES, t=SLOTS),
+            wb_scale_raw[:].rearrange("p (s g t) -> p s t g", s=PASSES, t=SLOTS),
         )
         nc.vector.tensor_copy(user_codes[1][:], user_code_tab[1][:].bitcast(U32).indirect(users[:]))
 
-        for u in range(6):
+        for u in range(B_BUFS):
             make_b(u)
-        gate_tile(0, 0, S)
-        make_b(6)
-        gate_tile(1, 0, S)
-        make_b(7)
-        gate_tile(2, 0, S)
-        gate_tile(3, 0, S)
+        for u in range(SLOTS):
+            gate_tile(u, S)
+            if B_BUFS + u < TILES:
+                make_b(B_BUFS + u)
         nc.vector.tensor_copy(user_scales[:], user_scale_tab[:].bitcast(U8).indirect(users[:]))
-        round_wa(("a", 0, 0))
-        round_wa(("a", 0, 1))
-        load_weight(("a", 1, 1), wa_rows(1, 1))
+        round_wa(0, 0)
+        round_wa(0, 1)
+        load_wa(1, 1)
         load_gate(5)
         load_wo(0)
-        quantize_weight(("a", 0, 0))
-        quantize_weight(("a", 0, 1))
-        round_wa(("a", 1, 0))
+        quantize_weight("wa", 0, 0)
+        quantize_weight("wa", 0, 1)
+        round_wa(1, 0)
         load_wo(1)
         load_gate(6)
         load_gate(7)
         with nc.allow_non_contiguous_dma(reason="one bias value for each partition and output tile"):
             nc.sync.dma_start(bias[:], bo.rearrange("(c p) -> p c", p=P))
-        round_wa(("a", 1, 1))
-        gate_tile(4, 0, BANK)
-        make_h_tile(0)
-        make_h_tile(1)
-        gate_tile(4, BANK, BANK)
-        make_h_tile(2)
-        make_h_tile(3)
-        quantize_weight(("a", 1, 0))
-        quantize_weight(("a", 1, 1))
-        round_weight(("o", 0, 0))
-        round_weight(("o", 1, 0))
-        hb0 = interleave(nc.scalar.copy, 0, 0, BANK)
-        hb1 = interleave(nc.scalar.copy, 0, BANK, BANK)
-        gate_tile(5, 0, S)
+        round_wa(1, 1)
+        gate_tile(4, S)
+        for u in range(SLOTS):
+            make_h_tile(u)
+
+        quantize_weight("wa", 1, 0)
+        quantize_weight("wa", 1, 1)
+        round_wo(0)
+        round_wo(1)
+        packed0 = interleave(nc.scalar.copy, 0, 0, BANK)
+        packed1 = interleave(nc.scalar.copy, 0, BANK, BANK)
+        gate_tile(5, S)
         make_h_tile(4)
-        quantize_h(0, hb0, 0, BANK)
+        quantize_h(0, packed0, 0, BANK)
         make_h_tile(5)
-        quantize_h(0, hb1, BANK, BANK)
-        quantize_weight(("o", 0, 0))
-        quantize_weight(("o", 1, 0))
-        gate_tile(6, 0, BANK)
+        quantize_h(0, packed1, BANK, BANK)
+        quantize_weight("wo", 0, 0)
+        quantize_weight("wo", 1, 0)
+        gate_tile(6, BANK)
         make_a(6, 0)
         make_h(6, 0, BANK)
         make_a(7, 0)
         make_a(6, 1)
         make_a(7, 1)
 
-        starts = [sum(LAST_CHUNKS[:i]) for i in range(len(LAST_CHUNKS))]
-        last = len(LAST_CHUNKS) - 1
-        jobs = []
-        for i, n in enumerate(LAST_CHUNKS):
-            if starts[i] >= BANK:
-                jobs.append((6, i))
-            jobs.append((7, i))
-        gate_piece(7, 0, LAST_CHUNKS[0], 0)
+        starts = [sum(CHUNKS[:i]) for i in range(len(CHUNKS))]
+        jobs = [(u, i) for i in range(len(CHUNKS)) for u in (6, 7) if u == 7 or starts[i] >= BANK]
+        gate_piece(7, 0, CHUNKS[0], 0)
         for e, (u, i) in enumerate(jobs):
-            n = LAST_CHUNKS[i]
+            j0, n = starts[i], CHUNKS[i]
             if e + 1 < len(jobs):
-                nu, ni = jobs[e + 1]
-                gate_piece(nu, starts[ni], LAST_CHUNKS[ni], (e + 1) % 2)
-            make_h(u, starts[i], n)
+                next_u, next_i = jobs[e + 1]
+                gate_piece(next_u, starts[next_i], CHUNKS[next_i], (e + 1) % len(pieces))
+            make_h(u, j0, n)
             if u == 7:
-                hb = interleave(nc.scalar.copy if i == 1 else nc.vector.tensor_copy, 1, starts[i], n)
-                if i < last:
-                    quantize_h(1, hb, starts[i], n)
-                    finish(starts[i], n)
+                packed = interleave(nc.scalar.copy if i == SCALAR_CHUNK else nc.vector.tensor_copy, 1, j0, n)
+                if i + 1 < len(CHUNKS):
+                    quantize_h(1, packed, j0, n)
+                    finish(j0, n)
                 else:
-                    accs = open_last(starts[i], n)
-                    quantize_h(1, hb, starts[i], n)
-                    finish_last(accs, starts[i], n)
+                    accs = open_last(j0, n)
+                    quantize_h(1, packed, j0, n)
+                    finish_last(accs, j0, n)

@@ -31,8 +31,21 @@ OUT_TILES = N // P
 TILES_PER_BANK = 2
 CHUNKS = (256, 256, 256, 128, 128)
 PIECE = max(CHUNKS)
-SCALAR_CHUNK = 1
-GATE_BUFS, GATED_BUFS, B_BUFS, STAGE_BUFS, PSUM_BUFS = 4, 5, 6, 3, 4
+SCALAR_CHUNKS = 2
+PLAIN = 0
+EARLY = 0
+V_SHARE = 16
+POOL0 = 0
+POOL1 = 0
+LAP = 8
+HOLD = 1
+NST = 2
+OPEN0 = 1
+LATE = 1
+V_SHARE2 = 0
+ALIAS0 = 1
+ALIAS1 = 1
+GATE_BUFS, GATED_BUFS, B_BUFS, STAGE_BUFS, PSUM_BUFS = 4, 5, 7, 3, 4
 
 
 def tile_list_gated_preference_features_kernel(
@@ -50,8 +63,8 @@ def tile_list_gated_preference_features_kernel(
         user_scale_tab = keep.tile([P, T // 4], I32, name="user_scale_tab")
         wb_scale_raw = keep.tile([P, H // 4], I32, name="wb_scale_raw")
         wb_code_raw = keep.tile([P, H // 2], I32, name="wb_code_raw")
-        item_code_tab = keep.tile([P, T], I32, name="item_code_tab")
-        user_code_tab = [keep.tile([P, T], I32, name=f"user_code_tab{s}") for s in range(PASSES)]
+        item_code_tab = keep.tile([P, T], I32, name="item_code_tab", align_bytes=64)
+        user_code_tab = [keep.tile([P, T], I32, name=f"user_code_tab{s}", align_bytes=64) for s in range(PASSES)]
         bias = keep.tile([P, OUT_TILES], F32, name="bias")
 
         item_codes = keep.tile([P, S], U32, name="item_codes", align_bytes=64)
@@ -60,10 +73,11 @@ def tile_list_gated_preference_features_kernel(
         user_scales = keep.tile([P, S], U8, name="user_scales", align_bytes=64)
         wb_codes = keep.tile([P, 2 * H], U8, name="wb_codes", align_bytes=64)
         wb_scale = keep.tile([P, H], U8, name="wb_scale", align_bytes=64)
-        h_tiles = [keep.tile([P, SLOTS, S], BF16, name=f"h_tiles{s}") for s in range(PASSES)]
-        h_codes = [keep.tile([P, S], U32, name=f"h_codes{s}", align_bytes=64) for s in range(PASSES)]
+        h_tiles = {(1, bank): keep.tile([P, SLOTS, BANK], BF16, name=f"h_tiles1{bank}", align_bytes=64) for bank in range(2)}
+        h_codes = {}
         h_scales = [keep.tile([P, S], U8, name=f"h_scales{s}", align_bytes=64) for s in range(PASSES)]
-        pieces = [keep.tile([P, PIECE], F32, name=f"piece{e}") for e in range(2)]
+        stage = [keep.tile([P, 3 * PIECE], F32, name=f"stage{e}", align_bytes=64) for e in range(NST)]
+        late = keep.tile([P, BANK], F32, name="late", align_bytes=64)
         result = keep.tile([P, OUT_TILES, S], F32, name="result")
         out_rows = out.rearrange("(c p) j -> p c j", p=P)
 
@@ -72,10 +86,13 @@ def tile_list_gated_preference_features_kernel(
         def words(ap):
             return ap.rearrange("p t i -> p (t i)").bitcast(I32)
 
-        def load_scale_rows(tile, first_row, source, quad):
-            row = QUAD * quad + first_row
-            rows = source[SCALE_ROWS * quad : SCALE_ROWS * (quad + 1), :]
-            nc.sync.dma_start(tile[row : row + SCALE_ROWS, :], rows.bitcast(I32))
+        def load_scale_row(tile, source, r):
+            rows = source.rearrange("(q r) c -> r q c", r=SCALE_ROWS)[r]
+            nc.sync.dma_start(tile[r:P:QUAD, :], rows.bitcast(I32))
+
+        def load_user_scales(quad):
+            rows = tab_scales[:, SCALE_ROWS * quad : SCALE_ROWS * (quad + 1), :]
+            nc.sync.dma_start(user_scale_tab[QUAD * quad : QUAD * quad + PASSES * SCALE_ROWS, :], rows.bitcast(I32))
 
         def factor_rows(ap, s):
             return ap[s * PASS : (s + 1) * PASS, :].rearrange("(g t i) c -> t g i c", t=SLOTS, i=RUN)
@@ -87,41 +104,59 @@ def tile_list_gated_preference_features_kernel(
 
         def load_wa(s, ks):
             key = ("wa", s, ks)
-            raw[key] = ring.tile([P, SLOTS, PASS], F32, name="raw")
+            if (s, ks) == (1, 1):
+                raw[key] = keep.tile([P, SLOTS, PASS], F32, name="item_code_tab", align_bytes=64)
+            else:
+                raw[key] = ring.tile([P, SLOTS, PASS], F32, name="raw", align_bytes=64)
             rows = wa[ks * PASS : (ks + 1) * PASS, s * PASS : (s + 1) * PASS]
             nc.sync.dma_start(raw[key][:], rows.rearrange("(p j) c -> p j c", j=SLOTS))
 
         def load_wo(s):
             key = ("wo", s, 0)
-            raw[key] = ring.tile([P, SLOTS, N], F32, name="raw")
+            raw[key] = keep.tile([P, SLOTS, N], F32, name=f"user_code_tab{s}", align_bytes=64)
             for t in range(SLOTS):
                 nc.sync.dma_start(raw[key][:, t, :], factor_rows(wo, s)[t])
 
-        def round_wa(s, ks):
+        def round_wa(s, ks, share=0):
             key = ("wa", s, ks)
-            rounded[key] = ring.tile([P, SLOTS * PASS], BF16, name="rounded", align_bytes=64)
-            nc.scalar.copy(
-                rounded[key][:].rearrange("p (t g i j) -> p g t j i", t=SLOTS, i=RUN, j=SLOTS),
-                raw[key][:].rearrange("p j (g t i) -> p g t j i", t=SLOTS, i=RUN),
-            )
+            if (s, ks) == (1, 1):
+                rounded[key] = keep.tile([P, SLOTS * PASS], BF16, name="rounded11", align_bytes=64)
+            else:
+                rounded[key] = ring.tile([P, SLOTS * PASS], BF16, name="rounded", bufs=2, align_bytes=64)
+            dest = rounded[key][:].rearrange("p (t g i j) -> p g t j i", t=SLOTS, i=RUN, j=SLOTS)
+            source = raw[key][:].rearrange("p j (g t i) -> p g t j i", t=SLOTS, i=RUN)
+            if share < QUAD:
+                nc.scalar.copy(dest[:, share:], source[:, share:])
+            if share:
+                nc.vector.tensor_copy(dest[:, :share], source[:, :share])
 
         def round_wo(s):
             key = ("wo", s, 0)
-            rounded[key] = ring.tile([P, SLOTS * N], BF16, name="rounded", align_bytes=64)
+            if s == 0:
+                rounded[key] = keep.tile([P, SLOTS * N], BF16, name="h_tiles00", align_bytes=64)
+            else:
+                rounded[key] = ring.tile([P, SLOTS * N], BF16, name="rounded", bufs=2, align_bytes=64)
             nc.scalar.copy(
                 rounded[key][:].rearrange("p (c i t) -> p c t i", i=RUN, t=SLOTS),
                 raw[key][:].rearrange("p t (c i) -> p c t i", i=RUN),
             )
 
-        def quantize_weight(name, s, ks):
+        def quantize_weight(name, s, ks, place=None):
             key = (name, s, ks)
-            codes[key] = keep.tile([P, PASS], U32, name=f"codes_{name}{s}{ks}", align_bytes=64)
+            codes[key] = keep.tile([P, PASS], U32, name=place or f"codes_{name}{s}{ks}", align_bytes=64)
             scales[key] = keep.tile([P, PASS], U8, name=f"scales_{name}{s}{ks}", align_bytes=64)
             nc.vector.quantize_mx(codes[key][:].bitcast(FP8X4), scales[key][:], rounded[key][:])
 
         def make_b(u):
-            b_tile[u] = ring.tile([P, S], F32, name="b_tile", bufs=B_BUFS)
+            if u != 4:
+                whole = ring.tile([P, S], F32, name="b_tile", bufs=B_BUFS)
+                b_tile[u] = whole[:]
             for j0 in range(0, S, BANK):
+                if u == 4:
+                    half = keep.tile([P, BANK], F32, name=f"h_tiles0{j0 // BANK}", align_bytes=64)
+                    b_tile[u, j0] = half[:]
+                else:
+                    b_tile[u, j0] = whole[:, j0 : j0 + BANK]
                 acc = psum.tile([P, BANK], F32, name="b_or_y")
                 nc.tensor.matmul_mx(
                     acc[:],
@@ -132,20 +167,32 @@ def tile_list_gated_preference_features_kernel(
                     start=True,
                     stop=True,
                 )
-                nc.scalar.copy(b_tile[u][:, j0 : j0 + BANK], acc[:])
+                nc.scalar.copy(b_tile[u, j0], acc[:])
 
         def gate_b(dest, u, j0, n):
             picked = gate[u][:].indirect(users[:, j0 // GROUP : (j0 + n) // GROUP])
-            nc.vector.tensor_tensor(dest, picked, b_tile[u][:, j0 : j0 + n], MULT)
+            nc.vector.tensor_tensor(dest, picked, b_tile[u, j0] if u == 4 else b_tile[u][:, j0 : j0 + n], MULT)
 
         def gate_tile(u, n):
-            whole = ring.tile([P, S], F32, name="gated", bufs=GATED_BUFS)
+            whole = keep.tile([P, S], F32, name="rounded11" if u == 5 else f"gated{u}", align_bytes=64)
             for j0 in range(0, n, BANK):
-                gated[u, j0] = whole[:, j0 : j0 + BANK]
-            gate_b(whole[:, :n], u, 0, n)
+                gated[u, j0] = whole[:, j0 : min(n, j0 + BANK)]
+            if u < PLAIN:
+                nc.vector.tensor_copy(whole[:, :n], gate[u][:].indirect(users[:, : n // GROUP]))
+                nc.gpsimd.tensor_tensor(whole[:, :n], whole[:, :n], b_tile[u][:, :n], MULT)
+            elif u == 4:
+                for j0 in range(0, S, BANK):
+                    gate_b(gated[u, j0], u, j0, BANK)
+            else:
+                gate_b(whole[:, :n], u, 0, n)
 
         def gate_piece(u, j0, n, e):
-            gated[u, j0] = pieces[e][:, :n]
+            if u == 7 and j0 == (CHUNKS[0] if HOLD else 0):
+                gated[u, j0] = late[:, :n]
+            elif u == 7:
+                gated[u, j0] = stage[(e - 1) % NST][:, 2 * PIECE : 2 * PIECE + n]
+            else:
+                gated[u, j0] = stage[e][:, 2 * PIECE + LAP - n : 2 * PIECE + LAP]
             gate_b(gated[u, j0], u, j0, n)
 
         def make_a(u, bank):
@@ -167,25 +214,44 @@ def tile_list_gated_preference_features_kernel(
         def make_h(u, j0, n):
             s, t = divmod(u, SLOTS)
             bank, c0 = divmod(j0, BANK)
-            nc.vector.tensor_tensor(h_tiles[s][:, t, j0 : j0 + n], a_sum[u, bank][:, c0 : c0 + n], gated[u, j0], MULT)
+            nc.vector.tensor_tensor(h_tiles[s, bank][:, t, c0 : c0 + n], a_sum[u, bank][:, c0 : c0 + n], gated[u, j0], MULT)
 
-        def make_h_tile(u):
+        def make_h_tile(u, pool_pairs=0):
+            s, t = divmod(u, SLOTS)
             for bank in range(S // BANK):
+                j0 = bank * BANK
                 make_a(u, bank)
-                make_h(u, bank * BANK, BANK)
+                n = min(BANK, max(0, pool_pairs - j0))
+                if n:
+                    a_copy = ring.tile([P, BANK], F32, name="a_copy", bufs=2)
+                    nc.scalar.copy(a_copy[:, :n], a_sum[u, bank][:, :n])
+                    nc.gpsimd.tensor_tensor(h_tiles[s, bank][:, t, :n], a_copy[:, :n], gated[u, j0][:, :n], MULT)
+                if n < BANK:
+                    nc.vector.tensor_tensor(
+                        h_tiles[s, bank][:, t, n:], a_sum[u, bank][:, n:], gated[u, j0][:, n:], MULT
+                    )
 
-        def interleave(copy, s, j0, n):
-            packed = ring.tile([P, SLOTS * n], BF16, name="packed", align_bytes=64)
+        def interleave(copy, s, j0, n, packed=None):
+            if packed is None:
+                packed = ring.tile([P, SLOTS * n], BF16, name="packed", bufs=2, align_bytes=64)
+                packed = packed[:]
             step = min(n, PIECE)
             for c0 in range(0, n, step):
                 copy(
                     packed[:, SLOTS * c0 : SLOTS * (c0 + step)].rearrange("p (c i t) -> p c t i", i=RUN, t=SLOTS),
-                    h_tiles[s][:, :, j0 + c0 : j0 + c0 + step].rearrange("p t (c i) -> p c t i", i=RUN),
+                    h_tiles[s, j0 // BANK][:, :, j0 % BANK + c0 : j0 % BANK + c0 + step].rearrange("p t (c i) -> p c t i", i=RUN),
                 )
             return packed
 
+        def spent(key):
+            return raw[key][:].rearrange("p j c -> p (j c)").bitcast(BF16)[:, : SLOTS * BANK]
+
         def quantize_h(s, packed, j0, n):
-            nc.vector.quantize_mx(h_codes[s][:, j0 : j0 + n].bitcast(FP8X4), h_scales[s][:, j0 : j0 + n], packed[:])
+            bank, c0 = divmod(j0, BANK)
+            if c0 == 0:
+                place = "late" if (s, bank) == (0, 1) else f"h_codes{s}{bank}"
+                h_codes[s, bank] = keep.tile([P, BANK], U32, name=place, align_bytes=64)
+            nc.vector.quantize_mx(h_codes[s, bank][:, c0 : c0 + n].bitcast(FP8X4), h_scales[s][:, j0 : j0 + n], packed)
 
         def y_pass(acc, c, s, j0, n):
             key = ("wo", s, 0)
@@ -193,7 +259,7 @@ def tile_list_gated_preference_features_kernel(
                 acc,
                 lhsT=codes[key][:, P * c : P * (c + 1)].bitcast(FP8X4),
                 lhsT_scale=scales[key][:, P * c : P * (c + 1)],
-                rhs=h_codes[s][:, j0 : j0 + n].bitcast(FP8X4),
+                rhs=h_codes[s, j0 // BANK][:, j0 % BANK : j0 % BANK + n].bitcast(FP8X4),
                 rhs_scale=h_scales[s][:, j0 : j0 + n],
                 start=(s == 0),
                 stop=(s == PASSES - 1),
@@ -216,8 +282,8 @@ def tile_list_gated_preference_features_kernel(
                     tanh_out(c, acc[:, c - c0, :], j0, n)
                 store(c0, j0, n)
 
-        def open_last(j0, n):
-            accs = [psum.tile([P, n], F32, name="a_or_last_y") for c in range(OUT_TILES)]
+        def open_last(j0, n, tag="a_or_last_y"):
+            accs = [psum.tile([P, n], F32, name=tag) for c in range(OUT_TILES)]
             for c in range(OUT_TILES):
                 y_pass(accs[c][:], c, 0, j0, n)
             return accs
@@ -234,19 +300,18 @@ def tile_list_gated_preference_features_kernel(
         nc.vector.memset(user_scale_tab[:], 0)
 
         nc.sync.dma_start(items[:], offs2)
-        nc.sync.dma_start(users[:], offs)
-        for quad in range(QUADS):
-            load_scale_rows(item_scale_tab, 0, tab2_scales[0], quad)
-        nc.sync.dma_start(item_code_tab[:], words(tab2_words[0]))
-        nc.sync.dma_start(user_code_tab[0][:], words(tab_words[0]))
+        for r in range(SCALE_ROWS):
+            load_scale_row(item_scale_tab, tab2_scales[0], r)
         nc.sync.dma_start(wb_code_raw[:], wb_words[0].bitcast(I32))
-        for quad in range(QUADS):
-            load_scale_rows(wb_scale_raw, 0, wb_scales[0], quad)
+        nc.sync.dma_start(item_code_tab[:], words(tab2_words[0]))
+        for r in range(SCALE_ROWS):
+            load_scale_row(wb_scale_raw, wb_scales[0], r)
+        nc.sync.dma_start(users[:], offs)
+        nc.sync.dma_start(user_code_tab[0][:], words(tab_words[0]))
         nc.sync.dma_start(user_code_tab[1][:], words(tab_words[1]))
         for quad in range(QUADS):
             load_gate(quad)
-            for ks in range(PASSES):
-                load_scale_rows(user_scale_tab, SCALE_ROWS * ks, tab_scales[ks], quad)
+            load_user_scales(quad)
         load_wa(0, 0)
         load_wa(0, 1)
         load_gate(4)
@@ -265,15 +330,13 @@ def tile_list_gated_preference_features_kernel(
         )
         nc.vector.tensor_copy(user_codes[1][:], user_code_tab[1][:].bitcast(U32).indirect(users[:]))
 
-        for u in range(B_BUFS):
+        for u in range(TILES):
             make_b(u)
         for u in range(SLOTS):
             gate_tile(u, S)
-            if B_BUFS + u < TILES:
-                make_b(B_BUFS + u)
         nc.vector.tensor_copy(user_scales[:], user_scale_tab[:].bitcast(U8).indirect(users[:]))
         round_wa(0, 0)
-        round_wa(0, 1)
+        round_wa(0, 1, V_SHARE)
         load_wa(1, 1)
         load_gate(5)
         load_wo(0)
@@ -285,46 +348,54 @@ def tile_list_gated_preference_features_kernel(
         load_gate(7)
         with nc.allow_non_contiguous_dma(reason="one bias value for each partition and output tile"):
             nc.sync.dma_start(bias[:], bo.rearrange("(c p) -> p c", p=P))
-        round_wa(1, 1)
+        round_wa(1, 1, V_SHARE2)
         gate_tile(4, S)
+        for bank in range(2):
+            h_tiles[0, bank] = keep.tile([P, SLOTS, BANK], BF16, name=f"h_tiles0{bank}", align_bytes=64)
         for u in range(SLOTS):
-            make_h_tile(u)
+            make_h_tile(u, POOL0 - u * S)
 
-        quantize_weight("wa", 1, 0)
-        quantize_weight("wa", 1, 1)
+        quantize_weight("wa", 1, 0, "gated2")
+        quantize_weight("wa", 1, 1, "gated3")
+        packed0 = interleave(nc.scalar.copy, 0, 0, BANK, spent(("wa", 1, 1)) if ALIAS0 else None)
         round_wo(0)
         round_wo(1)
-        packed0 = interleave(nc.scalar.copy, 0, 0, BANK)
-        packed1 = interleave(nc.scalar.copy, 0, BANK, BANK)
+        packed1 = interleave(nc.scalar.copy, 0, BANK, BANK, spent(("wo", 1, 0)) if ALIAS1 else None)
         gate_tile(5, S)
-        make_h_tile(4)
-        quantize_h(0, packed0, 0, BANK)
+        make_h_tile(4, POOL1)
         make_h_tile(5)
-        quantize_h(0, packed1, BANK, BANK)
-        quantize_weight("wo", 0, 0)
-        quantize_weight("wo", 1, 0)
-        gate_tile(6, BANK)
+        quantize_h(0, packed0, 0, BANK)
+        quantize_weight("wo", 0, 0, "rounded11")
+        quantize_weight("wo", 1, 0, "gated4")
+        if EARLY:
+            gate_tile(6, EARLY)
         make_a(6, 0)
-        make_h(6, 0, BANK)
+        if EARLY:
+            make_h(6, 0, EARLY)
         make_a(7, 0)
         make_a(6, 1)
         make_a(7, 1)
 
         starts = [sum(CHUNKS[:i]) for i in range(len(CHUNKS))]
-        jobs = [(u, i) for i in range(len(CHUNKS)) for u in (6, 7) if u == 7 or starts[i] >= BANK]
-        gate_piece(7, 0, CHUNKS[0], 0)
-        for e, (u, i) in enumerate(jobs):
-            j0, n = starts[i], CHUNKS[i]
-            if e + 1 < len(jobs):
-                next_u, next_i = jobs[e + 1]
-                gate_piece(next_u, starts[next_i], CHUNKS[next_i], (e + 1) % len(pieces))
-            make_h(u, j0, n)
-            if u == 7:
-                packed = interleave(nc.scalar.copy if i == SCALAR_CHUNK else nc.vector.tensor_copy, 1, j0, n)
-                if i + 1 < len(CHUNKS):
-                    quantize_h(1, packed, j0, n)
-                    finish(j0, n)
-                else:
-                    accs = open_last(j0, n)
-                    quantize_h(1, packed, j0, n)
-                    finish_last(accs, j0, n)
+        last = len(CHUNKS) - 1
+        waiting = None
+        for i, (j0, n) in enumerate(zip(starts, CHUNKS)):
+            tiles = [u for u in (7, 6) if u == 7 or j0 >= EARLY]
+            for u in tiles:
+                gate_piece(u, j0, n, i % NST)
+            for u in tiles:
+                make_h(u, j0, n)
+            if i == LATE:
+                quantize_h(0, packed1, BANK, BANK)
+            if i == 1 and OPEN0:
+                accs = open_last(*waiting[1:], "b_or_y")
+                quantize_h(1, *waiting)
+                finish_last(accs, *waiting[1:])
+            elif waiting:
+                quantize_h(1, *waiting)
+                finish(*waiting[1:])
+            copy = nc.scalar.copy if i < SCALAR_CHUNKS else nc.vector.tensor_copy
+            waiting = (interleave(copy, 1, j0, n, stage[i % NST][:].bitcast(BF16)[:, SLOTS * (PIECE - n) : SLOTS * PIECE]), j0, n)
+        accs = open_last(*waiting[1:])
+        quantize_h(1, *waiting)
+        finish_last(accs, *waiting[1:])

@@ -29,23 +29,14 @@ PASSES = 2
 TILES = PASSES * SLOTS
 OUT_TILES = N // P
 TILES_PER_BANK = 2
-CHUNKS = (256, 256, 256, 128, 128)
+CHUNKS = (128, 128, 256, 256, 128, 128)
 PIECE = max(CHUNKS)
 SCALAR_CHUNKS = 2
-PLAIN = 0
-EARLY = 0
-V_SHARE = 16
-POOL0 = 0
-POOL1 = 0
-LAP = 8
-HOLD = 1
-NST = 2
-OPEN0 = 1
-LATE = 1
-V_SHARE2 = 0
-ALIAS0 = 1
-ALIAS1 = 1
-GATE_BUFS, GATED_BUFS, B_BUFS, STAGE_BUFS, PSUM_BUFS = 4, 5, 7, 3, 4
+LEAD = 512
+SHIFT = 512
+USER_ROW = 8
+GATE_BUFS, PSUM_BUFS = 4, 8
+HALF = SLOTS // 2
 
 
 def tile_list_gated_preference_features_kernel(
@@ -54,110 +45,98 @@ def tile_list_gated_preference_features_kernel(
     nc = tc.nc
     with ExitStack() as ctx:
         keep = ctx.enter_context(tc.tile_pool(name="keep", bufs=1))
-        ring = ctx.enter_context(tc.tile_pool(name="ring", bufs=STAGE_BUFS))
+        ring = ctx.enter_context(tc.tile_pool(name="ring", bufs=GATE_BUFS))
         psum = ctx.enter_context(tc.psum_pool(name="psum", bufs=PSUM_BUFS))
+
+        def place(name, columns, dtype):
+            return keep.tile([P, columns], dtype, name=name, align_bytes=64)
 
         users = keep.tile([P, S // GROUP], U16, name="users")
         items = keep.tile([P, S // GROUP], U16, name="items")
-        item_scale_tab = keep.tile([P, T // 4], I32, name="item_scale_tab")
-        user_scale_tab = keep.tile([P, T // 4], I32, name="user_scale_tab")
-        wb_scale_raw = keep.tile([P, H // 4], I32, name="wb_scale_raw")
-        wb_code_raw = keep.tile([P, H // 2], I32, name="wb_code_raw")
-        item_code_tab = keep.tile([P, T], I32, name="item_code_tab", align_bytes=64)
-        user_code_tab = [keep.tile([P, T], I32, name=f"user_code_tab{s}", align_bytes=64) for s in range(PASSES)]
+        item_scale_tab = place("item_scale_tab", T // 4, I32)
+        user_scale_tab = place("user_scale_tab", T // 4, I32)
+        wb_scale_raw = place("wb_scale_raw", H // 4, I32)
+        wb_code_raw = place("wb_code_raw", H // 2, I32)
+        item_code_tab = place("big0", T, I32)
+        user_code_tab = [place(f"big{1 + s}", T, I32) for s in range(PASSES)]
         bias = keep.tile([P, OUT_TILES], F32, name="bias")
 
-        item_codes = keep.tile([P, S], U32, name="item_codes", align_bytes=64)
-        item_scales = keep.tile([P, S], U8, name="item_scales", align_bytes=64)
-        user_codes = [keep.tile([P, S], U32, name=f"user_codes{s}", align_bytes=64) for s in range(PASSES)]
-        user_scales = keep.tile([P, S], U8, name="user_scales", align_bytes=64)
-        wb_codes = keep.tile([P, 2 * H], U8, name="wb_codes", align_bytes=64)
-        wb_scale = keep.tile([P, H], U8, name="wb_scale", align_bytes=64)
-        h_tiles = {(1, bank): keep.tile([P, SLOTS, BANK], BF16, name=f"h_tiles1{bank}", align_bytes=64) for bank in range(2)}
-        h_codes = {}
-        h_scales = [keep.tile([P, S], U8, name=f"h_scales{s}", align_bytes=64) for s in range(PASSES)]
-        stage = [keep.tile([P, 3 * PIECE], F32, name=f"stage{e}", align_bytes=64) for e in range(NST)]
-        late = keep.tile([P, BANK], F32, name="late", align_bytes=64)
+        item_codes = place("item_codes", S, U32)
+        item_scales = place("item_scales", S, U8)
+        user_codes = [place(f"user_codes{s}", S, U32) for s in range(PASSES)]
+        user_scales = place("user_scales", S, U8)
+        wb_codes = place("wb_codes", 2 * H, U8)
+        wb_scale = place("wb_scale", H, U8)
+        starts = [sum(CHUNKS[:i]) for i in range(len(CHUNKS))]
+        last = len(CHUNKS) - 1
+        ROW = S + SHIFT
+        h1 = place("h1", SLOTS * ROW, F32)
+        h1_rows = h1[:].rearrange("p (t c) -> p t c", t=SLOTS)
+        packed1 = place("packed1", SLOTS * S, BF16)
+        h_codes = [place(f"h_codes{s}", S, U32) for s in range(PASSES)]
+        h_scales = [place(f"h_scales{s}", S, U8) for s in range(PASSES)]
         result = keep.tile([P, OUT_TILES, S], F32, name="result")
         out_rows = out.rearrange("(c p) j -> p c j", p=P)
 
-        gate, raw, rounded, codes, scales, b_tile, gated, a_sum = {}, {}, {}, {}, {}, {}, {}, {}
+        gate, raw, rounded, codes, scales, b_tile, product, a_sum = {}, {}, {}, {}, {}, {}, {}, {}
 
         def words(ap):
             return ap.rearrange("p t i -> p (t i)").bitcast(I32)
 
-        def load_scale_row(tile, source, r):
-            rows = source.rearrange("(q r) c -> r q c", r=SCALE_ROWS)[r]
-            nc.sync.dma_start(tile[r:P:QUAD, :], rows.bitcast(I32))
-
-        def load_user_scales(quad):
-            rows = tab_scales[:, SCALE_ROWS * quad : SCALE_ROWS * (quad + 1), :]
-            nc.sync.dma_start(user_scale_tab[QUAD * quad : QUAD * quad + PASSES * SCALE_ROWS, :], rows.bitcast(I32))
+        def load_scale_rows(tile, source, first):
+            for r in range(SCALE_ROWS):
+                rows = source.rearrange("(q r) c -> r q c", r=SCALE_ROWS)[r]
+                nc.sync.dma_start(tile[first + r : P : QUAD, :], rows.bitcast(I32))
 
         def factor_rows(ap, s):
             return ap[s * PASS : (s + 1) * PASS, :].rearrange("(g t i) c -> t g i c", t=SLOTS, i=RUN)
 
         def load_gate(u):
             s, t = divmod(u, SLOTS)
-            gate[u] = ring.tile([P, T], F32, name="gate", bufs=GATE_BUFS)
+            gate[u] = ring.tile([P, T], F32, name="gate")
             nc.sync.dma_start(gate[u][:], factor_rows(gT, s)[t])
 
-        def load_wa(s, ks):
-            key = ("wa", s, ks)
-            if (s, ks) == (1, 1):
-                raw[key] = keep.tile([P, SLOTS, PASS], F32, name="item_code_tab", align_bytes=64)
-            else:
-                raw[key] = ring.tile([P, SLOTS, PASS], F32, name="raw", align_bytes=64)
+        def load_wa(s, ks, name):
+            raw["wa", s, ks] = place(name, SLOTS * PASS, F32)
             rows = wa[ks * PASS : (ks + 1) * PASS, s * PASS : (s + 1) * PASS]
-            nc.sync.dma_start(raw[key][:], rows.rearrange("(p j) c -> p j c", j=SLOTS))
-
-        def load_wo(s):
-            key = ("wo", s, 0)
-            raw[key] = keep.tile([P, SLOTS, N], F32, name=f"user_code_tab{s}", align_bytes=64)
-            for t in range(SLOTS):
-                nc.sync.dma_start(raw[key][:, t, :], factor_rows(wo, s)[t])
-
-        def round_wa(s, ks, share=0):
-            key = ("wa", s, ks)
-            if (s, ks) == (1, 1):
-                rounded[key] = keep.tile([P, SLOTS * PASS], BF16, name="rounded11", align_bytes=64)
-            else:
-                rounded[key] = ring.tile([P, SLOTS * PASS], BF16, name="rounded", bufs=2, align_bytes=64)
-            dest = rounded[key][:].rearrange("p (t g i j) -> p g t j i", t=SLOTS, i=RUN, j=SLOTS)
-            source = raw[key][:].rearrange("p j (g t i) -> p g t j i", t=SLOTS, i=RUN)
-            if share < QUAD:
-                nc.scalar.copy(dest[:, share:], source[:, share:])
-            if share:
-                nc.vector.tensor_copy(dest[:, :share], source[:, :share])
-
-        def round_wo(s):
-            key = ("wo", s, 0)
-            if s == 0:
-                rounded[key] = keep.tile([P, SLOTS * N], BF16, name="h_tiles00", align_bytes=64)
-            else:
-                rounded[key] = ring.tile([P, SLOTS * N], BF16, name="rounded", bufs=2, align_bytes=64)
-            nc.scalar.copy(
-                rounded[key][:].rearrange("p (c i t) -> p c t i", i=RUN, t=SLOTS),
-                raw[key][:].rearrange("p t (c i) -> p c t i", i=RUN),
+            nc.sync.dma_start(
+                raw["wa", s, ks][:].rearrange("p (j c) -> p j c", j=SLOTS), rows.rearrange("(p j) c -> p j c", j=SLOTS)
             )
 
-        def quantize_weight(name, s, ks, place=None):
-            key = (name, s, ks)
-            codes[key] = keep.tile([P, PASS], U32, name=place or f"codes_{name}{s}{ks}", align_bytes=64)
-            scales[key] = keep.tile([P, PASS], U8, name=f"scales_{name}{s}{ks}", align_bytes=64)
-            nc.vector.quantize_mx(codes[key][:].bitcast(FP8X4), scales[key][:], rounded[key][:])
+        def load_wo(s, name, slots):
+            if slots[0] == 0:
+                raw["wo", s, 0] = place(name, SLOTS * N, F32)
+            for t in slots:
+                nc.sync.dma_start(raw["wo", s, 0][:, N * t : N * (t + 1)], factor_rows(wo, s)[t])
 
-        def make_b(u):
-            if u != 4:
-                whole = ring.tile([P, S], F32, name="b_tile", bufs=B_BUFS)
-                b_tile[u] = whole[:]
+        def round_wa(s, ks, t0, tiles, name, on_vector=0):
+            rounded["wa", s, ks, t0] = place(name, tiles * PASS, BF16)
+            dest = rounded["wa", s, ks, t0][:].rearrange("p (t g i j) -> p g t j i", t=tiles, i=RUN, j=SLOTS)
+            source = raw["wa", s, ks][:].rearrange("p (j g t i) -> p g t j i", j=SLOTS, t=SLOTS, i=RUN)
+            split = tiles - on_vector
+            nc.scalar.copy(dest[:, :, :split], source[:, :, t0 : t0 + split])
+            if on_vector:
+                nc.vector.tensor_copy(dest[:, :, split:], source[:, :, t0 + split : t0 + tiles])
+
+        def round_wo(s, name):
+            rounded["wo", s, 0, 0] = place(name, SLOTS * N, BF16)
+            nc.scalar.copy(
+                rounded["wo", s, 0, 0][:].rearrange("p (c i t) -> p c t i", i=RUN, t=SLOTS),
+                raw["wo", s, 0][:].rearrange("p (t c i) -> p c t i", t=SLOTS, i=RUN),
+            )
+
+        def quantize_weight(name, s, ks, t0, tiles, spot=None):
+            key = (name, s, ks)
+            if t0 == 0:
+                codes[key] = place(spot or f"codes_{name}{s}{ks}", PASS, U32)
+                scales[key] = place(f"scales_{name}{s}{ks}", PASS, U8)
+            cols = slice(P * t0, P * (t0 + tiles))
+            nc.vector.quantize_mx(codes[key][:, cols].bitcast(FP8X4), scales[key][:, cols], rounded[name, s, ks, t0][:])
+
+        def make_b(u, halves):
+            b_tile[u] = halves
             for j0 in range(0, S, BANK):
-                if u == 4:
-                    half = keep.tile([P, BANK], F32, name=f"h_tiles0{j0 // BANK}", align_bytes=64)
-                    b_tile[u, j0] = half[:]
-                else:
-                    b_tile[u, j0] = whole[:, j0 : j0 + BANK]
-                acc = psum.tile([P, BANK], F32, name="b_or_y")
+                acc = psum.tile([P, BANK], F32, name="bank")
                 nc.tensor.matmul_mx(
                     acc[:],
                     lhsT=wb_codes[:, 2 * P * u : 2 * P * (u + 1)].bitcast(FP4X4),
@@ -167,102 +146,68 @@ def tile_list_gated_preference_features_kernel(
                     start=True,
                     stop=True,
                 )
-                nc.scalar.copy(b_tile[u, j0], acc[:])
+                nc.scalar.copy(halves[j0 // BANK], acc[:])
 
-        def gate_b(dest, u, j0, n):
+        def gate_times(dest, u, factor, j0, n):
             picked = gate[u][:].indirect(users[:, j0 // GROUP : (j0 + n) // GROUP])
-            nc.vector.tensor_tensor(dest, picked, b_tile[u, j0] if u == 4 else b_tile[u][:, j0 : j0 + n], MULT)
+            nc.vector.tensor_tensor(dest, picked, factor, MULT)
 
-        def gate_tile(u, n):
-            whole = keep.tile([P, S], F32, name="rounded11" if u == 5 else f"gated{u}", align_bytes=64)
-            for j0 in range(0, n, BANK):
-                gated[u, j0] = whole[:, j0 : min(n, j0 + BANK)]
-            if u < PLAIN:
-                nc.vector.tensor_copy(whole[:, :n], gate[u][:].indirect(users[:, : n // GROUP]))
-                nc.gpsimd.tensor_tensor(whole[:, :n], whole[:, :n], b_tile[u][:, :n], MULT)
-            elif u == 4:
-                for j0 in range(0, S, BANK):
-                    gate_b(gated[u, j0], u, j0, BANK)
-            else:
-                gate_b(whole[:, :n], u, 0, n)
+        def halves(ap):
+            return [ap[:, :BANK], ap[:, BANK:]]
 
-        def gate_piece(u, j0, n, e):
-            if u == 7 and j0 == (CHUNKS[0] if HOLD else 0):
-                gated[u, j0] = late[:, :n]
-            elif u == 7:
-                gated[u, j0] = stage[(e - 1) % NST][:, 2 * PIECE : 2 * PIECE + n]
-            else:
-                gated[u, j0] = stage[e][:, 2 * PIECE + LAP - n : 2 * PIECE + LAP]
-            gate_b(gated[u, j0], u, j0, n)
+        def gate_b(u, name):
+            product[u] = place(name, S, F32)[:]
+            gate_times(product[u], u, b_whole[u], 0, S)
 
-        def make_a(u, bank):
-            s, t = divmod(u, SLOTS)
-            pairs = slice(bank * BANK, (bank + 1) * BANK)
-            a_sum[u, bank] = psum.tile([P, BANK], F32, name="a_or_last_y")
-            for ks in range(PASSES):
-                key = ("wa", s, ks)
-                nc.tensor.matmul_mx(
-                    a_sum[u, bank][:],
-                    lhsT=codes[key][:, P * t : P * (t + 1)].bitcast(FP8X4),
-                    lhsT_scale=scales[key][:, P * t : P * (t + 1)],
-                    rhs=user_codes[ks][:, pairs].bitcast(FP8X4),
-                    rhs_scale=user_scales[SCALE_ROWS * ks : P, pairs],
-                    start=(ks == 0),
-                    stop=(ks == PASSES - 1),
-                )
+        def pool_a_b(u, name):
+            a_copy = place(name, S, F32)[:]
+            times_a(u, None, halves(a_copy))
+            nc.gpsimd.tensor_tensor(product[u], a_copy, b_whole[u], MULT)
 
-        def make_h(u, j0, n):
-            s, t = divmod(u, SLOTS)
-            bank, c0 = divmod(j0, BANK)
-            nc.vector.tensor_tensor(h_tiles[s, bank][:, t, c0 : c0 + n], a_sum[u, bank][:, c0 : c0 + n], gated[u, j0], MULT)
-
-        def make_h_tile(u, pool_pairs=0):
+        def times_a(u, factor, dest):
             s, t = divmod(u, SLOTS)
             for bank in range(S // BANK):
-                j0 = bank * BANK
-                make_a(u, bank)
-                n = min(BANK, max(0, pool_pairs - j0))
-                if n:
-                    a_copy = ring.tile([P, BANK], F32, name="a_copy", bufs=2)
-                    nc.scalar.copy(a_copy[:, :n], a_sum[u, bank][:, :n])
-                    nc.gpsimd.tensor_tensor(h_tiles[s, bank][:, t, :n], a_copy[:, :n], gated[u, j0][:, :n], MULT)
-                if n < BANK:
-                    nc.vector.tensor_tensor(
-                        h_tiles[s, bank][:, t, n:], a_sum[u, bank][:, n:], gated[u, j0][:, n:], MULT
+                pairs = slice(bank * BANK, (bank + 1) * BANK)
+                acc = psum.tile([P, BANK], F32, name="bank")
+                for ks in range(PASSES):
+                    key = ("wa", s, ks)
+                    nc.tensor.matmul_mx(
+                        acc[:],
+                        lhsT=codes[key][:, P * t : P * (t + 1)].bitcast(FP8X4),
+                        lhsT_scale=scales[key][:, P * t : P * (t + 1)],
+                        rhs=user_codes[ks][:, pairs].bitcast(FP8X4),
+                        rhs_scale=user_scales[USER_ROW + SCALE_ROWS * ks : P, pairs],
+                        start=(ks == 0),
+                        stop=(ks == PASSES - 1),
                     )
+                if isinstance(dest[bank], list):
+                    for e, part in enumerate(dest[bank]):
+                        cols = slice(e * PIECE, (e + 1) * PIECE)
+                        nc.vector.tensor_tensor(part, acc[:, cols], factor[bank][:, cols], MULT)
+                elif factor:
+                    nc.vector.tensor_tensor(dest[bank], acc[:], factor[bank], MULT)
+                else:
+                    nc.scalar.copy(dest[bank], acc[:])
 
-        def interleave(copy, s, j0, n, packed=None):
-            if packed is None:
-                packed = ring.tile([P, SLOTS * n], BF16, name="packed", bufs=2, align_bytes=64)
-                packed = packed[:]
-            step = min(n, PIECE)
-            for c0 in range(0, n, step):
-                copy(
-                    packed[:, SLOTS * c0 : SLOTS * (c0 + step)].rearrange("p (c i t) -> p c t i", i=RUN, t=SLOTS),
-                    h_tiles[s, j0 // BANK][:, :, j0 % BANK + c0 : j0 % BANK + c0 + step].rearrange("p t (c i) -> p c t i", i=RUN),
-                )
-            return packed
-
-        def spent(key):
-            return raw[key][:].rearrange("p j c -> p (j c)").bitcast(BF16)[:, : SLOTS * BANK]
+        def interleave(copy, packed, rows):
+            copy(
+                packed.rearrange("p (c i t) -> p c t i", i=RUN, t=SLOTS),
+                rows.rearrange("p t (c i) -> p c t i", i=RUN),
+            )
 
         def quantize_h(s, packed, j0, n):
-            bank, c0 = divmod(j0, BANK)
-            if c0 == 0:
-                place = "late" if (s, bank) == (0, 1) else f"h_codes{s}{bank}"
-                h_codes[s, bank] = keep.tile([P, BANK], U32, name=place, align_bytes=64)
-            nc.vector.quantize_mx(h_codes[s, bank][:, c0 : c0 + n].bitcast(FP8X4), h_scales[s][:, j0 : j0 + n], packed)
+            nc.vector.quantize_mx(h_codes[s][:, j0 : j0 + n].bitcast(FP8X4), h_scales[s][:, j0 : j0 + n], packed)
 
-        def y_pass(acc, c, s, j0, n):
+        def y_pass(acc, c, s, j0, n, start, stop):
             key = ("wo", s, 0)
             nc.tensor.matmul_mx(
                 acc,
                 lhsT=codes[key][:, P * c : P * (c + 1)].bitcast(FP8X4),
                 lhsT_scale=scales[key][:, P * c : P * (c + 1)],
-                rhs=h_codes[s, j0 // BANK][:, j0 % BANK : j0 % BANK + n].bitcast(FP8X4),
+                rhs=h_codes[s][:, j0 : j0 + n].bitcast(FP8X4),
                 rhs_scale=h_scales[s][:, j0 : j0 + n],
-                start=(s == 0),
-                stop=(s == PASSES - 1),
+                start=start,
+                stop=stop,
             )
 
         def tanh_out(c, acc, j0, n):
@@ -272,130 +217,147 @@ def tile_list_gated_preference_features_kernel(
             tiles = slice(c0, c0 + TILES_PER_BANK)
             nc.sync.dma_start(out_rows[:, tiles, j0 : j0 + n], result[:, tiles, j0 : j0 + n])
 
-        def finish(j0, n):
-            for c0 in range(0, OUT_TILES, TILES_PER_BANK):
-                acc = psum.tile([P, TILES_PER_BANK, n], F32, name="b_or_y")
-                for c in range(c0, c0 + TILES_PER_BANK):
-                    for s in range(PASSES):
-                        y_pass(acc[:, c - c0, :], c, s, j0, n)
-                for c in range(c0, c0 + TILES_PER_BANK):
-                    tanh_out(c, acc[:, c - c0, :], j0, n)
-                store(c0, j0, n)
+        def open_sums(tiles, j0, n):
+            acc = psum.tile([P, len(tiles), n], F32, name="bank")
+            for e, c in enumerate(tiles):
+                y_pass(acc[:, e, :], c, 0, j0, n, e == 0, False)
+            return acc
 
-        def open_last(j0, n, tag="a_or_last_y"):
-            accs = [psum.tile([P, n], F32, name=tag) for c in range(OUT_TILES)]
-            for c in range(OUT_TILES):
-                y_pass(accs[c][:], c, 0, j0, n)
-            return accs
-
-        def finish_last(accs, j0, n):
-            for c in range(OUT_TILES):
-                y_pass(accs[c][:], c, 1, j0, n)
-                tanh_out(c, accs[c][:], j0, n)
+        def close_sums(acc, tiles, j0, n):
+            for e, c in enumerate(tiles):
+                y_pass(acc[:, e, :], c, 1, j0, n, False, e == len(tiles) - 1)
+            for e, c in enumerate(tiles):
+                tanh_out(c, acc[:, e, :], j0, n)
                 if (c + 1) % TILES_PER_BANK == 0:
                     store(c + 1 - TILES_PER_BANK, j0, n)
 
         nc.gpsimd.memset(item_scale_tab[:], 0)
         nc.vector.memset(wb_scale_raw[:], 0)
-        nc.vector.memset(user_scale_tab[:], 0)
+        nc.gpsimd.memset(user_scale_tab[:], 0)
 
         nc.sync.dma_start(items[:], offs2)
-        for r in range(SCALE_ROWS):
-            load_scale_row(item_scale_tab, tab2_scales[0], r)
+        load_scale_rows(item_scale_tab, tab2_scales[0], 0)
         nc.sync.dma_start(wb_code_raw[:], wb_words[0].bitcast(I32))
         nc.sync.dma_start(item_code_tab[:], words(tab2_words[0]))
-        for r in range(SCALE_ROWS):
-            load_scale_row(wb_scale_raw, wb_scales[0], r)
+        load_scale_rows(wb_scale_raw, wb_scales[0], 0)
         nc.sync.dma_start(users[:], offs)
-        nc.sync.dma_start(user_code_tab[0][:], words(tab_words[0]))
-        nc.sync.dma_start(user_code_tab[1][:], words(tab_words[1]))
-        for quad in range(QUADS):
-            load_gate(quad)
-            load_user_scales(quad)
-        load_wa(0, 0)
-        load_wa(0, 1)
-        load_gate(4)
-        load_wa(1, 0)
+        for s in range(PASSES):
+            nc.sync.dma_start(user_code_tab[s][:], words(tab_words[s]))
+        for s in range(PASSES):
+            load_scale_rows(user_scale_tab, tab_scales[s], USER_ROW + SCALE_ROWS * s)
+            if s == 0:
+                load_gate(0)
 
-        nc.vector.tensor_copy(item_scales[:], item_scale_tab[:].bitcast(U8).indirect(items[:]))
-        nc.vector.tensor_copy(item_codes[:], item_code_tab[:].bitcast(U32).indirect(items[:]))
-        nc.vector.tensor_copy(user_codes[0][:], user_code_tab[0][:].bitcast(U32).indirect(users[:]))
         nc.vector.tensor_copy(
             wb_codes[:].bitcast(I32).rearrange("p (s t g w) -> p s t g w", s=PASSES, t=SLOTS, w=2),
             wb_code_raw[:].rearrange("p (s g t w) -> p s t g w", s=PASSES, t=SLOTS, w=2),
         )
+        nc.vector.tensor_copy(item_scales[:], item_scale_tab[:].bitcast(U8).indirect(items[:]))
+        nc.vector.tensor_copy(item_codes[:], item_code_tab[:].bitcast(U32).indirect(items[:]))
         nc.vector.tensor_copy(
             wb_scale[:].bitcast(I32).rearrange("p (s t g) -> p s t g", s=PASSES, t=SLOTS),
             wb_scale_raw[:].rearrange("p (s g t) -> p s t g", s=PASSES, t=SLOTS),
         )
-        nc.vector.tensor_copy(user_codes[1][:], user_code_tab[1][:].bitcast(U32).indirect(users[:]))
-
-        for u in range(TILES):
-            make_b(u)
-        for u in range(SLOTS):
-            gate_tile(u, S)
+        for s in range(PASSES):
+            nc.vector.tensor_copy(user_codes[s][:], user_code_tab[s][:].bitcast(U32).indirect(users[:]))
         nc.vector.tensor_copy(user_scales[:], user_scale_tab[:].bitcast(U8).indirect(users[:]))
-        round_wa(0, 0)
-        round_wa(0, 1, V_SHARE)
-        load_wa(1, 1)
+
+        load_wa(0, 0, "big0")
+        load_gate(1)
+        load_wa(0, 1, "big3")
+        load_gate(2)
+        load_wa(1, 0, "big1")
+        load_gate(3)
+        load_wa(1, 1, "big2")
+
+        b_whole = {}
+        for u in range(5):
+            b_whole[u] = place(f"b{u}", S, F32)[:]
+            make_b(u, halves(b_whole[u]))
+        gate_b(0, "product0")
+        round_wa(0, 0, 0, SLOTS, "rounded_whole")
+        later_b = place("big0", 2 * S, F32)
+        for u in (5, 6):
+            b_whole[u] = later_b[:, (u - 5) * S : (u - 4) * S]
+            make_b(u, halves(b_whole[u]))
+        quantize_weight("wa", 0, 0, 0, SLOTS)
+        gate_b(1, "product1")
+        round_wa(0, 1, 0, SLOTS, "rounded_first", 2)
+        load_wo(0, "big4", (0,))
+        load_gate(4)
+        load_wo(0, "big4", (1, 2, 3))
         load_gate(5)
-        load_wo(0)
-        quantize_weight("wa", 0, 0)
-        quantize_weight("wa", 0, 1)
-        round_wa(1, 0)
-        load_wo(1)
-        load_gate(6)
-        load_gate(7)
+        make_b(TILES - 1, halves(place("big3", S, F32)[:]))
+        quantize_weight("wa", 0, 1, 0, SLOTS)
+        gate_b(2, "product2")
+        h0 = keep.tile([P, SLOTS, S], F32, name="h0", align_bytes=64)
+        product[3] = place("b2", S, F32)[:]
+        pool_a_b(3, "b0")
+        round_wa(1, 0, 0, SLOTS, "rounded_whole")
+        for u in range(SLOTS - 1):
+            times_a(u, halves(product[u]), halves(h0[:, u, :]))
+        quantize_weight("wa", 1, 0, 0, SLOTS)
+        for bank in range(2):
+            gate_times(halves(h0[:, 3, :])[bank], 3, halves(product[3])[bank], bank * BANK, BANK)
+
+        load_wo(1, "big1", (0, 1, 2, 3))
         with nc.allow_non_contiguous_dma(reason="one bias value for each partition and output tile"):
             nc.sync.dma_start(bias[:], bo.rearrange("(c p) -> p c", p=P))
-        round_wa(1, 1, V_SHARE2)
-        gate_tile(4, S)
-        for bank in range(2):
-            h_tiles[0, bank] = keep.tile([P, SLOTS, BANK], BF16, name=f"h_tiles0{bank}", align_bytes=64)
-        for u in range(SLOTS):
-            make_h_tile(u, POOL0 - u * S)
+        load_gate(6)
+        load_gate(7)
+        round_wa(1, 1, 0, HALF, "product4")
+        round_wa(1, 1, HALF, HALF, "rounded_half")
+        quantize_weight("wa", 1, 1, 0, HALF)
+        quantize_weight("wa", 1, 1, HALF, HALF)
+        gate_b(4, "product4")
+        product[5] = place("b4", S, F32)[:]
+        pool_a_b(5, "b1")
+        packed0 = place("big2", SLOTS * S, BF16)
+        for j0 in range(0, S, PIECE):
+            interleave(nc.scalar.copy, packed0[:, SLOTS * j0 : SLOTS * (j0 + PIECE)], h0[:, :, j0 : j0 + PIECE])
+        round_wo(0, "rounded_whole")
+        round_wo(1, "product2")
+        product[6] = place("product0", S, F32)[:]
+        product[7] = h1_rows[:, 2, SHIFT:]
+        lead = [place(f"lead{e}", PIECE, F32)[:] for e in range(2)]
+        times_a(6, b_tile[6], [lead, halves(product[6])[1]])
+        times_a(7, b_tile[7], halves(product[7]))
+        times_a(4, halves(product[4]), halves(h1_rows[:, 0, :S]))
+        for j0 in range(0, S, BANK):
+            quantize_h(0, packed0[:, SLOTS * j0 : SLOTS * (j0 + BANK)], j0, BANK)
+        quantize_weight("wo", 0, 0, 0, SLOTS)
+        gate_times(h1_rows[:, 1, :S], 5, product[5], 0, S)
+        for e in range(2):
+            gate_times(h1_rows[:, 2, e * PIECE : (e + 1) * PIECE], 6, lead[e], e * PIECE, PIECE)
+        quantize_weight("wo", 1, 0, 0, SLOTS, "lead0")
 
-        quantize_weight("wa", 1, 0, "gated2")
-        quantize_weight("wa", 1, 1, "gated3")
-        packed0 = interleave(nc.scalar.copy, 0, 0, BANK, spent(("wa", 1, 1)) if ALIAS0 else None)
-        round_wo(0)
-        round_wo(1)
-        packed1 = interleave(nc.scalar.copy, 0, BANK, BANK, spent(("wo", 1, 0)) if ALIAS1 else None)
-        gate_tile(5, S)
-        make_h_tile(4, POOL1)
-        make_h_tile(5)
-        quantize_h(0, packed0, 0, BANK)
-        quantize_weight("wo", 0, 0, "rounded11")
-        quantize_weight("wo", 1, 0, "gated4")
-        if EARLY:
-            gate_tile(6, EARLY)
-        make_a(6, 0)
-        if EARLY:
-            make_h(6, 0, EARLY)
-        make_a(7, 0)
-        make_a(6, 1)
-        make_a(7, 1)
+        groups = []
+        for i, n in enumerate(CHUNKS):
+            width = TILES_PER_BANK if i == last else BANK // n
+            groups.append([tuple(range(c0, c0 + width)) for c0 in range(0, OUT_TILES, width)])
+        sums = {}
+        for i, (j0, n) in enumerate(zip(starts, CHUNKS)):
+            for tiles in groups[i][: 1 if i == last else None]:
+                sums[i, tiles] = open_sums(tiles, j0, n)
 
-        starts = [sum(CHUNKS[:i]) for i in range(len(CHUNKS))]
-        last = len(CHUNKS) - 1
+        def finish(i, parts):
+            for part in parts:
+                quantize_h(1, *part)
+            for tiles in groups[i]:
+                close_sums(sums[i, tiles], tiles, starts[i], CHUNKS[i])
+            if i == 0:
+                tiles = groups[last][1]
+                sums[last, tiles] = open_sums(tiles, starts[last], CHUNKS[last])
+
         waiting = None
         for i, (j0, n) in enumerate(zip(starts, CHUNKS)):
-            tiles = [u for u in (7, 6) if u == 7 or j0 >= EARLY]
-            for u in tiles:
-                gate_piece(u, j0, n, i % NST)
-            for u in tiles:
-                make_h(u, j0, n)
-            if i == LATE:
-                quantize_h(0, packed1, BANK, BANK)
-            if i == 1 and OPEN0:
-                accs = open_last(*waiting[1:], "b_or_y")
-                quantize_h(1, *waiting)
-                finish_last(accs, *waiting[1:])
-            elif waiting:
-                quantize_h(1, *waiting)
-                finish(*waiting[1:])
+            if j0 >= LEAD:
+                gate_times(h1_rows[:, 2, j0 : j0 + n], 6, product[6][:, j0 : j0 + n], j0, n)
+            gate_times(h1_rows[:, 3, j0 : j0 + n], 7, product[7][:, j0 : j0 + n], j0, n)
+            if waiting:
+                finish(i - 1, waiting)
+            waiting = [(packed1[:, SLOTS * j0 : SLOTS * (j0 + n)], j0, n)]
             copy = nc.scalar.copy if i < SCALAR_CHUNKS else nc.vector.tensor_copy
-            waiting = (interleave(copy, 1, j0, n, stage[i % NST][:].bitcast(BF16)[:, SLOTS * (PIECE - n) : SLOTS * PIECE]), j0, n)
-        accs = open_last(*waiting[1:])
-        quantize_h(1, *waiting)
-        finish_last(accs, *waiting[1:])
+            for packed, c0, m in waiting:
+                interleave(copy, packed, h1_rows[:, :, c0 : c0 + m])
+        finish(last, waiting)

@@ -30,13 +30,16 @@ TILES = PASSES * SLOTS
 OUT_TILES = N // P
 TILES_PER_BANK = 2
 CHUNKS = (128, 128, 256, 256, 128, 128)
-PIECE = max(CHUNKS)
-SCALAR_CHUNKS = 2
+PIECE = 256
 LEAD = 512
-SHIFT = 512
+AHEAD = 256
+ROW = S + LEAD
 USER_ROW = 8
 GATE_BUFS, PSUM_BUFS = 4, 8
 HALF = SLOTS // 2
+OPEN_AHEAD = PSUM_BUFS // OUT_TILES
+TILES_PER_STORE = 2
+OFFSETS = {"low": 0, "rounded2": 1024, "high": 2048}
 
 
 def tile_list_gated_preference_features_kernel(
@@ -48,7 +51,11 @@ def tile_list_gated_preference_features_kernel(
         ring = ctx.enter_context(tc.tile_pool(name="ring", bufs=GATE_BUFS))
         psum = ctx.enter_context(tc.psum_pool(name="psum", bufs=PSUM_BUFS))
 
+        spots = ctx.enter_context(tc.tile_pool(name="spots", bufs=1))
+
         def place(name, columns, dtype):
+            if name in OFFSETS:
+                return spots.tile([P, columns], dtype, name=name, align_bytes=64, offset=OFFSETS[name])
             return keep.tile([P, columns], dtype, name=name, align_bytes=64)
 
         users = keep.tile([P, S // GROUP], U16, name="users")
@@ -67,26 +74,18 @@ def tile_list_gated_preference_features_kernel(
         user_scales = place("user_scales", S, U8)
         wb_codes = place("wb_codes", 2 * H, U8)
         wb_scale = place("wb_scale", H, U8)
-        starts = [sum(CHUNKS[:i]) for i in range(len(CHUNKS))]
-        last = len(CHUNKS) - 1
-        ROW = S + SHIFT
-        h1 = place("h1", SLOTS * ROW, F32)
-        h1_rows = h1[:].rearrange("p (t c) -> p t c", t=SLOTS)
-        packed1 = place("packed1", SLOTS * S, BF16)
         h_codes = [place(f"h_codes{s}", S, U32) for s in range(PASSES)]
         h_scales = [place(f"h_scales{s}", S, U8) for s in range(PASSES)]
-        result = keep.tile([P, OUT_TILES, S], F32, name="result")
         out_rows = out.rearrange("(c p) j -> p c j", p=P)
 
-        gate, raw, rounded, codes, scales, b_tile, product, a_sum = {}, {}, {}, {}, {}, {}, {}, {}
+        gate, raw, rounded, codes, scales = {}, {}, {}, {}, {}
 
         def words(ap):
             return ap.rearrange("p t i -> p (t i)").bitcast(I32)
 
-        def load_scale_rows(tile, source, first):
-            for r in range(SCALE_ROWS):
-                rows = source.rearrange("(q r) c -> r q c", r=SCALE_ROWS)[r]
-                nc.sync.dma_start(tile[first + r : P : QUAD, :], rows.bitcast(I32))
+        def load_scale_row(tile, source, first, r):
+            rows = source.rearrange("(q r) c -> r q c", r=SCALE_ROWS)[r]
+            nc.sync.dma_start(tile[first + r : P : QUAD, :], rows.bitcast(I32))
 
         def factor_rows(ap, s):
             return ap[s * PASS : (s + 1) * PASS, :].rearrange("(g t i) c -> t g i c", t=SLOTS, i=RUN)
@@ -103,38 +102,36 @@ def tile_list_gated_preference_features_kernel(
                 raw["wa", s, ks][:].rearrange("p (j c) -> p j c", j=SLOTS), rows.rearrange("(p j) c -> p j c", j=SLOTS)
             )
 
-        def load_wo(s, name, slots):
-            if slots[0] == 0:
-                raw["wo", s, 0] = place(name, SLOTS * N, F32)
-            for t in slots:
-                nc.sync.dma_start(raw["wo", s, 0][:, N * t : N * (t + 1)], factor_rows(wo, s)[t])
+        def load_wo(s, dest):
+            raw["wo", s, 0] = dest
+            for t in range(SLOTS):
+                nc.sync.dma_start(dest[:, N * t : N * (t + 1)], factor_rows(wo, s)[t])
 
-        def round_wa(s, ks, t0, tiles, name, on_vector=0):
+        def round_wa(copy, s, ks, t0, tiles, name):
             rounded["wa", s, ks, t0] = place(name, tiles * PASS, BF16)
             dest = rounded["wa", s, ks, t0][:].rearrange("p (t g i j) -> p g t j i", t=tiles, i=RUN, j=SLOTS)
             source = raw["wa", s, ks][:].rearrange("p (j g t i) -> p g t j i", j=SLOTS, t=SLOTS, i=RUN)
-            split = tiles - on_vector
-            nc.scalar.copy(dest[:, :, :split], source[:, :, t0 : t0 + split])
-            if on_vector:
-                nc.vector.tensor_copy(dest[:, :, split:], source[:, :, t0 + split : t0 + tiles])
+            copy(dest, source[:, :, t0 : t0 + tiles])
 
         def round_wo(s, name):
             rounded["wo", s, 0, 0] = place(name, SLOTS * N, BF16)
             nc.scalar.copy(
                 rounded["wo", s, 0, 0][:].rearrange("p (c i t) -> p c t i", i=RUN, t=SLOTS),
-                raw["wo", s, 0][:].rearrange("p (t c i) -> p c t i", t=SLOTS, i=RUN),
+                raw["wo", s, 0].rearrange("p (t c i) -> p c t i", t=SLOTS, i=RUN),
             )
 
-        def quantize_weight(name, s, ks, t0, tiles, spot=None):
-            key = (name, s, ks)
-            if t0 == 0:
-                codes[key] = place(spot or f"codes_{name}{s}{ks}", PASS, U32)
-                scales[key] = place(f"scales_{name}{s}{ks}", PASS, U8)
-            cols = slice(P * t0, P * (t0 + tiles))
-            nc.vector.quantize_mx(codes[key][:, cols].bitcast(FP8X4), scales[key][:, cols], rounded[name, s, ks, t0][:])
+        def quantize_weight(name, s, part, t0, tiles, spot=None):
+            made = place(spot or f"codes_{name}{s}{part}{t0}", P * tiles, U32)
+            scale = place(f"scales_{name}{s}{part}{t0}", P * tiles, U8)
+            nc.vector.quantize_mx(made[:].bitcast(FP8X4), scale[:], rounded[name, s, part, t0][:])
+            for e in range(tiles):
+                codes[name, s, part, t0 + e] = made[:, P * e : P * (e + 1)].bitcast(FP8X4)
+                scales[name, s, part, t0 + e] = scale[:, P * e : P * (e + 1)]
 
-        def make_b(u, halves):
-            b_tile[u] = halves
+        def halves(ap):
+            return [ap[:, :BANK], ap[:, BANK:]]
+
+        def make_b(u, dest):
             for j0 in range(0, S, BANK):
                 acc = psum.tile([P, BANK], F32, name="bank")
                 nc.tensor.matmul_mx(
@@ -146,113 +143,100 @@ def tile_list_gated_preference_features_kernel(
                     start=True,
                     stop=True,
                 )
-                nc.scalar.copy(halves[j0 // BANK], acc[:])
+                nc.scalar.copy(dest[:, j0 : j0 + BANK], acc[:])
 
         def gate_times(dest, u, factor, j0, n):
             picked = gate[u][:].indirect(users[:, j0 // GROUP : (j0 + n) // GROUP])
             nc.vector.tensor_tensor(dest, picked, factor, MULT)
 
-        def halves(ap):
-            return [ap[:, :BANK], ap[:, BANK:]]
-
-        def gate_b(u, name):
-            product[u] = place(name, S, F32)[:]
-            gate_times(product[u], u, b_whole[u], 0, S)
-
-        def pool_a_b(u, name):
-            a_copy = place(name, S, F32)[:]
-            times_a(u, None, halves(a_copy))
-            nc.gpsimd.tensor_tensor(product[u], a_copy, b_whole[u], MULT)
+        def make_a(u, bank):
+            s, t = divmod(u, SLOTS)
+            pairs = slice(bank * BANK, (bank + 1) * BANK)
+            acc = psum.tile([P, BANK], F32, name="bank")
+            for ks in range(PASSES):
+                nc.tensor.matmul_mx(
+                    acc[:],
+                    lhsT=codes["wa", s, ks, t],
+                    lhsT_scale=scales["wa", s, ks, t],
+                    rhs=user_codes[ks][:, pairs].bitcast(FP8X4),
+                    rhs_scale=user_scales[USER_ROW + SCALE_ROWS * ks : P, pairs],
+                    start=(ks == 0),
+                    stop=(ks == PASSES - 1),
+                )
+            return acc
 
         def times_a(u, factor, dest):
-            s, t = divmod(u, SLOTS)
             for bank in range(S // BANK):
-                pairs = slice(bank * BANK, (bank + 1) * BANK)
-                acc = psum.tile([P, BANK], F32, name="bank")
-                for ks in range(PASSES):
-                    key = ("wa", s, ks)
-                    nc.tensor.matmul_mx(
-                        acc[:],
-                        lhsT=codes[key][:, P * t : P * (t + 1)].bitcast(FP8X4),
-                        lhsT_scale=scales[key][:, P * t : P * (t + 1)],
-                        rhs=user_codes[ks][:, pairs].bitcast(FP8X4),
-                        rhs_scale=user_scales[USER_ROW + SCALE_ROWS * ks : P, pairs],
-                        start=(ks == 0),
-                        stop=(ks == PASSES - 1),
-                    )
-                if isinstance(dest[bank], list):
-                    for e, part in enumerate(dest[bank]):
-                        cols = slice(e * PIECE, (e + 1) * PIECE)
-                        nc.vector.tensor_tensor(part, acc[:, cols], factor[bank][:, cols], MULT)
-                elif factor:
-                    nc.vector.tensor_tensor(dest[bank], acc[:], factor[bank], MULT)
-                else:
-                    nc.scalar.copy(dest[bank], acc[:])
+                nc.vector.tensor_tensor(dest[bank], make_a(u, bank)[:], halves(factor)[bank], MULT)
 
-        def interleave(copy, packed, rows):
+        def pool_a_b(u, factor, dest):
+            for bank in range(S // BANK):
+                a_copy = place(f"a_copy{bank}", BANK, F32)
+                nc.scalar.copy(a_copy[:], make_a(u, bank)[:])
+                nc.gpsimd.tensor_tensor(dest[bank], a_copy[:], halves(factor)[bank], MULT)
+
+        def interleave(copy, packed, rows, j0, n):
             copy(
-                packed.rearrange("p (c i t) -> p c t i", i=RUN, t=SLOTS),
-                rows.rearrange("p t (c i) -> p c t i", i=RUN),
+                packed[:, SLOTS * j0 : SLOTS * (j0 + n)].rearrange("p (c i t) -> p c t i", i=RUN, t=SLOTS),
+                rows[:, :, j0 : j0 + n].rearrange("p t (c i) -> p c t i", i=RUN),
             )
 
         def quantize_h(s, packed, j0, n):
-            nc.vector.quantize_mx(h_codes[s][:, j0 : j0 + n].bitcast(FP8X4), h_scales[s][:, j0 : j0 + n], packed)
+            nc.vector.quantize_mx(
+                h_codes[s][:, j0 : j0 + n].bitcast(FP8X4),
+                h_scales[s][:, j0 : j0 + n],
+                packed[:, SLOTS * j0 : SLOTS * (j0 + n)],
+            )
 
         def y_pass(acc, c, s, j0, n, start, stop):
-            key = ("wo", s, 0)
             nc.tensor.matmul_mx(
                 acc,
-                lhsT=codes[key][:, P * c : P * (c + 1)].bitcast(FP8X4),
-                lhsT_scale=scales[key][:, P * c : P * (c + 1)],
+                lhsT=codes["wo", s, 0, c],
+                lhsT_scale=scales["wo", s, 0, c],
                 rhs=h_codes[s][:, j0 : j0 + n].bitcast(FP8X4),
                 rhs_scale=h_scales[s][:, j0 : j0 + n],
                 start=start,
                 stop=stop,
             )
 
-        def tanh_out(c, acc, j0, n):
-            nc.scalar.activation(result[:, c, j0 : j0 + n], acc, TANH, bias=bias[:, c : c + 1])
+        def open_sums(j0, n):
+            banks = [psum.tile([P, n], F32, name="bank") for c in range(OUT_TILES)]
+            for c, acc in enumerate(banks):
+                y_pass(acc[:], c, 0, j0, n, True, False)
+            return banks
 
-        def store(c0, j0, n):
-            tiles = slice(c0, c0 + TILES_PER_BANK)
-            nc.sync.dma_start(out_rows[:, tiles, j0 : j0 + n], result[:, tiles, j0 : j0 + n])
-
-        def open_sums(tiles, j0, n):
-            acc = psum.tile([P, len(tiles), n], F32, name="bank")
-            for e, c in enumerate(tiles):
-                y_pass(acc[:, e, :], c, 0, j0, n, e == 0, False)
-            return acc
-
-        def close_sums(acc, tiles, j0, n):
-            for e, c in enumerate(tiles):
-                y_pass(acc[:, e, :], c, 1, j0, n, False, e == len(tiles) - 1)
-            for e, c in enumerate(tiles):
-                tanh_out(c, acc[:, e, :], j0, n)
-                if (c + 1) % TILES_PER_BANK == 0:
-                    store(c + 1 - TILES_PER_BANK, j0, n)
+        def close_sums(banks, j0, n):
+            for c, acc in enumerate(banks):
+                y_pass(acc[:], c, 1, j0, n, False, True)
+            for c, acc in enumerate(banks):
+                nc.scalar.activation(result[:, c, j0 : j0 + n], acc[:], TANH, bias=bias[:, c : c + 1])
+                if (c + 1) % TILES_PER_STORE == 0:
+                    stored = slice(c + 1 - TILES_PER_STORE, c + 1)
+                    nc.sync.dma_start(out_rows[:, stored, j0 : j0 + n], result[:, stored, j0 : j0 + n])
 
         nc.gpsimd.memset(item_scale_tab[:], 0)
         nc.vector.memset(wb_scale_raw[:], 0)
         nc.gpsimd.memset(user_scale_tab[:], 0)
 
         nc.sync.dma_start(items[:], offs2)
-        load_scale_rows(item_scale_tab, tab2_scales[0], 0)
+        for r in range(SCALE_ROWS):
+            load_scale_row(item_scale_tab, tab2_scales[0], 0, r)
         nc.sync.dma_start(wb_code_raw[:], wb_words[0].bitcast(I32))
         nc.sync.dma_start(item_code_tab[:], words(tab2_words[0]))
-        load_scale_rows(wb_scale_raw, wb_scales[0], 0)
+        for r in range(SCALE_ROWS):
+            load_scale_row(wb_scale_raw, wb_scales[0], 0, r)
         nc.sync.dma_start(users[:], offs)
-        for s in range(PASSES):
-            nc.sync.dma_start(user_code_tab[s][:], words(tab_words[s]))
-        for s in range(PASSES):
-            load_scale_rows(user_scale_tab, tab_scales[s], USER_ROW + SCALE_ROWS * s)
-            if s == 0:
-                load_gate(0)
+        for half in range(PASSES):
+            nc.sync.dma_start(user_code_tab[half][:], words(tab_words[half]))
+            for r in range(HALF * half, HALF * (half + 1)):
+                for s in range(PASSES):
+                    load_scale_row(user_scale_tab, tab_scales[s], USER_ROW + SCALE_ROWS * s, r)
 
+        nc.vector.tensor_copy(item_scales[:], item_scale_tab[:].bitcast(U8).indirect(items[:]))
         nc.vector.tensor_copy(
             wb_codes[:].bitcast(I32).rearrange("p (s t g w) -> p s t g w", s=PASSES, t=SLOTS, w=2),
             wb_code_raw[:].rearrange("p (s g t w) -> p s t g w", s=PASSES, t=SLOTS, w=2),
         )
-        nc.vector.tensor_copy(item_scales[:], item_scale_tab[:].bitcast(U8).indirect(items[:]))
         nc.vector.tensor_copy(item_codes[:], item_code_tab[:].bitcast(U32).indirect(items[:]))
         nc.vector.tensor_copy(
             wb_scale[:].bitcast(I32).rearrange("p (s t g) -> p s t g", s=PASSES, t=SLOTS),
@@ -263,101 +247,127 @@ def tile_list_gated_preference_features_kernel(
         nc.vector.tensor_copy(user_scales[:], user_scale_tab[:].bitcast(U8).indirect(users[:]))
 
         load_wa(0, 0, "big0")
-        load_gate(1)
         load_wa(0, 1, "big3")
-        load_gate(2)
+        load_gate(0)
         load_wa(1, 0, "big1")
-        load_gate(3)
+        load_gate(1)
+        load_gate(2)
         load_wa(1, 1, "big2")
+        load_gate(3)
+        load_wo(0, place("big4", SLOTS * N, F32)[:])
 
-        b_whole = {}
-        for u in range(5):
-            b_whole[u] = place(f"b{u}", S, F32)[:]
-            make_b(u, halves(b_whole[u]))
-        gate_b(0, "product0")
-        round_wa(0, 0, 0, SLOTS, "rounded_whole")
-        later_b = place("big0", 2 * S, F32)
-        for u in (5, 6):
-            b_whole[u] = later_b[:, (u - 5) * S : (u - 4) * S]
-            make_b(u, halves(b_whole[u]))
+        def pack_pair(copy, t0, j0, n):
+            copy(
+                packed1[:, SLOTS * j0 : SLOTS * (j0 + n)].rearrange("p (c t) -> p c t", t=SLOTS)[:, :, t0 : t0 + HALF],
+                h1[:, t0 : t0 + HALF, j0 : j0 + n].rearrange("p t c -> p c t"),
+            )
+
+        b, product = {}, {}
+        for u in range(3):
+            b[u] = place(f"b{u}", S, F32)[:]
+            make_b(u, b[u])
+        round_wa(nc.scalar.copy, 0, 0, 0, SLOTS, "rounded0")
+        round_wa(nc.scalar.copy, 0, 1, 0, HALF, "rounded1")
+        round_wa(nc.vector.tensor_copy, 0, 1, HALF, HALF, "rounded2")
+        later = place("big3", 2 * S, F32)
+        for u in (3, 4):
+            b[u] = later[:, (u - 3) * S : (u - 2) * S]
+            make_b(u, b[u])
         quantize_weight("wa", 0, 0, 0, SLOTS)
-        gate_b(1, "product1")
-        round_wa(0, 1, 0, SLOTS, "rounded_first", 2)
-        load_wo(0, "big4", (0,))
+        quantize_weight("wa", 0, 1, HALF, HALF)
+        quantize_weight("wa", 0, 1, 0, HALF)
+        product[0] = place("product0", S, F32)[:]
+        gate_times(product[0], 0, b[0], 0, S)
         load_gate(4)
-        load_wo(0, "big4", (1, 2, 3))
-        load_gate(5)
-        make_b(TILES - 1, halves(place("big3", S, F32)[:]))
-        quantize_weight("wa", 0, 1, 0, SLOTS)
-        gate_b(2, "product2")
         h0 = keep.tile([P, SLOTS, S], F32, name="h0", align_bytes=64)
-        product[3] = place("b2", S, F32)[:]
-        pool_a_b(3, "b0")
-        round_wa(1, 0, 0, SLOTS, "rounded_whole")
-        for u in range(SLOTS - 1):
-            times_a(u, halves(product[u]), halves(h0[:, u, :]))
+        stage = place("stage", 3 * ROW + AHEAD + 2 * S, F32)
+        h1 = stage[:, : SLOTS * ROW].rearrange("p (t c) -> p t c", t=SLOTS)
+        packed1 = stage[:, 3 * ROW + AHEAD :].bitcast(BF16)
+        for u in (1, 2):
+            product[u] = place(f"product{u}", S, F32)[:]
+        pooled = [place(f"pooled{e}", BANK, F32)[:] for e in range(2)]
+        pool_a_b(3, b[3], pooled)
+        times_a(1, b[1], halves(product[1]))
+        times_a(2, b[2], halves(product[2]))
+        times_a(0, product[0], halves(h0[:, 0, :]))
+        round_wa(nc.scalar.copy, 1, 0, 0, SLOTS, "rounded0")
+        later = place("big1", 3 * S, F32)
+        for u in (5, 6, 7):
+            b[u] = later[:, (u - 5) * S : (u - 4) * S]
+            make_b(u, b[u])
+        gate_times(h0[:, 1, :], 1, product[1], 0, S)
+        load_gate(5)
+        load_wo(1, stage[:, 3 * ROW + AHEAD :])
         quantize_weight("wa", 1, 0, 0, SLOTS)
-        for bank in range(2):
-            gate_times(halves(h0[:, 3, :])[bank], 3, halves(product[3])[bank], bank * BANK, BANK)
-
-        load_wo(1, "big1", (0, 1, 2, 3))
+        gate_times(h0[:, 2, :], 2, product[2], 0, S)
         with nc.allow_non_contiguous_dma(reason="one bias value for each partition and output tile"):
             nc.sync.dma_start(bias[:], bo.rearrange("(c p) -> p c", p=P))
         load_gate(6)
-        load_gate(7)
-        round_wa(1, 1, 0, HALF, "product4")
-        round_wa(1, 1, HALF, HALF, "rounded_half")
+        round_wa(nc.scalar.copy, 1, 1, 0, HALF, "rounded1")
+        round_wa(nc.scalar.copy, 1, 1, HALF, HALF, "rounded2")
         quantize_weight("wa", 1, 1, 0, HALF)
-        quantize_weight("wa", 1, 1, HALF, HALF)
-        gate_b(4, "product4")
-        product[5] = place("b4", S, F32)[:]
-        pool_a_b(5, "b1")
+        for e in range(2):
+            gate_times(halves(h0[:, 3, :])[e], 3, pooled[e], e * BANK, BANK)
+        load_gate(7)
+        quantize_weight("wa", 1, 1, HALF, HALF, "pooled0")
+        product[4] = place("product0", S, F32)[:]
+        product[6] = place("product2", S, F32)[:]
+        product[7] = h1[:, 2, LEAD:]
+        pooled = [place(name, BANK, F32)[:] for name in ("low", "high")]
+        pool_a_b(5, b[5], pooled)
         packed0 = place("big2", SLOTS * S, BF16)
         for j0 in range(0, S, PIECE):
-            interleave(nc.scalar.copy, packed0[:, SLOTS * j0 : SLOTS * (j0 + PIECE)], h0[:, :, j0 : j0 + PIECE])
-        round_wo(0, "rounded_whole")
-        round_wo(1, "product2")
-        product[6] = place("product0", S, F32)[:]
-        product[7] = h1_rows[:, 2, SHIFT:]
-        lead = [place(f"lead{e}", PIECE, F32)[:] for e in range(2)]
-        times_a(6, b_tile[6], [lead, halves(product[6])[1]])
-        times_a(7, b_tile[7], halves(product[7]))
-        times_a(4, halves(product[4]), halves(h1_rows[:, 0, :S]))
+            interleave(nc.scalar.copy, packed0, h0, j0, PIECE)
+        for u in (4, 6, 7):
+            times_a(u, b[u], halves(product[u]))
+        round_wo(0, "rounded0")
+        round_wo(1, "rounded1")
+        gate_times(h1[:, 0, :S], 4, product[4], 0, S)
         for j0 in range(0, S, BANK):
-            quantize_h(0, packed0[:, SLOTS * j0 : SLOTS * (j0 + BANK)], j0, BANK)
-        quantize_weight("wo", 0, 0, 0, SLOTS)
-        gate_times(h1_rows[:, 1, :S], 5, product[5], 0, S)
-        for e in range(2):
-            gate_times(h1_rows[:, 2, e * PIECE : (e + 1) * PIECE], 6, lead[e], e * PIECE, PIECE)
-        quantize_weight("wo", 1, 0, 0, SLOTS, "lead0")
+            quantize_h(0, packed0, j0, BANK)
+        gate_times(h1[:, 1, :BANK], 5, pooled[0], 0, BANK)
+        pack_pair(nc.scalar.copy, 0, 0, BANK)
+        gate_times(h1[:, 1, BANK:S], 5, pooled[1], BANK, BANK)
+        quantize_weight("wo", 0, 0, 0, SLOTS, "low")
+        pack_pair(nc.scalar.copy, 0, BANK, BANK)
+        gate_times(h1[:, 2, :LEAD], 6, product[6][:, :LEAD], 0, LEAD)
+        quantize_weight("wo", 1, 0, 0, SLOTS, "high")
 
-        groups = []
-        for i, n in enumerate(CHUNKS):
-            width = TILES_PER_BANK if i == last else BANK // n
-            groups.append([tuple(range(c0, c0 + width)) for c0 in range(0, OUT_TILES, width)])
-        sums = {}
-        for i, (j0, n) in enumerate(zip(starts, CHUNKS)):
-            for tiles in groups[i][: 1 if i == last else None]:
-                sums[i, tiles] = open_sums(tiles, j0, n)
+        result = keep.tile([P, OUT_TILES, S], F32, name="h0", align_bytes=64)
+        starts = [sum(CHUNKS[:i]) for i in range(len(CHUNKS))]
+        sums = [open_sums(starts[i], CHUNKS[i]) for i in range(OPEN_AHEAD)]
 
-        def finish(i, parts):
-            for part in parts:
-                quantize_h(1, *part)
-            for tiles in groups[i]:
-                close_sums(sums[i, tiles], tiles, starts[i], CHUNKS[i])
-            if i == 0:
-                tiles = groups[last][1]
-                sums[last, tiles] = open_sums(tiles, starts[last], CHUNKS[last])
+        def gather(u, i):
+            cols = slice(starts[i], starts[i] + CHUNKS[i])
+            gate_times(h1[:, u - SLOTS, cols], u, product[u][:, cols], starts[i], CHUNKS[i])
 
-        waiting = None
-        for i, (j0, n) in enumerate(zip(starts, CHUNKS)):
-            if j0 >= LEAD:
-                gate_times(h1_rows[:, 2, j0 : j0 + n], 6, product[6][:, j0 : j0 + n], j0, n)
-            gate_times(h1_rows[:, 3, j0 : j0 + n], 7, product[7][:, j0 : j0 + n], j0, n)
-            if waiting:
-                finish(i - 1, waiting)
-            waiting = [(packed1[:, SLOTS * j0 : SLOTS * (j0 + n)], j0, n)]
-            copy = nc.scalar.copy if i < SCALAR_CHUNKS else nc.vector.tensor_copy
-            for packed, c0, m in waiting:
-                interleave(copy, packed, h1_rows[:, :, c0 : c0 + m])
-        finish(last, waiting)
+        def pack(i):
+            pack_pair(nc.vector.tensor_copy, HALF, starts[i], CHUNKS[i])
+
+        def finish(i):
+            quantize_h(1, packed1, starts[i], CHUNKS[i])
+            close_sums(sums[i], starts[i], CHUNKS[i])
+            if i + OPEN_AHEAD < len(CHUNKS):
+                sums.append(open_sums(starts[i + OPEN_AHEAD], CHUNKS[i + OPEN_AHEAD]))
+
+        gather(7, 0)
+        gather(7, 1)
+        pack(0)
+        gather(6, 3)
+        finish(0)
+        pack(1)
+        gather(7, 2)
+        finish(1)
+        pack(2)
+        gather(7, 3)
+        finish(2)
+        pack(3)
+        gather(6, 4)
+        finish(3)
+        gather(7, 4)
+        gather(6, 5)
+        pack(4)
+        gather(7, 5)
+        finish(4)
+        pack(5)
+        finish(5)

@@ -28,18 +28,19 @@ RUN = 4
 PASSES = 2
 TILES = PASSES * SLOTS
 OUT_TILES = N // P
-TILES_PER_BANK = 2
-CHUNKS = (128, 128, 256, 256, 128, 128)
+TILES_PER_BANK = 1
+CHUNKS = (256, 256, 256, 128, 128)
 PIECE = 256
-LEAD = 512
-AHEAD = 256
+LEAD = 256
+AHEAD = 512
 ROW = S + LEAD
 USER_ROW = 8
 GATE_BUFS, PSUM_BUFS = 4, 8
 HALF = SLOTS // 2
-OPEN_AHEAD = PSUM_BUFS // OUT_TILES
+OPEN_AHEAD = PSUM_BUFS * TILES_PER_BANK // OUT_TILES
 TILES_PER_STORE = 2
 OFFSETS = {"low": 0, "rounded2": 1024, "high": 2048}
+SCALAR_CHUNKS = (0, 1)
 
 
 def tile_list_gated_preference_features_kernel(
@@ -200,16 +201,19 @@ def tile_list_gated_preference_features_kernel(
             )
 
         def open_sums(j0, n):
-            banks = [psum.tile([P, n], F32, name="bank") for c in range(OUT_TILES)]
-            for c, acc in enumerate(banks):
-                y_pass(acc[:], c, 0, j0, n, True, False)
+            banks = [psum.tile([P, TILES_PER_BANK, n], F32, name="bank") for c in range(OUT_TILES // TILES_PER_BANK)]
+            for c in range(OUT_TILES):
+                k, e = divmod(c, TILES_PER_BANK)
+                y_pass(banks[k][:, e, :], c, 0, j0, n, e == 0, False)
             return banks
 
         def close_sums(banks, j0, n):
-            for c, acc in enumerate(banks):
-                y_pass(acc[:], c, 1, j0, n, False, True)
-            for c, acc in enumerate(banks):
-                nc.scalar.activation(result[:, c, j0 : j0 + n], acc[:], TANH, bias=bias[:, c : c + 1])
+            for c in range(OUT_TILES):
+                k, e = divmod(c, TILES_PER_BANK)
+                y_pass(banks[k][:, e, :], c, 1, j0, n, False, e == TILES_PER_BANK - 1)
+            for c in range(OUT_TILES):
+                k, e = divmod(c, TILES_PER_BANK)
+                nc.scalar.activation(result[:, c, j0 : j0 + n], banks[k][:, e, :], TANH, bias=bias[:, c : c + 1])
                 if (c + 1) % TILES_PER_STORE == 0:
                     stored = slice(c + 1 - TILES_PER_STORE, c + 1)
                     nc.sync.dma_start(out_rows[:, stored, j0 : j0 + n], result[:, stored, j0 : j0 + n])
@@ -256,12 +260,6 @@ def tile_list_gated_preference_features_kernel(
         load_gate(3)
         load_wo(0, place("big4", SLOTS * N, F32)[:])
 
-        def pack_pair(copy, t0, j0, n):
-            copy(
-                packed1[:, SLOTS * j0 : SLOTS * (j0 + n)].rearrange("p (c t) -> p c t", t=SLOTS)[:, :, t0 : t0 + HALF],
-                h1[:, t0 : t0 + HALF, j0 : j0 + n].rearrange("p t c -> p c t"),
-            )
-
         b, product = {}, {}
         for u in range(3):
             b[u] = place(f"b{u}", S, F32)[:]
@@ -300,8 +298,6 @@ def tile_list_gated_preference_features_kernel(
         load_wo(1, stage[:, 3 * ROW + AHEAD :])
         quantize_weight("wa", 1, 0, 0, SLOTS)
         gate_times(h0[:, 2, :], 2, product[2], 0, S)
-        with nc.allow_non_contiguous_dma(reason="one bias value for each partition and output tile"):
-            nc.sync.dma_start(bias[:], bo.rearrange("(c p) -> p c", p=P))
         load_gate(6)
         round_wa(nc.scalar.copy, 1, 1, 0, HALF, "rounded1")
         round_wa(nc.scalar.copy, 1, 1, HALF, HALF, "rounded2")
@@ -309,6 +305,8 @@ def tile_list_gated_preference_features_kernel(
         for e in range(2):
             gate_times(halves(h0[:, 3, :])[e], 3, pooled[e], e * BANK, BANK)
         load_gate(7)
+        with nc.allow_non_contiguous_dma(reason="one bias value for each partition and output tile"):
+            nc.sync.dma_start(bias[:], bo.rearrange("(c p) -> p c", p=P))
         quantize_weight("wa", 1, 1, HALF, HALF, "pooled0")
         product[4] = place("product0", S, F32)[:]
         product[6] = place("product2", S, F32)[:]
@@ -326,10 +324,8 @@ def tile_list_gated_preference_features_kernel(
         for j0 in range(0, S, BANK):
             quantize_h(0, packed0, j0, BANK)
         gate_times(h1[:, 1, :BANK], 5, pooled[0], 0, BANK)
-        pack_pair(nc.scalar.copy, 0, 0, BANK)
         gate_times(h1[:, 1, BANK:S], 5, pooled[1], BANK, BANK)
         quantize_weight("wo", 0, 0, 0, SLOTS, "low")
-        pack_pair(nc.scalar.copy, 0, BANK, BANK)
         gate_times(h1[:, 2, :LEAD], 6, product[6][:, :LEAD], 0, LEAD)
         quantize_weight("wo", 1, 0, 0, SLOTS, "high")
 
@@ -342,7 +338,8 @@ def tile_list_gated_preference_features_kernel(
             gate_times(h1[:, u - SLOTS, cols], u, product[u][:, cols], starts[i], CHUNKS[i])
 
         def pack(i):
-            pack_pair(nc.vector.tensor_copy, HALF, starts[i], CHUNKS[i])
+            copy = nc.scalar.copy if i in SCALAR_CHUNKS else nc.vector.tensor_copy
+            interleave(copy, packed1, h1, starts[i], CHUNKS[i])
 
         def finish(i):
             quantize_h(1, packed1, starts[i], CHUNKS[i])
@@ -351,23 +348,21 @@ def tile_list_gated_preference_features_kernel(
                 sums.append(open_sums(starts[i + OPEN_AHEAD], CHUNKS[i + OPEN_AHEAD]))
 
         gather(7, 0)
-        gather(7, 1)
         pack(0)
-        gather(6, 3)
-        finish(0)
+        gather(6, 1)
+        gather(7, 1)
         pack(1)
+        finish(0)
+        gather(6, 2)
         gather(7, 2)
         finish(1)
         pack(2)
-        gather(7, 3)
+        gather(6, 3)
         finish(2)
-        pack(3)
+        gather(7, 3)
         gather(6, 4)
-        finish(3)
+        pack(3)
         gather(7, 4)
-        gather(6, 5)
+        finish(3)
         pack(4)
-        gather(7, 5)
         finish(4)
-        pack(5)
-        finish(5)

@@ -28,19 +28,14 @@ RUN = 4
 PASSES = 2
 TILES = PASSES * SLOTS
 OUT_TILES = N // P
-TILES_PER_BANK = 1
-CHUNKS = (256, 256, 256, 128, 128)
 PIECE = 256
-LEAD = 256
-AHEAD = 512
+LEAD = 512
 ROW = S + LEAD
 USER_ROW = 8
 GATE_BUFS, PSUM_BUFS = 4, 8
 HALF = SLOTS // 2
-OPEN_AHEAD = PSUM_BUFS * TILES_PER_BANK // OUT_TILES
-TILES_PER_STORE = 2
 OFFSETS = {"low": 0, "rounded2": 1024, "high": 2048}
-SCALAR_CHUNKS = (0, 1)
+PACK_AT = {0: 512, 128: 1280, 256: 768, 512: 2048, 768: 2560, 896: 2816}
 
 
 def tile_list_gated_preference_features_kernel(
@@ -79,7 +74,7 @@ def tile_list_gated_preference_features_kernel(
         h_scales = [place(f"h_scales{s}", S, U8) for s in range(PASSES)]
         out_rows = out.rearrange("(c p) j -> p c j", p=P)
 
-        gate, raw, rounded, codes, scales = {}, {}, {}, {}, {}
+        gate, raw, rounded, codes, scales, sums = {}, {}, {}, {}, {}, {}
 
         def words(ap):
             return ap.rearrange("p t i -> p (t i)").bitcast(I32)
@@ -178,7 +173,7 @@ def tile_list_gated_preference_features_kernel(
 
         def interleave(copy, packed, rows, j0, n):
             copy(
-                packed[:, SLOTS * j0 : SLOTS * (j0 + n)].rearrange("p (c i t) -> p c t i", i=RUN, t=SLOTS),
+                packed.rearrange("p (c i t) -> p c t i", i=RUN, t=SLOTS),
                 rows[:, :, j0 : j0 + n].rearrange("p t (c i) -> p c t i", i=RUN),
             )
 
@@ -186,7 +181,7 @@ def tile_list_gated_preference_features_kernel(
             nc.vector.quantize_mx(
                 h_codes[s][:, j0 : j0 + n].bitcast(FP8X4),
                 h_scales[s][:, j0 : j0 + n],
-                packed[:, SLOTS * j0 : SLOTS * (j0 + n)],
+                packed,
             )
 
         def y_pass(acc, c, s, j0, n, start, stop):
@@ -200,23 +195,23 @@ def tile_list_gated_preference_features_kernel(
                 stop=stop,
             )
 
-        def open_sums(j0, n):
-            banks = [psum.tile([P, TILES_PER_BANK, n], F32, name="bank") for c in range(OUT_TILES // TILES_PER_BANK)]
-            for c in range(OUT_TILES):
-                k, e = divmod(c, TILES_PER_BANK)
-                y_pass(banks[k][:, e, :], c, 0, j0, n, e == 0, False)
-            return banks
+        def open_sums(j0, n, together):
+            banks = []
+            for c0 in range(0, OUT_TILES, together):
+                acc = psum.tile([P, together, n], F32, name="bank")
+                for e in range(together):
+                    y_pass(acc[:, e, :], c0 + e, 0, j0, n, e == 0, False)
+                    banks.append((acc[:, e, :], e == together - 1))
+            sums[j0] = banks
 
-        def close_sums(banks, j0, n):
-            for c in range(OUT_TILES):
-                k, e = divmod(c, TILES_PER_BANK)
-                y_pass(banks[k][:, e, :], c, 1, j0, n, False, e == TILES_PER_BANK - 1)
-            for c in range(OUT_TILES):
-                k, e = divmod(c, TILES_PER_BANK)
-                nc.scalar.activation(result[:, c, j0 : j0 + n], banks[k][:, e, :], TANH, bias=bias[:, c : c + 1])
-                if (c + 1) % TILES_PER_STORE == 0:
-                    stored = slice(c + 1 - TILES_PER_STORE, c + 1)
-                    nc.sync.dma_start(out_rows[:, stored, j0 : j0 + n], result[:, stored, j0 : j0 + n])
+        def close_sums(j0, n, store_from, together=HALF):
+            for c, (acc, last) in enumerate(sums[j0]):
+                y_pass(acc, c, 1, j0, n, False, last)
+            for c, (acc, last) in enumerate(sums[j0]):
+                nc.scalar.activation(result[:, c, j0 : j0 + n], acc, TANH, bias=bias[:, c : c + 1])
+                if store_from is not None and (c + 1) % together == 0:
+                    where = (slice(None), slice(c + 1 - together, c + 1), slice(store_from, j0 + n))
+                    nc.sync.dma_start(out_rows[where], result[where])
 
         nc.gpsimd.memset(item_scale_tab[:], 0)
         nc.vector.memset(wb_scale_raw[:], 0)
@@ -278,9 +273,8 @@ def tile_list_gated_preference_features_kernel(
         gate_times(product[0], 0, b[0], 0, S)
         load_gate(4)
         h0 = keep.tile([P, SLOTS, S], F32, name="h0", align_bytes=64)
-        stage = place("stage", 3 * ROW + AHEAD + 2 * S, F32)
+        stage = place("stage", 3 * ROW + 3 * S, F32)
         h1 = stage[:, : SLOTS * ROW].rearrange("p (t c) -> p t c", t=SLOTS)
-        packed1 = stage[:, 3 * ROW + AHEAD :].bitcast(BF16)
         for u in (1, 2):
             product[u] = place(f"product{u}", S, F32)[:]
         pooled = [place(f"pooled{e}", BANK, F32)[:] for e in range(2)]
@@ -295,7 +289,7 @@ def tile_list_gated_preference_features_kernel(
             make_b(u, b[u])
         gate_times(h0[:, 1, :], 1, product[1], 0, S)
         load_gate(5)
-        load_wo(1, stage[:, 3 * ROW + AHEAD :])
+        load_wo(1, stage[:, 3 * ROW + S :])
         quantize_weight("wa", 1, 0, 0, SLOTS)
         gate_times(h0[:, 2, :], 2, product[2], 0, S)
         load_gate(6)
@@ -310,19 +304,24 @@ def tile_list_gated_preference_features_kernel(
         quantize_weight("wa", 1, 1, HALF, HALF, "pooled0")
         product[4] = place("product0", S, F32)[:]
         product[6] = place("product2", S, F32)[:]
-        product[7] = h1[:, 2, LEAD:]
+        early = h1[:, 2, S + PIECE :]
+        late = h1[:, 2, LEAD : S + PIECE]
         pooled = [place(name, BANK, F32)[:] for name in ("low", "high")]
         pool_a_b(5, b[5], pooled)
         packed0 = place("big2", SLOTS * S, BF16)
         for j0 in range(0, S, PIECE):
-            interleave(nc.scalar.copy, packed0, h0, j0, PIECE)
-        for u in (4, 6, 7):
+            interleave(nc.scalar.copy, packed0[:, SLOTS * j0 : SLOTS * (j0 + PIECE)], h0, j0, PIECE)
+        for u in (4, 6):
             times_a(u, b[u], halves(product[u]))
+        acc = make_a(7, 0)
+        nc.vector.tensor_tensor(early, acc[:, :PIECE], b[7][:, :PIECE], MULT)
+        nc.vector.tensor_tensor(late[:, :PIECE], acc[:, PIECE:], b[7][:, PIECE:BANK], MULT)
+        nc.vector.tensor_tensor(late[:, PIECE:], make_a(7, 1)[:], b[7][:, BANK:], MULT)
         round_wo(0, "rounded0")
         round_wo(1, "rounded1")
         gate_times(h1[:, 0, :S], 4, product[4], 0, S)
         for j0 in range(0, S, BANK):
-            quantize_h(0, packed0, j0, BANK)
+            quantize_h(0, packed0[:, SLOTS * j0 : SLOTS * (j0 + BANK)], j0, BANK)
         gate_times(h1[:, 1, :BANK], 5, pooled[0], 0, BANK)
         gate_times(h1[:, 1, BANK:S], 5, pooled[1], BANK, BANK)
         quantize_weight("wo", 0, 0, 0, SLOTS, "low")
@@ -330,39 +329,59 @@ def tile_list_gated_preference_features_kernel(
         quantize_weight("wo", 1, 0, 0, SLOTS, "high")
 
         result = keep.tile([P, OUT_TILES, S], F32, name="h0", align_bytes=64)
-        starts = [sum(CHUNKS[:i]) for i in range(len(CHUNKS))]
-        sums = [open_sums(starts[i], CHUNKS[i]) for i in range(OPEN_AHEAD)]
 
-        def gather(u, i):
-            cols = slice(starts[i], starts[i] + CHUNKS[i])
-            gate_times(h1[:, u - SLOTS, cols], u, product[u][:, cols], starts[i], CHUNKS[i])
+        def packed(j0, n):
+            return stage[:, 3 * ROW + PACK_AT[j0] : 3 * ROW + PACK_AT[j0] + 2 * n].bitcast(BF16)
 
-        def pack(i):
-            copy = nc.scalar.copy if i in SCALAR_CHUNKS else nc.vector.tensor_copy
-            interleave(copy, packed1, h1, starts[i], CHUNKS[i])
+        def gather(u, j0, n):
+            if u == 6:
+                factor = product[6][:, j0 : j0 + n]
+            else:
+                factor = early[:, j0 : j0 + n] if j0 < PIECE else late[:, j0 - PIECE : j0 - PIECE + n]
+            gate_times(h1[:, u - SLOTS, j0 : j0 + n], u, factor, j0, n)
 
-        def finish(i):
-            quantize_h(1, packed1, starts[i], CHUNKS[i])
-            close_sums(sums[i], starts[i], CHUNKS[i])
-            if i + OPEN_AHEAD < len(CHUNKS):
-                sums.append(open_sums(starts[i + OPEN_AHEAD], CHUNKS[i + OPEN_AHEAD]))
+        def pack(copy, j0, n):
+            interleave(copy, packed(j0, n), h1, j0, n)
 
-        gather(7, 0)
-        pack(0)
-        gather(6, 1)
-        gather(7, 1)
-        pack(1)
-        finish(0)
-        gather(6, 2)
-        gather(7, 2)
-        finish(1)
-        pack(2)
-        gather(6, 3)
-        finish(2)
-        gather(7, 3)
-        gather(6, 4)
-        pack(3)
-        gather(7, 4)
-        finish(3)
-        pack(4)
-        finish(4)
+        def pack_pair(copy, t0, j0, n):
+            copy(
+                packed(j0, n).rearrange("p (c t) -> p c t", t=SLOTS)[:, :, t0 : t0 + HALF],
+                h1[:, t0 : t0 + HALF, j0 : j0 + n].rearrange("p t c -> p c t"),
+            )
+
+        def quant(j0, n):
+            quantize_h(1, packed(j0, n), j0, n)
+
+        on_scalar, on_vector = nc.scalar.copy, nc.vector.tensor_copy
+        for j0, n in ((0, 128), (128, 128), (256, 256), (512, 256), (768, 128), (896, 128)):
+            open_sums(j0, n, BANK // n)
+        pack_pair(on_scalar, 0, 256, 256)
+        pack_pair(on_scalar, 0, 512, 512)
+        gather(7, 0, 128)
+        gather(7, 128, 128)
+        pack(on_scalar, 128, 128)
+        gather(7, 256, 128)
+        pack(on_vector, 0, 128)
+        gather(7, 384, 128)
+        pack_pair(on_scalar, HALF, 256, 256)
+        quant(0, 128)
+        close_sums(0, 128, 0)
+        gather(6, 512, 256)
+        quant(128, 128)
+        close_sums(128, 128, 128)
+        gather(7, 512, 256)
+        quant(256, 256)
+        close_sums(256, 256, 256)
+        pack_pair(on_vector, HALF, 512, 256)
+        gather(6, 768, 128)
+        quant(512, 256)
+        close_sums(512, 256, 512)
+        gather(7, 768, 128)
+        gather(6, 896, 128)
+        pack_pair(on_vector, HALF, 768, 128)
+        gather(7, 896, 128)
+        quant(768, 128)
+        close_sums(768, 128, None)
+        pack_pair(on_vector, HALF, 896, 128)
+        quant(896, 128)
+        close_sums(896, 128, 768)

@@ -145,10 +145,10 @@ def tile_list_gated_preference_features_kernel(
             picked = gate[u][:].indirect(users[:, j0 // GROUP : (j0 + n) // GROUP])
             nc.vector.tensor_tensor(dest, picked, factor, MULT)
 
-        def make_a(u, bank):
+        def make_a(u, j0, n=BANK):
             s, t = divmod(u, SLOTS)
-            pairs = slice(bank * BANK, (bank + 1) * BANK)
-            acc = psum.tile([P, BANK], F32, name="bank")
+            pairs = slice(j0, j0 + n)
+            acc = psum.tile([P, n], F32, name="bank")
             for ks in range(PASSES):
                 nc.tensor.matmul_mx(
                     acc[:],
@@ -163,13 +163,17 @@ def tile_list_gated_preference_features_kernel(
 
         def times_a(u, factor, dest):
             for bank in range(S // BANK):
-                nc.vector.tensor_tensor(dest[bank], make_a(u, bank)[:], halves(factor)[bank], MULT)
+                nc.vector.tensor_tensor(dest[bank], make_a(u, bank * BANK)[:], halves(factor)[bank], MULT)
 
-        def pool_a_b(u, factor, dest):
-            for bank in range(S // BANK):
-                a_copy = place(f"a_copy{bank}", BANK, F32)
-                nc.scalar.copy(a_copy[:], make_a(u, bank)[:])
-                nc.gpsimd.tensor_tensor(dest[bank], a_copy[:], halves(factor)[bank], MULT)
+        def pool_a_b(u, j0, parts):
+            n = sum(part.shape[1] for part in parts)
+            a_copy = place(f"a_copy{j0 // BANK}", n, F32)
+            nc.scalar.copy(a_copy[:], make_a(u, j0, n)[:])
+            done = 0
+            for part in parts:
+                width = part.shape[1]
+                nc.gpsimd.tensor_tensor(part, a_copy[:, done : done + width], b[u][:, j0 + done : j0 + done + width], MULT)
+                done = done + width
 
         def interleave(copy, packed, rows, j0, n):
             copy(
@@ -204,13 +208,14 @@ def tile_list_gated_preference_features_kernel(
                     banks.append((acc[:, e, :], e == together - 1))
             sums[j0] = banks
 
-        def close_sums(j0, n, store_from, together=HALF):
+        def close_sums(j0, n, stores):
             for c, (acc, last) in enumerate(sums[j0]):
                 y_pass(acc, c, 1, j0, n, False, last)
             for c, (acc, last) in enumerate(sums[j0]):
                 nc.scalar.activation(result[:, c, j0 : j0 + n], acc, TANH, bias=bias[:, c : c + 1])
-                if store_from is not None and (c + 1) % together == 0:
-                    where = (slice(None), slice(c + 1 - together, c + 1), slice(store_from, j0 + n))
+                if c in stores:
+                    first_tile, first_pair = stores[c]
+                    where = (slice(None), slice(first_tile, c + 1), slice(first_pair, j0 + n))
                     nc.sync.dma_start(out_rows[where], result[where])
 
         nc.gpsimd.memset(item_scale_tab[:], 0)
@@ -277,8 +282,9 @@ def tile_list_gated_preference_features_kernel(
         h1 = stage[:, : SLOTS * ROW].rearrange("p (t c) -> p t c", t=SLOTS)
         for u in (1, 2):
             product[u] = place(f"product{u}", S, F32)[:]
-        pooled = [place(f"pooled{e}", BANK, F32)[:] for e in range(2)]
-        pool_a_b(3, b[3], pooled)
+        pooled = [place(f"pooled{e}", n, F32)[:] for e, n in enumerate((PIECE, PIECE, BANK))]
+        pool_a_b(3, 0, pooled[:2])
+        pool_a_b(3, BANK, pooled[2:])
         times_a(1, b[1], halves(product[1]))
         times_a(2, b[2], halves(product[2]))
         times_a(0, product[0], halves(h0[:, 0, :]))
@@ -297,26 +303,32 @@ def tile_list_gated_preference_features_kernel(
         round_wa(nc.scalar.copy, 1, 1, HALF, HALF, "rounded2")
         quantize_weight("wa", 1, 1, 0, HALF)
         for e in range(2):
-            gate_times(halves(h0[:, 3, :])[e], 3, pooled[e], e * BANK, BANK)
+            gate_times(h0[:, 3, e * PIECE : (e + 1) * PIECE], 3, pooled[e], e * PIECE, PIECE)
+        quantize_weight("wa", 1, 1, HALF, HALF, "pooled0")
+        gate_times(h0[:, 3, BANK:], 3, pooled[2], BANK, BANK)
         load_gate(7)
         with nc.allow_non_contiguous_dma(reason="one bias value for each partition and output tile"):
             nc.sync.dma_start(bias[:], bo.rearrange("(c p) -> p c", p=P))
-        quantize_weight("wa", 1, 1, HALF, HALF, "pooled0")
         product[4] = place("product0", S, F32)[:]
         product[6] = place("product2", S, F32)[:]
         early = h1[:, 2, S + PIECE :]
         late = h1[:, 2, LEAD : S + PIECE]
         pooled = [place(name, BANK, F32)[:] for name in ("low", "high")]
-        pool_a_b(5, b[5], pooled)
+        for e in range(2):
+            pool_a_b(5, e * BANK, [pooled[e]])
+        a_copy = place("a_copy0", PIECE, F32)
+        nc.scalar.copy(a_copy[:], make_a(4, S - PIECE, PIECE)[:])
+        nc.gpsimd.tensor_tensor(product[4][:, S - PIECE :], a_copy[:], b[4][:, S - PIECE :], MULT)
         packed0 = place("big2", SLOTS * S, BF16)
         for j0 in range(0, S, PIECE):
             interleave(nc.scalar.copy, packed0[:, SLOTS * j0 : SLOTS * (j0 + PIECE)], h0, j0, PIECE)
-        for u in (4, 6):
-            times_a(u, b[u], halves(product[u]))
+        for j0, n in ((0, BANK), (BANK, PIECE)):
+            nc.vector.tensor_tensor(product[4][:, j0 : j0 + n], make_a(4, j0, n)[:], b[4][:, j0 : j0 + n], MULT)
+        times_a(6, b[6], halves(product[6]))
         acc = make_a(7, 0)
         nc.vector.tensor_tensor(early, acc[:, :PIECE], b[7][:, :PIECE], MULT)
         nc.vector.tensor_tensor(late[:, :PIECE], acc[:, PIECE:], b[7][:, PIECE:BANK], MULT)
-        nc.vector.tensor_tensor(late[:, PIECE:], make_a(7, 1)[:], b[7][:, BANK:], MULT)
+        nc.vector.tensor_tensor(late[:, PIECE:], make_a(7, BANK)[:], b[7][:, BANK:], MULT)
         round_wo(0, "rounded0")
         round_wo(1, "rounded1")
         gate_times(h1[:, 0, :S], 4, product[4], 0, S)
@@ -365,23 +377,23 @@ def tile_list_gated_preference_features_kernel(
         gather(7, 384, 128)
         pack_pair(on_scalar, HALF, 256, 256)
         quant(0, 128)
-        close_sums(0, 128, 0)
+        close_sums(0, 128, {1: (0, 0), 3: (2, 0)})
         gather(6, 512, 256)
         quant(128, 128)
-        close_sums(128, 128, 128)
+        close_sums(128, 128, {1: (0, 128), 3: (2, 128)})
         gather(7, 512, 256)
         quant(256, 256)
-        close_sums(256, 256, 256)
+        close_sums(256, 256, {1: (0, 256), 3: (2, 256)})
         pack_pair(on_vector, HALF, 512, 256)
         gather(6, 768, 128)
         quant(512, 256)
-        close_sums(512, 256, 512)
+        close_sums(512, 256, {1: (0, 512), 3: (2, 512)})
         gather(7, 768, 128)
         gather(6, 896, 128)
         pack_pair(on_vector, HALF, 768, 128)
         gather(7, 896, 128)
         quant(768, 128)
-        close_sums(768, 128, None)
+        close_sums(768, 128, {})
         pack_pair(on_vector, HALF, 896, 128)
         quant(896, 128)
-        close_sums(896, 128, 768)
+        close_sums(896, 128, {c: (c, 768) for c in range(OUT_TILES)})

from contextlib import ExitStack

import concourse.mybir as mybir

K, I, H, N, T, S = 1024, 512, 1024, 512, 2048, 1024
FLOPS = 2 * S * (K * H + I * H + H * N)

F32 = mybir.dt.float32
BF16 = mybir.dt.bfloat16
I32 = mybir.dt.int32
U32 = mybir.dt.uint32
U16 = mybir.dt.uint16
U8 = mybir.dt.uint8
FP8X4 = mybir.dt.float8_e4m3fn_x4
FP4X4 = mybir.dt.float4_e2m1fn_x4
MULT = mybir.AluOpType.mult
TANH = mybir.ActivationFunctionType.Tanh

P = 128
SLOTS = 4
PASS = P * SLOTS
BANK = 512
GROUP = 16
QUADS = 4
QUAD = P // QUADS
SCALE_ROWS = 4
RUN = 4
PASSES = 2
TILES = PASSES * SLOTS
OUT_TILES = N // P
PIECE = 256
LEAD = 512
ROW = S + LEAD
USER_ROW = 8
GATE_BUFS, PSUM_BUFS = 4, 8
HALF = SLOTS // 2
OFFSETS = {"low": 0, "rounded2": 1024, "high": 2048}
PACK_AT = {0: 512, 128: 1280, 256: 768, 512: 2048, 768: 2560, 896: 2816}


def tile_list_gated_preference_features_kernel(
    tc, tab_words, tab_scales, tab2_words, tab2_scales, offs, offs2, gT, wa, wb_words, wb_scales, wo, bo, out
):
    nc = tc.nc
    with ExitStack() as ctx:
        keep = ctx.enter_context(tc.tile_pool(name="keep", bufs=1))
        ring = ctx.enter_context(tc.tile_pool(name="ring", bufs=GATE_BUFS))
        psum = ctx.enter_context(tc.psum_pool(name="psum", bufs=PSUM_BUFS))

        spots = ctx.enter_context(tc.tile_pool(name="spots", bufs=1))

        def place(name, columns, dtype):
            if name in OFFSETS:
                return spots.tile([P, columns], dtype, name=name, align_bytes=64, offset=OFFSETS[name])
            return keep.tile([P, columns], dtype, name=name, align_bytes=64)

        users = keep.tile([P, S // GROUP], U16, name="users")
        items = keep.tile([P, S // GROUP], U16, name="items")
        item_scale_tab = place("item_scale_tab", T // 4, I32)
        user_scale_tab = place("user_scale_tab", T // 4, I32)
        wb_scale_raw = place("wb_scale_raw", H // 4, I32)
        wb_code_raw = place("wb_code_raw", H // 2, I32)
        item_code_tab = place("big0", T, I32)
        user_code_tab = [place(f"big{1 + s}", T, I32) for s in range(PASSES)]
        bias = keep.tile([P, OUT_TILES], F32, name="bias")

        item_codes = place("item_codes", S, U32)
        item_scales = place("item_scales", S, U8)
        user_codes = [place(f"user_codes{s}", S, U32) for s in range(PASSES)]
        user_scales = place("user_scales", S, U8)
        wb_codes = place("wb_codes", 2 * H, U8)
        wb_scale = place("wb_scale", H, U8)
        h_codes = [place(f"h_codes{s}", S, U32) for s in range(PASSES)]
        h_scales = [place(f"h_scales{s}", S, U8) for s in range(PASSES)]
        out_rows = out.rearrange("(c p) j -> p c j", p=P)

        gate, raw, rounded, codes, scales, sums = {}, {}, {}, {}, {}, {}

        def words(ap):
            return ap.rearrange("p t i -> p (t i)").bitcast(I32)

        def load_scale_row(tile, source, first, r):
            rows = source.rearrange("(q r) c -> r q c", r=SCALE_ROWS)[r]
            nc.sync.dma_start(tile[first + r : P : QUAD, :], rows.bitcast(I32))

        def factor_rows(ap, s):
            return ap[s * PASS : (s + 1) * PASS, :].rearrange("(g t i) c -> t g i c", t=SLOTS, i=RUN)

        def load_gate(u):
            s, t = divmod(u, SLOTS)
            gate[u] = ring.tile([P, T], F32, name="gate")
            nc.sync.dma_start(gate[u][:], factor_rows(gT, s)[t])

        def load_wa(s, ks, name):
            raw["wa", s, ks] = place(name, SLOTS * PASS, F32)
            rows = wa[ks * PASS : (ks + 1) * PASS, s * PASS : (s + 1) * PASS]
            nc.sync.dma_start(
                raw["wa", s, ks][:].rearrange("p (j c) -> p j c", j=SLOTS), rows.rearrange("(p j) c -> p j c", j=SLOTS)
            )

        def load_wo(s, dest):
            raw["wo", s, 0] = dest
            for t in range(SLOTS):
                nc.sync.dma_start(dest[:, N * t : N * (t + 1)], factor_rows(wo, s)[t])

        def round_wa(copy, s, ks, t0, tiles, name):
            rounded["wa", s, ks, t0] = place(name, tiles * PASS, BF16)
            dest = rounded["wa", s, ks, t0][:].rearrange("p (t g i j) -> p g t j i", t=tiles, i=RUN, j=SLOTS)
            source = raw["wa", s, ks][:].rearrange("p (j g t i) -> p g t j i", j=SLOTS, t=SLOTS, i=RUN)
            copy(dest, source[:, :, t0 : t0 + tiles])

        def round_wo(s, name):
            rounded["wo", s, 0, 0] = place(name, SLOTS * N, BF16)
            nc.scalar.copy(
                rounded["wo", s, 0, 0][:].rearrange("p (c i t) -> p c t i", i=RUN, t=SLOTS),
                raw["wo", s, 0].rearrange("p (t c i) -> p c t i", t=SLOTS, i=RUN),
            )

        def quantize_weight(name, s, part, t0, tiles, spot=None):
            made = place(spot or f"codes_{name}{s}{part}{t0}", P * tiles, U32)
            scale = place(f"scales_{name}{s}{part}{t0}", P * tiles, U8)
            nc.vector.quantize_mx(made[:].bitcast(FP8X4), scale[:], rounded[name, s, part, t0][:])
            for e in range(tiles):
                codes[name, s, part, t0 + e] = made[:, P * e : P * (e + 1)].bitcast(FP8X4)
                scales[name, s, part, t0 + e] = scale[:, P * e : P * (e + 1)]

        def halves(ap):
            return [ap[:, :BANK], ap[:, BANK:]]

        def make_b(u, dest):
            for j0 in range(0, S, BANK):
                acc = psum.tile([P, BANK], F32, name="bank")
                nc.tensor.matmul_mx(
                    acc[:],
                    lhsT=wb_codes[:, 2 * P * u : 2 * P * (u + 1)].bitcast(FP4X4),
                    lhsT_scale=wb_scale[:, P * u : P * (u + 1)],
                    rhs=item_codes[:, j0 : j0 + BANK].bitcast(FP8X4),
                    rhs_scale=item_scales[:, j0 : j0 + BANK],
                    start=True,
                    stop=True,
                )
                nc.scalar.copy(dest[:, j0 : j0 + BANK], acc[:])

        def gate_times(dest, u, factor, j0, n):
            picked = gate[u][:].indirect(users[:, j0 // GROUP : (j0 + n) // GROUP])
            nc.vector.tensor_tensor(dest, picked, factor, MULT)

        def make_a(u, j0, n=BANK):
            s, t = divmod(u, SLOTS)
            pairs = slice(j0, j0 + n)
            acc = psum.tile([P, n], F32, name="bank")
            for ks in range(PASSES):
                nc.tensor.matmul_mx(
                    acc[:],
                    lhsT=codes["wa", s, ks, t],
                    lhsT_scale=scales["wa", s, ks, t],
                    rhs=user_codes[ks][:, pairs].bitcast(FP8X4),
                    rhs_scale=user_scales[USER_ROW + SCALE_ROWS * ks : P, pairs],
                    start=(ks == 0),
                    stop=(ks == PASSES - 1),
                )
            return acc

        def times_a(u, factor, dest):
            for bank in range(S // BANK):
                nc.vector.tensor_tensor(dest[bank], make_a(u, bank * BANK)[:], halves(factor)[bank], MULT)

        def pool_a_b(u, j0, parts):
            n = sum(part.shape[1] for part in parts)
            a_copy = place(f"a_copy{j0 // BANK}", n, F32)
            nc.scalar.copy(a_copy[:], make_a(u, j0, n)[:])
            done = 0
            for part in parts:
                width = part.shape[1]
                nc.gpsimd.tensor_tensor(part, a_copy[:, done : done + width], b[u][:, j0 + done : j0 + done + width], MULT)
                done = done + width

        def interleave(copy, packed, rows, j0, n):
            copy(
                packed.rearrange("p (c i t) -> p c t i", i=RUN, t=SLOTS),
                rows[:, :, j0 : j0 + n].rearrange("p t (c i) -> p c t i", i=RUN),
            )

        def quantize_h(s, packed, j0, n):
            nc.vector.quantize_mx(
                h_codes[s][:, j0 : j0 + n].bitcast(FP8X4),
                h_scales[s][:, j0 : j0 + n],
                packed,
            )

        def y_pass(acc, c, s, j0, n, start, stop):
            nc.tensor.matmul_mx(
                acc,
                lhsT=codes["wo", s, 0, c],
                lhsT_scale=scales["wo", s, 0, c],
                rhs=h_codes[s][:, j0 : j0 + n].bitcast(FP8X4),
                rhs_scale=h_scales[s][:, j0 : j0 + n],
                start=start,
                stop=stop,
            )

        def open_sums(j0, n, together):
            banks = []
            for c0 in range(0, OUT_TILES, together):
                acc = psum.tile([P, together, n], F32, name="bank")
                for e in range(together):
                    y_pass(acc[:, e, :], c0 + e, 0, j0, n, e == 0, False)
                    banks.append((acc[:, e, :], e == together - 1))
            sums[j0] = banks

        def close_sums(j0, n, stores):
            for c, (acc, last) in enumerate(sums[j0]):
                y_pass(acc, c, 1, j0, n, False, last)
            for c, (acc, last) in enumerate(sums[j0]):
                nc.scalar.activation(result[:, c, j0 : j0 + n], acc, TANH, bias=bias[:, c : c + 1])
                if c in stores:
                    first_tile, first_pair = stores[c]
                    where = (slice(None), slice(first_tile, c + 1), slice(first_pair, j0 + n))
                    nc.sync.dma_start(out_rows[where], result[where])

        nc.gpsimd.memset(item_scale_tab[:], 0)
        nc.vector.memset(wb_scale_raw[:], 0)
        nc.gpsimd.memset(user_scale_tab[:], 0)

        nc.sync.dma_start(items[:], offs2)
        for r in range(SCALE_ROWS):
            load_scale_row(item_scale_tab, tab2_scales[0], 0, r)
        nc.sync.dma_start(wb_code_raw[:], wb_words[0].bitcast(I32))
        nc.sync.dma_start(item_code_tab[:], words(tab2_words[0]))
        for r in range(SCALE_ROWS):
            load_scale_row(wb_scale_raw, wb_scales[0], 0, r)
        nc.sync.dma_start(users[:], offs)
        for half in range(PASSES):
            nc.sync.dma_start(user_code_tab[half][:], words(tab_words[half]))
            for r in range(HALF * half, HALF * (half + 1)):
                for s in range(PASSES):
                    load_scale_row(user_scale_tab, tab_scales[s], USER_ROW + SCALE_ROWS * s, r)

        nc.vector.tensor_copy(item_scales[:], item_scale_tab[:].bitcast(U8).indirect(items[:]))
        nc.vector.tensor_copy(
            wb_codes[:].bitcast(I32).rearrange("p (s t g w) -> p s t g w", s=PASSES, t=SLOTS, w=2),
            wb_code_raw[:].rearrange("p (s g t w) -> p s t g w", s=PASSES, t=SLOTS, w=2),
        )
        nc.vector.tensor_copy(item_codes[:], item_code_tab[:].bitcast(U32).indirect(items[:]))
        nc.vector.tensor_copy(
            wb_scale[:].bitcast(I32).rearrange("p (s t g) -> p s t g", s=PASSES, t=SLOTS),
            wb_scale_raw[:].rearrange("p (s g t) -> p s t g", s=PASSES, t=SLOTS),
        )
        for s in range(PASSES):
            nc.vector.tensor_copy(user_codes[s][:], user_code_tab[s][:].bitcast(U32).indirect(users[:]))
        nc.vector.tensor_copy(user_scales[:], user_scale_tab[:].bitcast(U8).indirect(users[:]))

        load_wa(0, 0, "big0")
        load_wa(0, 1, "big3")
        load_gate(0)
        load_wa(1, 0, "big1")
        load_gate(1)
        load_gate(2)
        load_wa(1, 1, "big2")
        load_gate(3)
        load_wo(0, place("big4", SLOTS * N, F32)[:])

        b, product = {}, {}
        for u in range(3):
            b[u] = place(f"b{u}", S, F32)[:]
            make_b(u, b[u])
        round_wa(nc.scalar.copy, 0, 0, 0, SLOTS, "rounded0")
        round_wa(nc.scalar.copy, 0, 1, 0, HALF, "rounded1")
        round_wa(nc.vector.tensor_copy, 0, 1, HALF, HALF, "rounded2")
        later = place("big3", 2 * S, F32)
        for u in (3, 4):
            b[u] = later[:, (u - 3) * S : (u - 2) * S]
            make_b(u, b[u])
        quantize_weight("wa", 0, 0, 0, SLOTS)
        quantize_weight("wa", 0, 1, HALF, HALF)
        quantize_weight("wa", 0, 1, 0, HALF)
        product[0] = place("product0", S, F32)[:]
        gate_times(product[0], 0, b[0], 0, S)
        load_gate(4)
        h0 = keep.tile([P, SLOTS, S], F32, name="h0", align_bytes=64)
        stage = place("stage", 3 * ROW + 3 * S, F32)
        h1 = stage[:, : SLOTS * ROW].rearrange("p (t c) -> p t c", t=SLOTS)
        for u in (1, 2):
            product[u] = place(f"product{u}", S, F32)[:]
        pooled = [place(f"pooled{e}", n, F32)[:] for e, n in enumerate((PIECE, PIECE, BANK))]
        pool_a_b(3, 0, pooled[:2])
        pool_a_b(3, BANK, pooled[2:])
        times_a(1, b[1], halves(product[1]))
        times_a(2, b[2], halves(product[2]))
        times_a(0, product[0], halves(h0[:, 0, :]))
        round_wa(nc.scalar.copy, 1, 0, 0, SLOTS, "rounded0")
        later = place("big1", 3 * S, F32)
        for u in (5, 6, 7):
            b[u] = later[:, (u - 5) * S : (u - 4) * S]
            make_b(u, b[u])
        gate_times(h0[:, 1, :], 1, product[1], 0, S)
        load_gate(5)
        load_wo(1, stage[:, 3 * ROW + S :])
        quantize_weight("wa", 1, 0, 0, SLOTS)
        gate_times(h0[:, 2, :], 2, product[2], 0, S)
        load_gate(6)
        round_wa(nc.scalar.copy, 1, 1, 0, HALF, "rounded1")
        round_wa(nc.scalar.copy, 1, 1, HALF, HALF, "rounded2")
        quantize_weight("wa", 1, 1, 0, HALF)
        for e in range(2):
            gate_times(h0[:, 3, e * PIECE : (e + 1) * PIECE], 3, pooled[e], e * PIECE, PIECE)
        quantize_weight("wa", 1, 1, HALF, HALF, "pooled0")
        gate_times(h0[:, 3, BANK:], 3, pooled[2], BANK, BANK)
        load_gate(7)
        with nc.allow_non_contiguous_dma(reason="one bias value for each partition and output tile"):
            nc.sync.dma_start(bias[:], bo.rearrange("(c p) -> p c", p=P))
        product[4] = place("product0", S, F32)[:]
        product[6] = place("product2", S, F32)[:]
        early = h1[:, 2, S + PIECE :]
        late = h1[:, 2, LEAD : S + PIECE]
        pooled = [place(name, BANK, F32)[:] for name in ("low", "high")]
        for e in range(2):
            pool_a_b(5, e * BANK, [pooled[e]])
        a_copy = place("a_copy0", PIECE, F32)
        nc.scalar.copy(a_copy[:], make_a(4, S - PIECE, PIECE)[:])
        nc.gpsimd.tensor_tensor(product[4][:, S - PIECE :], a_copy[:], b[4][:, S - PIECE :], MULT)
        packed0 = place("big2", SLOTS * S, BF16)
        for j0 in range(0, S, PIECE):
            interleave(nc.scalar.copy, packed0[:, SLOTS * j0 : SLOTS * (j0 + PIECE)], h0, j0, PIECE)
        for j0, n in ((0, BANK), (BANK, PIECE)):
            nc.vector.tensor_tensor(product[4][:, j0 : j0 + n], make_a(4, j0, n)[:], b[4][:, j0 : j0 + n], MULT)
        times_a(6, b[6], halves(product[6]))
        acc = make_a(7, 0)
        nc.vector.tensor_tensor(early, acc[:, :PIECE], b[7][:, :PIECE], MULT)
        nc.vector.tensor_tensor(late[:, :PIECE], acc[:, PIECE:], b[7][:, PIECE:BANK], MULT)
        nc.vector.tensor_tensor(late[:, PIECE:], make_a(7, BANK)[:], b[7][:, BANK:], MULT)
        round_wo(0, "rounded0")
        round_wo(1, "rounded1")
        gate_times(h1[:, 0, :S], 4, product[4], 0, S)
        for j0 in range(0, S, BANK):
            quantize_h(0, packed0[:, SLOTS * j0 : SLOTS * (j0 + BANK)], j0, BANK)
        gate_times(h1[:, 1, :BANK], 5, pooled[0], 0, BANK)
        gate_times(h1[:, 1, BANK:S], 5, pooled[1], BANK, BANK)
        quantize_weight("wo", 0, 0, 0, SLOTS, "low")
        gate_times(h1[:, 2, :LEAD], 6, product[6][:, :LEAD], 0, LEAD)
        quantize_weight("wo", 1, 0, 0, SLOTS, "high")

        result = keep.tile([P, OUT_TILES, S], F32, name="h0", align_bytes=64)

        def packed(j0, n):
            return stage[:, 3 * ROW + PACK_AT[j0] : 3 * ROW + PACK_AT[j0] + 2 * n].bitcast(BF16)

        def gather(u, j0, n):
            if u == 6:
                factor = product[6][:, j0 : j0 + n]
            else:
                factor = early[:, j0 : j0 + n] if j0 < PIECE else late[:, j0 - PIECE : j0 - PIECE + n]
            gate_times(h1[:, u - SLOTS, j0 : j0 + n], u, factor, j0, n)

        def pack(copy, j0, n):
            interleave(copy, packed(j0, n), h1, j0, n)

        def pack_pair(copy, t0, j0, n):
            copy(
                packed(j0, n).rearrange("p (c t) -> p c t", t=SLOTS)[:, :, t0 : t0 + HALF],
                h1[:, t0 : t0 + HALF, j0 : j0 + n].rearrange("p t c -> p c t"),
            )

        def quant(j0, n):
            quantize_h(1, packed(j0, n), j0, n)

        on_scalar, on_vector = nc.scalar.copy, nc.vector.tensor_copy
        for j0, n in ((0, 128), (128, 128), (256, 256), (512, 256), (768, 128), (896, 128)):
            open_sums(j0, n, BANK // n)
        pack_pair(on_scalar, 0, 256, 256)
        pack_pair(on_scalar, 0, 512, 512)
        gather(7, 0, 128)
        gather(7, 128, 128)
        pack(on_scalar, 128, 128)
        gather(7, 256, 128)
        pack(on_vector, 0, 128)
        gather(7, 384, 128)
        pack_pair(on_scalar, HALF, 256, 256)
        quant(0, 128)
        close_sums(0, 128, {1: (0, 0), 3: (2, 0)})
        gather(6, 512, 256)
        quant(128, 128)
        close_sums(128, 128, {1: (0, 128), 3: (2, 128)})
        gather(7, 512, 256)
        quant(256, 256)
        close_sums(256, 256, {1: (0, 256), 3: (2, 256)})
        pack_pair(on_vector, HALF, 512, 256)
        gather(6, 768, 128)
        quant(512, 256)
        close_sums(512, 256, {1: (0, 512), 3: (2, 512)})
        gather(7, 768, 128)
        gather(6, 896, 128)
        pack_pair(on_vector, HALF, 768, 128)
        gather(7, 896, 128)
        quant(768, 128)
        close_sums(768, 128, {})
        pack_pair(on_vector, HALF, 896, 128)
        quant(896, 128)
        close_sums(896, 128, {c: (c, 768) for c in range(OUT_TILES)})
